import numpy as np
import ml_dtypes


def mxq(x, axis, fmt="e4m3"):
    dtype, down = {"e4m3": (ml_dtypes.float8_e4m3fn, 7), "e5m2": (ml_dtypes.float8_e5m2, 14)}[fmt]
    v = np.moveaxis(np.asarray(x, np.float32).astype(ml_dtypes.bfloat16).astype(np.float64), axis, -1)
    blocks = v.reshape(v.shape[:-1] + (-1, 32))
    amax = np.abs(blocks).max(-1, keepdims=True)
    byte = np.maximum(np.where(amax > 0, np.frexp(amax)[1] - 1 + 127, 0) - down, 1)
    scale = np.exp2(byte - 127.0)
    codes = (blocks / scale).astype(np.float32).astype(dtype).astype(np.float64)
    return np.moveaxis((codes * scale).reshape(v.shape), -1, axis)


WIDE = False


def mx_kscale(k):
    if not WIDE:
        return np.ones(k)
    levels = np.array([10, -10, 5, -5, 0])
    if k % 512:
        return np.exp2(np.random.permutation(np.resize(levels, k // 32))).repeat(32)
    a = np.empty((k // 512, 16))
    for p in range(k // 512):
        a[p, :8] = np.random.permutation(np.resize(levels, 8))
        for g in range(8):
            far = levels[np.abs(levels - a[p, g]) >= 10]
            a[p, g + 8] = far[np.random.randint(len(far))]
    return np.exp2(a.ravel()).repeat(32)


BF16 = ml_dtypes.bfloat16


def bf(x):
    return np.asarray(x, np.float32).astype(BF16)


def f64(x):
    return np.asarray(x).astype(np.float64)


E2M1 = np.array([0.0, 0.5, 1.0, 1.5, 2.0, 3.0, 4.0, 6.0, -0.0, -0.5, -1.0, -1.5, -2.0, -3.0, -4.0, -6.0])


def pack_weight(w, fmt):
    k, n = w.shape
    w = f64(bf(w)).reshape(k // 32, 32, n)
    amax = np.abs(w).max(1)
    if fmt == "e4m3":
        byte = np.frexp(amax)[1] - 1 + 127 - 7
    else:
        mant, ex = np.frexp(amax / 6.0)
        byte = np.where(mant > 0.5, ex, ex - 1) + 127
    byte = np.clip(np.where(amax > 0, byte, 1), 1, 254)
    scaled = (w * np.exp2(127.0 - byte)[:, None, :]).reshape(k, n).astype(np.float32)
    by_word = np.ascontiguousarray(scaled.reshape(k // 512, 128, 4, n).transpose(0, 1, 3, 2))
    if fmt == "e4m3":
        words = by_word.astype(ml_dtypes.float8_e4m3fn).view(np.uint8)
    else:
        c = by_word.astype(ml_dtypes.float4_e2m1fn).view(np.uint8) & 0xF
        words = c[..., 0::2] | (c[..., 1::2] << 4)
    return np.ascontiguousarray(words), np.ascontiguousarray(byte.astype(np.uint8).reshape(k // 512, 16, n))


def unpack_weight(words, scales, fmt):
    g, p, n, _ = words.shape
    if fmt == "e4m3":
        vals = np.ascontiguousarray(words).view(ml_dtypes.float8_e4m3fn).astype(np.float64)
    else:
        nib = np.empty((g, p, n, 4), np.uint8)
        nib[..., 0::2] = words & 0xF
        nib[..., 1::2] = words >> 4
        vals = E2M1[nib]
    vals = vals * np.repeat(np.exp2(scales.astype(np.float64) - 127.0), 8, axis=1)[..., None]
    return vals.transpose(0, 1, 3, 2).reshape(g * 512, n)
def pack4(w):
    words, scales = pack_weight(w, "e2m1")
    return words.reshape(words.shape[0], 128, -1), scales


def unpack4(words, scales):
    return unpack_weight(words.reshape(words.shape[0], 128, -1, 2), scales, "e2m1")


def planes(Y):
    n, m = Y.shape
    b = f64(bf(Y)).reshape(n // 32, 32, m)
    amax = np.abs(b).max(1)
    byte = np.clip(np.where(amax > 0, np.frexp(amax)[1] - 1 + 127 - 7, 1), 1, 254)
    codes = (b * np.exp2(127.0 - byte)[:, None, :]).reshape(n, m).astype(np.float32).astype(ml_dtypes.float8_e4m3fn).view(np.uint8)
    words = codes.reshape(n // 512, 128, 4, m).transpose(0, 1, 3, 2)
    return np.ascontiguousarray(words), np.ascontiguousarray(byte.astype(np.uint8).reshape(n // 512, 16, m))


N1, N2, F, B, P, R, J = 2048, 1024, 32, 32, 1024, 512, 1024

def draw_gh(n, spread_g, spread_h):
    g = 3.0 * np.sqrt(B / N1) * np.random.randn(n, R) * spread_g
    h = 0.2 * B / (N1 + N2) * np.random.uniform(0.2, 1.0, (n, R)) * spread_h
    return np.concatenate([g, h], axis=1)

def setup_inputs():
    s1, s2, t = mx_kscale(N1)[:, None], mx_kscale(N2)[:, None], mx_kscale(P)
    spread_g, spread_h = np.exp(0.3 * np.random.randn(R)), np.exp(0.3 * np.random.randn(R))
    hot = np.stack([np.random.permutation(np.eye(B)) for _ in range(N1 // B * F)])
    hot = hot.reshape(N1 // B, F, B, B).transpose(0, 2, 1, 3).reshape(N1, P)
    e = np.exp(1.5 * np.random.randn(N2, F, B))
    soft = (e / e.sum(axis=2, keepdims=True)).reshape(N2, P)
    table = np.random.randn(P, J) / np.sqrt(P)
    hot_words, hot_scales = pack4(hot * t / s1)
    return {
        "gh_hard": bf(draw_gh(N1, spread_g, spread_h) * s1),
        "hot_words": hot_words, "hot_scales": hot_scales,
        "gh_soft": bf(draw_gh(N2, spread_g, spread_h) * s2),
        "soft": bf(soft * t / s2),
        "steps": bf(table / t[:, None]),
        "curve": bf(F * table ** 2 / t[:, None]),
        "lam": bf(np.exp(0.3 * np.random.randn(R))),
        "rho": bf(np.exp(0.8 * np.random.randn(R))),
    }

def reference(gh_hard, hot_words, hot_scales, gh_soft, soft, steps, curve, lam, rho):
    hot = unpack4(hot_words, hot_scales)
    hist = (hot.T @ mxq(f64(gh_hard), 0, "e4m3")) + (mxq(f64(soft), 0, "e4m3").T @ mxq(f64(gh_soft), 0, "e4m3"))
    q = mxq(hist, 0, "e4m3")
    num = mxq(f64(steps), 0, "e4m3").T @ q[:, :R]
    den = mxq(f64(curve), 0, "e4m3").T @ q[:, R:]
    y = f64(rho) * (num * num) / (den + f64(lam))
    Y = y.T
    words, scales = planes(Y)
    return y, words, scales

@@ -1,0 +1,378 @@
+from contextlib import ExitStack
+
+import concourse.mybir as mybir
+from concourse.masks import make_identity
+
+N1, N2, BINS, R, J = 2048, 1024, 1024, 512, 1024
+FLOPS = 2 * (N1 + N2) * BINS * 2 * R + 2 * BINS * J * 2 * R
+
+F32 = mybir.dt.float32
+BF16 = mybir.dt.bfloat16
+I32 = mybir.dt.int32
+U32 = mybir.dt.uint32
+U8 = mybir.dt.uint8
+FP8X4 = mybir.dt.float8_e4m3fn_x4
+FP4X4 = mybir.dt.float4_e2m1fn_x4
+ACT = mybir.ActivationFunctionType
+ALU = mybir.AluOpType
+
+P = 128
+PACK = 4
+K_PASS = P * PACK
+W = 512
+HARD = N1 // K_PASS
+SOFT = N2 // K_PASS
+PASS_ORDER = (0, 4, 1, 2, 5, 3)
+V_A = (256, 512, 320, 128, 512, 128, 448, 320, 256, 256)
+V_B = (256, 384, 384, 384, 384, 256)
+V_T = (320, 320, 512, 320, 384, 320, 256, 384)
+E_A = "SSSSSSVS"
+E_TA = "SSSS"
+E_B = "SVSSSVSV"
+E_TB = "SSVS"
+E_SQ = "SSVSSSSV"
+E_ROWS = "SSVSSSSS"
+E_Y = "VVVVSSSV"
+N_DEN = (0, 1, 1, 0, 0, 1)
+
+
+def tile_boosting_histogram_step_scores_k6_kernel(
+    tc, gh_hard, hot_words, hot_scales, gh_soft, soft, steps, curve, lam, rho, out_0, out_1, out_2
+):
+    nc = tc.nc
+    with ExitStack() as ctx:
+        keep = ctx.enter_context(tc.tile_pool(name="keep", bufs=1))
+        work = ctx.enter_context(tc.tile_pool(name="work", bufs=2))
+        psum = ctx.enter_context(tc.psum_pool(name="psum", bufs=1))
+        ctx.enter_context(tc.manual_schedule(engines={mybir.EngineType.PE, mybir.EngineType.SP}))
+
+        def planes(name, groups, width):
+            codes = keep.tile([P, groups, width], U32, name=name + "_codes", align_bytes=64)
+            scales = keep.tile([P, groups, width], U8, name=name + "_scales", align_bytes=64)
+            return codes, scales
+
+        gh_q = planes("gh", HARD + SOFT, 2 * R)
+        soft_q = planes("soft", SOFT, BINS)
+        steps_q = planes("steps", 2, J)
+        curve_q = planes("curve", 2, J)
+        hist_q = planes("hist", 4, R)
+        y_q = planes("y", 1, J)
+        hot_w = keep.tile([P, HARD, 2 * BINS], U8, align_bytes=64)
+        hot_s = keep.tile([P, HARD, BINS], U8, align_bytes=64)
+        hist_t = keep.tile([P, 8, BINS], BF16, align_bytes=64)
+        ident = keep.tile([P, P], F32)
+        lam_bf = keep.tile([P, PACK], BF16)
+        rho_bf = keep.tile([P, PACK], BF16)
+        warm = keep.tile([P, 1], F32)
+        warm_out = keep.tile([P, 1], F32)
+
+        def bank(b):
+            return psum.tile([P, W], F32, name="bank%d" % b, tag="bank%d" % b)
+
+        def copy_on(engine, out, in_):
+            if engine == "V":
+                nc.vector.tensor_copy(out=out, in_=in_)
+            else:
+                nc.scalar.copy(out=out, in_=in_)
+
+        def gh_rows(k):
+            src = gh_hard if k < HARD else gh_soft
+            g = k if k < HARD else k - HARD
+            return src[g * K_PASS : (g + 1) * K_PASS, :].rearrange("(p t) c -> p t c", t=PACK)
+
+        raw = {}
+
+        def load_gh(k, kind, cuts=(0, W)):
+            t = work.tile([P, PACK, W], BF16, name="raw_half", bufs=8)
+            for a, b in zip(cuts, cuts[1:]):
+                nc.sync.dma_start(out=t[:, :, a:b], in_=gh_rows(k)[:, :, kind * W + a : kind * W + b])
+            raw["gh", k, kind] = t[:]
+
+        def load_full(name, src, g):
+            t = work.tile([P, PACK, 2 * W], BF16, name="raw_full", bufs=4)
+            nc.sync.dma_start(out=t[:], in_=src[g * K_PASS : (g + 1) * K_PASS, :].rearrange("(p t) c -> p t c", t=PACK))
+            raw[name, g, 0] = t[:, :, 0:W]
+            raw[name, g, 1] = t[:, :, W : 2 * W]
+
+        nc.vector.memset(hot_s[:].rearrange("p g n -> p (g n)").bitcast(I32), 0)
+        nc.vector.memset(warm[:], 1.0)
+        make_identity(nc, ident[:])
+
+        for i, k in enumerate(PASS_ORDER):
+            load_gh(k, 1)
+            if k < HARD:
+                nc.sync.dma_start(out=hot_w[:, k, :].bitcast(I32), in_=hot_words[k].bitcast(I32))
+            else:
+                load_full("soft", soft, k - HARD)
+            if i == 0:
+                for q in range(4):
+                    nc.sync.dma_start(
+                        out=hot_s[32 * q : 32 * q + 4, :, :].bitcast(I32),
+                        in_=hot_scales[:, 4 * q : 4 * q + 4, :].rearrange("g r n -> r g n").bitcast(I32),
+                    )
+                nc.scalar.activation(out=warm_out[:], in_=warm[:], func=ACT.Abs_reciprocal_sqrt)
+        for k in PASS_ORDER:
+            load_gh(k, 0)
+        nc.sync.dma_start(out=lam_bf[:], in_=lam.rearrange("(p t) -> p t", t=PACK))
+        nc.sync.dma_start(out=rho_bf[:], in_=rho.rearrange("(p t) -> p t", t=PACK))
+        for g in range(2):
+            load_full("curve", curve, g)
+        for g in range(2):
+            load_full("steps", steps, g)
+
+        quantised = {"gh": gh_q, "soft": soft_q, "steps": steps_q, "curve": curve_q}
+        pending = []
+
+        def flush():
+            while pending:
+                grouped, codes, scales = pending.pop(0)
+                nc.vector.quantize_mx(out=codes.bitcast(FP8X4), scales=scales, in_=grouped)
+
+        def interleave(engine, dst, src):
+            copy_on(engine, dst.rearrange("p (c i) t -> p c t i", i=4), src.rearrange("p t (c i) -> p c t i", i=4))
+
+        def prepare(key, v_cols):
+            name, g, half = key
+            grouped = work.tile([P, W, PACK], BF16, name="grouped", bufs=6, align_bytes=64)
+            if v_cols < W:
+                interleave("S", grouped[:, v_cols:W, :], raw[key][:, :, v_cols:W])
+            if v_cols > 0:
+                interleave("V", grouped[:, 0:v_cols, :], raw[key][:, :, 0:v_cols])
+            flush()
+            codes, scales = quantised[name]
+            cols = slice(half * W, (half + 1) * W)
+            pending.append((grouped[:].rearrange("p c t -> p (c t)"), codes[:, g, cols], scales[:, g, cols]))
+
+        def hist_pass(acc, kind, i, half, tiles=range(4)):
+            k = PASS_ORDER[i]
+            if k < HARD:
+                rhs = hot_w[:, k, 2 * W * half : 2 * W * (half + 1)].bitcast(FP4X4)
+                rhs_scale = hot_s[:, k, W * half : W * (half + 1)]
+            else:
+                rhs = soft_q[0][:, k - HARD, W * half : W * (half + 1)].bitcast(FP8X4)
+                rhs_scale = soft_q[1][:, k - HARD, W * half : W * (half + 1)]
+            for s in tiles:
+                cols = slice(kind * R + s * P, kind * R + (s + 1) * P)
+                nc.tensor.matmul_mx(
+                    out=acc[half, s][:],
+                    lhsT=gh_q[0][:, k, cols].bitcast(FP8X4),
+                    lhsT_scale=gh_q[1][:, k, cols],
+                    rhs=rhs,
+                    rhs_scale=rhs_scale,
+                    start=(i == 0),
+                    stop=(i == len(PASS_ORDER) - 1),
+                )
+
+        def empty_hist(engine, acc, kind, half, s):
+            copy_on(
+                engine,
+                hist_t[:, 4 * kind + s, half * W : (half + 1) * W].rearrange("c (u p e) -> c u p e", u=2, e=2),
+                acc[half, s][:].rearrange("c (p u e) -> c u p e", u=2, e=2),
+            )
+
+        turned = {}
+        grouped_hist = {}
+
+        def turn(n, b):
+            kind, g, pair = n // 4, n // 2 % 2, n % 2
+            turned[n] = bank(b)
+            words = hist_t[:].bitcast(F32)
+            for u in range(2):
+                for j in range(2):
+                    s = 4 * kind + 2 * pair + j
+                    nc.tensor.transpose(
+                        turned[n][:, (2 * u + j) * P : (2 * u + j + 1) * P],
+                        words[:, s, (2 * g + u) * P : (2 * g + u + 1) * P],
+                        ident[:],
+                    )
+
+        def empty_turned(engine, n):
+            pair = n % 2
+            if pair == 0:
+                grouped_hist[n // 2] = work.tile([P, W, PACK], BF16, name="grouped", bufs=6, align_bytes=64)
+            words = grouped_hist[n // 2][:].bitcast(F32).rearrange("p (t m) u -> p t m u", t=PACK)
+            copy_on(
+                engine,
+                words[:, :, 64 * pair : 64 * (pair + 1), :],
+                turned[n][:].rearrange("p (u m t) -> p t m u", u=2, t=PACK),
+            )
+
+        def quantise_hist(n):
+            nc.vector.quantize_mx(
+                out=hist_q[0][:, n, :].bitcast(FP8X4),
+                scales=hist_q[1][:, n, :],
+                in_=grouped_hist[n][:].rearrange("p c t -> p (c t)"),
+            )
+
+        units = [(jh, t) for jh in range(2) for t in range(PACK)]
+        y = keep.tile([P, PACK, J], F32)
+        sign = keep.tile([P, PACK, J], BF16)
+        y_turned = {}
+
+        def product(kind, table, n, b):
+            jh, t = units[n]
+            dst = bank(b)
+            for g in range(2):
+                nc.tensor.matmul_mx(
+                    out=dst[:],
+                    lhsT=hist_q[0][:, 2 * kind + g, t * P : (t + 1) * P].bitcast(FP8X4),
+                    lhsT_scale=hist_q[1][:, 2 * kind + g, t * P : (t + 1) * P],
+                    rhs=table[0][:, g, jh * W : (jh + 1) * W].bitcast(FP8X4),
+                    rhs_scale=table[1][:, g, jh * W : (jh + 1) * W],
+                    start=(g == 0),
+                    stop=(g == 1),
+                )
+            return dst
+
+        def denominator(n, b):
+            jh, t = units[n]
+            den = product(1, curve_q, n, b)
+            nc.scalar.activation(out=y[:, t, jh * W : (jh + 1) * W], in_=den[:], func=ACT.Abs_reciprocal_sqrt, bias=lam_bf[:, t : t + 1])
+            nc.scalar.activation(out=sign[:, t, jh * W : (jh + 1) * W], in_=den[:], func=ACT.Sign, bias=lam_bf[:, t : t + 1])
+
+        nums = {}
+        y_grouped = {}
+
+        def numerator(jb, b):
+            nums[jb] = bank(b)
+            for t in range(PACK):
+                for g in range(2):
+                    nc.tensor.matmul_mx(
+                        out=nums[jb][:, t * P : (t + 1) * P],
+                        lhsT=hist_q[0][:, g, t * P : (t + 1) * P].bitcast(FP8X4),
+                        lhsT_scale=hist_q[1][:, g, t * P : (t + 1) * P],
+                        rhs=steps_q[0][:, g, jb * P : (jb + 1) * P].bitcast(FP8X4),
+                        rhs_scale=steps_q[1][:, g, jb * P : (jb + 1) * P],
+                        start=(g == 0),
+                        stop=(g == 1),
+                    )
+
+        def ratio(jb):
+            block = y[:, :, jb * P : (jb + 1) * P]
+            nc.vector.tensor_tensor(out=block, in0=nums[jb][:].rearrange("p (t j) -> p t j", t=PACK), in1=block, op=ALU.mult)
+            if E_SQ[jb] == "S":
+                nc.scalar.activation(out=block, in_=block, func=ACT.Square)
+            else:
+                nc.vector.tensor_tensor(out=block, in0=block, in1=block, op=ALU.mult)
+
+        def score(jb):
+            cols = slice(jb * P, (jb + 1) * P)
+            for t in range(PACK):
+                nc.vector.scalar_tensor_tensor(
+                    out=y[:, t, cols], in0=y[:, t, cols], scalar=rho_bf[:, t : t + 1], in1=sign[:, t, cols], op0=ALU.mult, op1=ALU.mult
+                )
+
+        def turn_y(jb, b):
+            y_turned[jb] = bank(b)
+            for t in range(PACK):
+                nc.tensor.transpose(y_turned[jb][:, t * P : (t + 1) * P], y[:, t, jb * P : (jb + 1) * P], ident[:])
+
+        def store_rows(jb):
+            rows = work.tile([P, P, PACK], F32, name="rows", bufs=4)
+            copy_on(E_ROWS[jb], rows[:], y_turned[jb][:].rearrange("j (t p) -> j p t", t=PACK))
+            nc.sync.dma_start(out=out_0[jb * P : (jb + 1) * P, :], in_=rows[:].rearrange("j p t -> j (p t)"))
+
+        def y_interleave(jb):
+            y_grouped[jb] = work.tile([P, P, PACK], BF16, name="y_grouped", bufs=3, align_bytes=64)
+            interleave(E_Y[jb], y_grouped[jb][:], y[:, :, jb * P : (jb + 1) * P])
+
+        def y_quantise(jb):
+            cols = slice(jb * P, (jb + 1) * P)
+            nc.vector.quantize_mx(
+                out=y_q[0][:, 0, cols].bitcast(FP8X4), scales=y_q[1][:, 0, cols], in_=y_grouped[jb][:].rearrange("p c t -> p (c t)")
+            )
+            if jb % 2 == 1:
+                cols = slice((jb - 1) * P, (jb + 1) * P)
+                nc.sync.dma_start(
+                    out=out_1[0].rearrange("p m t -> p (m t)").bitcast(I32)[:, cols], in_=y_q[0][:, 0, cols].bitcast(I32)
+                )
+
+        acc = {(half, s): bank(4 * (s // 2) + 2 * half + s % 2) for half in range(2) for s in range(4)}
+        shares = list(V_A)
+        for i, k in enumerate(PASS_ORDER):
+            prepare(("gh", k, 1), shares.pop(0))
+            if k < HARD:
+                flush()
+                hist_pass(acc, 1, i, 0)
+                hist_pass(acc, 1, i, 1)
+            else:
+                flush()
+                prepare(("soft", k - HARD, 0), shares.pop(0))
+                prepare(("soft", k - HARD, 1), shares.pop(0))
+                hist_pass(acc, 1, i, 0)
+                flush()
+                hist_pass(acc, 1, i, 1)
+        prepare(("gh", PASS_ORDER[0], 0), V_B[0])
+        prepare(("gh", PASS_ORDER[1], 0), V_B[1])
+        for n, (s, half) in enumerate((s, half) for s in range(4) for half in range(2)):
+            empty_hist(E_A[n], acc, 1, half, s)
+
+        acc = {(half, s): bank(2 * half + s) for half in range(2) for s in range(2)}
+        for i in range(6):
+            if i + 2 < 6:
+                prepare(("gh", PASS_ORDER[i + 2], 0), V_B[i + 2])
+            else:
+                flush()
+            for half in range(2):
+                hist_pass(acc, 0, i, half, range(2))
+            if i in (2, 3):
+                for n in (2 * i, 2 * i + 1):
+                    turn(n, n)
+                    empty_turned(E_TA[n - 4], n)
+        quantise_hist(2)
+        prepare(("curve", 0, 0), V_T[0])
+        quantise_hist(3)
+        prepare(("curve", 1, 0), V_T[1])
+        prepare(("curve", 0, 1), V_T[2])
+        for half in range(2):
+            for s in range(2):
+                empty_hist(E_B[2 * half + s], acc, 0, half, s)
+
+        acc = {(half, s): bank(2 * half + s + 2) for half in range(2) for s in range(2, 4)}
+        rest = [("curve", 1, 1)] + [("steps", g, half) for half in range(2) for g in range(2)]
+        for i in range(6):
+            for half in range(2):
+                hist_pass(acc, 0, i, half, range(2, 4))
+            if i < 5:
+                prepare(rest[i], V_T[3 + i])
+            if i == 1:
+                for g in range(2):
+                    turn(2 * g, g)
+                    empty_turned(E_TB[g], 2 * g)
+            for n in range(sum(N_DEN[:i]), sum(N_DEN[: i + 1])):
+                denominator(n, 2 + n % 2)
+        flush()
+        dens = list(range(sum(N_DEN), 8))
+        for n, (half, s) in enumerate((half, s) for half in range(2) for s in range(2, 4)):
+            empty_hist(E_B[4 + n], acc, 0, half, s)
+        while dens and dens[0] < 3:
+            denominator(dens[0], 2 + dens.pop(0) % 2)
+        for g in range(2):
+            turn(2 * g + 1, 4 + g)
+            empty_turned(E_TB[2 + g], 2 * g + 1)
+        while dens and dens[0] < 4:
+            denominator(dens[0], 2 + dens.pop(0) % 2)
+        quantise_hist(0)
+        quantise_hist(1)
+
+        numerator(0, 0)
+        numerator(1, 1)
+        ratio(0)
+        for jb in range(8):
+            if dens:
+                denominator(dens[0], 2 + dens.pop(0) % 2)
+            if jb + 1 < 8:
+                ratio(jb + 1)
+            if jb + 2 < 8:
+                numerator(jb + 2, jb % 2)
+            score(jb)
+            if jb > 0:
+                y_quantise(jb - 1)
+            y_interleave(jb)
+            turn_y(jb, 4 + jb % 4)
+            if jb > 0:
+                store_rows(jb - 1)
+        store_rows(7)
+        y_quantise(7)
+        for q in range(4):
+            nc.sync.dma_start(out=out_2[0, 4 * q : 4 * q + 4, :].bitcast(I32), in_=y_q[1][32 * q : 32 * q + 4, 0, :].bitcast(I32))

@@ -22,18 +22,9 @@ K_PASS = P * PACK
 W = 512
 HARD = N1 // K_PASS
 SOFT = N2 // K_PASS
-PASS_ORDER = (0, 4, 1, 2, 5, 3)
-V_A = (256, 512, 320, 128, 512, 128, 448, 320, 256, 256)
-V_B = (256, 384, 384, 384, 384, 256)
-V_T = (320, 320, 512, 320, 384, 320, 256, 384)
-E_A = "SSSSSSVS"
-E_TA = "SSSS"
-E_B = "SVSSSVSV"
-E_TB = "SSVS"
-E_SQ = "SSVSSSSV"
-E_ROWS = "SSVSSSSS"
-E_Y = "VVVVSSSV"
-N_DEN = (0, 1, 1, 0, 0, 1)
+PASS_ORDER = (0, 1, 4, 2, 3, 5)
+FIRST_SHARE = 256
+WAITING = 2
 
 
 def tile_boosting_histogram_step_scores_k6_kernel(
@@ -44,7 +35,7 @@ def tile_boosting_histogram_step_scores_k6_kernel(
         keep = ctx.enter_context(tc.tile_pool(name="keep", bufs=1))
         work = ctx.enter_context(tc.tile_pool(name="work", bufs=2))
         psum = ctx.enter_context(tc.psum_pool(name="psum", bufs=1))
-        ctx.enter_context(tc.manual_schedule(engines={mybir.EngineType.PE, mybir.EngineType.SP}))
+        ctx.enter_context(tc.manual_schedule())
 
         def planes(name, groups, width):
             codes = keep.tile([P, groups, width], U32, name=name + "_codes", align_bytes=64)
@@ -59,7 +50,6 @@ def tile_boosting_histogram_step_scores_k6_kernel(
         y_q = planes("y", 1, J)
         hot_w = keep.tile([P, HARD, 2 * BINS], U8, align_bytes=64)
         hot_s = keep.tile([P, HARD, BINS], U8, align_bytes=64)
-        hist_t = keep.tile([P, 8, BINS], BF16, align_bytes=64)
         ident = keep.tile([P, P], F32)
         lam_bf = keep.tile([P, PACK], BF16)
         rho_bf = keep.tile([P, PACK], BF16)
@@ -75,75 +65,85 @@ def tile_boosting_histogram_step_scores_k6_kernel(
             else:
                 nc.scalar.copy(out=out, in_=in_)
 
-        def gh_rows(k):
-            src = gh_hard if k < HARD else gh_soft
-            g = k if k < HARD else k - HARD
+        def rows_of(src, g):
             return src[g * K_PASS : (g + 1) * K_PASS, :].rearrange("(p t) c -> p t c", t=PACK)
 
         raw = {}
 
-        def load_gh(k, kind, cuts=(0, W)):
-            t = work.tile([P, PACK, W], BF16, name="raw_half", bufs=8)
-            for a, b in zip(cuts, cuts[1:]):
-                nc.sync.dma_start(out=t[:, :, a:b], in_=gh_rows(k)[:, :, kind * W + a : kind * W + b])
-            raw["gh", k, kind] = t[:]
-
         def load_full(name, src, g):
             t = work.tile([P, PACK, 2 * W], BF16, name="raw_full", bufs=4)
-            nc.sync.dma_start(out=t[:], in_=src[g * K_PASS : (g + 1) * K_PASS, :].rearrange("(p t) c -> p t c", t=PACK))
+            nc.sync.dma_start(out=t[:], in_=rows_of(src, g))
             raw[name, g, 0] = t[:, :, 0:W]
             raw[name, g, 1] = t[:, :, W : 2 * W]
+
+        def load_half(key, src, g):
+            half = key[2]
+            t = work.tile([P, PACK, W], BF16, name="raw_half", bufs=8)
+            nc.sync.dma_start(out=t[:], in_=rows_of(src, g)[:, :, half * W : (half + 1) * W])
+            raw[key] = t[:]
+
+        def load_gh(k, kind):
+            if k < HARD:
+                load_half(("gh", k, kind), gh_hard, k)
+            else:
+                load_half(("gh", k, kind), gh_soft, k - HARD)
+
+        def load_hot(k):
+            nc.sync.dma_start(out=hot_w[:, k, :].bitcast(I32), in_=hot_words[k].bitcast(I32))
 
         nc.vector.memset(hot_s[:].rearrange("p g n -> p (g n)").bitcast(I32), 0)
         nc.vector.memset(warm[:], 1.0)
         make_identity(nc, ident[:])
+        nc.scalar.activation(out=warm_out[:], in_=warm[:], func=ACT.Abs_reciprocal_sqrt)
 
         for i, k in enumerate(PASS_ORDER):
-            load_gh(k, 1)
-            if k < HARD:
-                nc.sync.dma_start(out=hot_w[:, k, :].bitcast(I32), in_=hot_words[k].bitcast(I32))
-            else:
-                load_full("soft", soft, k - HARD)
             if i == 0:
+                load_gh(k, 1)
+                load_hot(k)
                 for q in range(4):
                     nc.sync.dma_start(
                         out=hot_s[32 * q : 32 * q + 4, :, :].bitcast(I32),
                         in_=hot_scales[:, 4 * q : 4 * q + 4, :].rearrange("g r n -> r g n").bitcast(I32),
                     )
-                nc.scalar.activation(out=warm_out[:], in_=warm[:], func=ACT.Abs_reciprocal_sqrt)
-        for k in PASS_ORDER:
-            load_gh(k, 0)
-        nc.sync.dma_start(out=lam_bf[:], in_=lam.rearrange("(p t) -> p t", t=PACK))
-        nc.sync.dma_start(out=rho_bf[:], in_=rho.rearrange("(p t) -> p t", t=PACK))
-        for g in range(2):
-            load_full("curve", curve, g)
-        for g in range(2):
-            load_full("steps", steps, g)
+            elif k < HARD:
+                load_hot(k)
+                load_gh(k, 1)
+            elif i + 1 < len(PASS_ORDER):
+                load_gh(k, 1)
+                load_full("soft", soft, k - HARD)
+            else:
+                load_gh(k, 1)
+                for half in range(2):
+                    load_half(("soft", k - HARD, half), soft, k - HARD)
+
+        def late_loads():
+            for g in range(2):
+                load_full("curve", curve, g)
+            nc.sync.dma_start(out=lam_bf[:], in_=lam.rearrange("(p t) -> p t", t=PACK))
+            nc.sync.dma_start(out=rho_bf[:], in_=rho.rearrange("(p t) -> p t", t=PACK))
+            for g in range(2):
+                load_full("steps", steps, g)
 
         quantised = {"gh": gh_q, "soft": soft_q, "steps": steps_q, "curve": curve_q}
-        pending = []
-
-        def flush():
-            while pending:
-                grouped, codes, scales = pending.pop(0)
-                nc.vector.quantize_mx(out=codes.bitcast(FP8X4), scales=scales, in_=grouped)
+        grouped = {}
 
         def interleave(engine, dst, src):
             copy_on(engine, dst.rearrange("p (c i) t -> p c t i", i=4), src.rearrange("p t (c i) -> p c t i", i=4))
 
-        def prepare(key, v_cols):
+        def group(engine, key, a, b):
+            if key not in grouped:
+                grouped[key] = work.tile([P, W, PACK], BF16, name="grouped", bufs=6, align_bytes=64)
+            interleave(engine, grouped[key][:, a:b, :], raw[key][:, :, a:b])
+
+        def quantise(key):
             name, g, half = key
-            grouped = work.tile([P, W, PACK], BF16, name="grouped", bufs=6, align_bytes=64)
-            if v_cols < W:
-                interleave("S", grouped[:, v_cols:W, :], raw[key][:, :, v_cols:W])
-            if v_cols > 0:
-                interleave("V", grouped[:, 0:v_cols, :], raw[key][:, :, 0:v_cols])
-            flush()
             codes, scales = quantised[name]
             cols = slice(half * W, (half + 1) * W)
-            pending.append((grouped[:].rearrange("p c t -> p (c t)"), codes[:, g, cols], scales[:, g, cols]))
+            nc.vector.quantize_mx(
+                out=codes[:, g, cols].bitcast(FP8X4), scales=scales[:, g, cols], in_=grouped[key][:].rearrange("p c t -> p (c t)")
+            )
 
-        def hist_pass(acc, kind, i, half, tiles=range(4)):
+        def hist_pass(acc, kind, i, half):
             k = PASS_ORDER[i]
             if k < HARD:
                 rhs = hot_w[:, k, 2 * W * half : 2 * W * (half + 1)].bitcast(FP4X4)
@@ -151,7 +151,7 @@ def tile_boosting_histogram_step_scores_k6_kernel(
             else:
                 rhs = soft_q[0][:, k - HARD, W * half : W * (half + 1)].bitcast(FP8X4)
                 rhs_scale = soft_q[1][:, k - HARD, W * half : W * (half + 1)]
-            for s in tiles:
+            for s in range(4):
                 cols = slice(kind * R + s * P, kind * R + (s + 1) * P)
                 nc.tensor.matmul_mx(
                     out=acc[half, s][:],
@@ -163,75 +163,71 @@ def tile_boosting_histogram_step_scores_k6_kernel(
                     stop=(i == len(PASS_ORDER) - 1),
                 )
 
+        hist_t = {}
+
         def empty_hist(engine, acc, kind, half, s):
+            hist_t[kind, half, s] = work.tile([P, W], BF16, name="hist_t", bufs=8, align_bytes=64)
             copy_on(
                 engine,
-                hist_t[:, 4 * kind + s, half * W : (half + 1) * W].rearrange("c (u p e) -> c u p e", u=2, e=2),
+                hist_t[kind, half, s][:].rearrange("c (u p e) -> c u p e", u=2, e=2),
                 acc[half, s][:].rearrange("c (p u e) -> c u p e", u=2, e=2),
             )
 
         turned = {}
         grouped_hist = {}
 
-        def turn(n, b):
-            kind, g, pair = n // 4, n // 2 % 2, n % 2
-            turned[n] = bank(b)
-            words = hist_t[:].bitcast(F32)
-            for u in range(2):
-                for j in range(2):
-                    s = 4 * kind + 2 * pair + j
+        def turn(kind, half, pair, b):
+            turned[kind, half, pair] = bank(b)
+            for j in range(2):
+                words = hist_t[kind, half, 2 * pair + j][:].bitcast(F32)
+                for u in range(2):
                     nc.tensor.transpose(
-                        turned[n][:, (2 * u + j) * P : (2 * u + j + 1) * P],
-                        words[:, s, (2 * g + u) * P : (2 * g + u + 1) * P],
-                        ident[:],
+                        turned[kind, half, pair][:, (2 * u + j) * P : (2 * u + j + 1) * P], words[:, u * P : (u + 1) * P], ident[:]
                     )
 
-        def empty_turned(engine, n):
-            pair = n % 2
+        def empty_turned(engine, kind, half, pair):
             if pair == 0:
-                grouped_hist[n // 2] = work.tile([P, W, PACK], BF16, name="grouped", bufs=6, align_bytes=64)
-            words = grouped_hist[n // 2][:].bitcast(F32).rearrange("p (t m) u -> p t m u", t=PACK)
+                grouped_hist[kind, half] = work.tile([P, W, PACK], BF16, name="grouped_hist", bufs=2, align_bytes=64)
+            words = grouped_hist[kind, half][:].bitcast(F32).rearrange("p (t m) u -> p t m u", t=PACK)
             copy_on(
                 engine,
                 words[:, :, 64 * pair : 64 * (pair + 1), :],
-                turned[n][:].rearrange("p (u m t) -> p t m u", u=2, t=PACK),
+                turned[kind, half, pair][:].rearrange("p (u m t) -> p t m u", u=2, t=PACK),
             )
 
-        def quantise_hist(n):
+        def quantise_hist(kind, half):
             nc.vector.quantize_mx(
-                out=hist_q[0][:, n, :].bitcast(FP8X4),
-                scales=hist_q[1][:, n, :],
-                in_=grouped_hist[n][:].rearrange("p c t -> p (c t)"),
+                out=hist_q[0][:, 2 * kind + half, :].bitcast(FP8X4),
+                scales=hist_q[1][:, 2 * kind + half, :],
+                in_=grouped_hist[kind, half][:].rearrange("p c t -> p (c t)"),
             )
 
-        units = [(jh, t) for jh in range(2) for t in range(PACK)]
         y = keep.tile([P, PACK, J], F32)
         sign = keep.tile([P, PACK, J], BF16)
+        dens = {}
+        nums = {}
         y_turned = {}
+        y_grouped = {}
 
-        def product(kind, table, n, b):
-            jh, t = units[n]
-            dst = bank(b)
+        def denominator(n, b):
+            jh, t = divmod(n, PACK)
+            dens[n] = bank(b)
             for g in range(2):
                 nc.tensor.matmul_mx(
-                    out=dst[:],
-                    lhsT=hist_q[0][:, 2 * kind + g, t * P : (t + 1) * P].bitcast(FP8X4),
-                    lhsT_scale=hist_q[1][:, 2 * kind + g, t * P : (t + 1) * P],
-                    rhs=table[0][:, g, jh * W : (jh + 1) * W].bitcast(FP8X4),
-                    rhs_scale=table[1][:, g, jh * W : (jh + 1) * W],
+                    out=dens[n][:],
+                    lhsT=hist_q[0][:, 2 + g, t * P : (t + 1) * P].bitcast(FP8X4),
+                    lhsT_scale=hist_q[1][:, 2 + g, t * P : (t + 1) * P],
+                    rhs=curve_q[0][:, g, jh * W : (jh + 1) * W].bitcast(FP8X4),
+                    rhs_scale=curve_q[1][:, g, jh * W : (jh + 1) * W],
                     start=(g == 0),
                     stop=(g == 1),
                 )
-            return dst
 
-        def denominator(n, b):
-            jh, t = units[n]
-            den = product(1, curve_q, n, b)
-            nc.scalar.activation(out=y[:, t, jh * W : (jh + 1) * W], in_=den[:], func=ACT.Abs_reciprocal_sqrt, bias=lam_bf[:, t : t + 1])
-            nc.scalar.activation(out=sign[:, t, jh * W : (jh + 1) * W], in_=den[:], func=ACT.Sign, bias=lam_bf[:, t : t + 1])
-
-        nums = {}
-        y_grouped = {}
+        def root_and_sign(n):
+            jh, t = divmod(n, PACK)
+            cols = slice(jh * W, (jh + 1) * W)
+            nc.scalar.activation(out=y[:, t, cols], in_=dens[n][:], func=ACT.Abs_reciprocal_sqrt, bias=lam_bf[:, t : t + 1])
+            nc.scalar.activation(out=sign[:, t, cols], in_=dens[n][:], func=ACT.Sign, bias=lam_bf[:, t : t + 1])
 
         def numerator(jb, b):
             nums[jb] = bank(b)
@@ -250,10 +246,10 @@ def tile_boosting_histogram_step_scores_k6_kernel(
         def ratio(jb):
             block = y[:, :, jb * P : (jb + 1) * P]
             nc.vector.tensor_tensor(out=block, in0=nums[jb][:].rearrange("p (t j) -> p t j", t=PACK), in1=block, op=ALU.mult)
-            if E_SQ[jb] == "S":
-                nc.scalar.activation(out=block, in_=block, func=ACT.Square)
-            else:
-                nc.vector.tensor_tensor(out=block, in0=block, in1=block, op=ALU.mult)
+
+        def square(jb):
+            block = y[:, :, jb * P : (jb + 1) * P]
+            nc.scalar.activation(out=block, in_=block, func=ACT.Square)
 
         def score(jb):
             cols = slice(jb * P, (jb + 1) * P)
@@ -267,14 +263,14 @@ def tile_boosting_histogram_step_scores_k6_kernel(
             for t in range(PACK):
                 nc.tensor.transpose(y_turned[jb][:, t * P : (t + 1) * P], y[:, t, jb * P : (jb + 1) * P], ident[:])
 
-        def store_rows(jb):
+        def store_rows(engine, jb):
             rows = work.tile([P, P, PACK], F32, name="rows", bufs=4)
-            copy_on(E_ROWS[jb], rows[:], y_turned[jb][:].rearrange("j (t p) -> j p t", t=PACK))
+            copy_on(engine, rows[:], y_turned[jb][:].rearrange("j (t p) -> j p t", t=PACK))
             nc.sync.dma_start(out=out_0[jb * P : (jb + 1) * P, :], in_=rows[:].rearrange("j p t -> j (p t)"))
 
-        def y_interleave(jb):
+        def y_interleave(engine, jb):
             y_grouped[jb] = work.tile([P, P, PACK], BF16, name="y_grouped", bufs=3, align_bytes=64)
-            interleave(E_Y[jb], y_grouped[jb][:], y[:, :, jb * P : (jb + 1) * P])
+            interleave(engine, y_grouped[jb][:], y[:, :, jb * P : (jb + 1) * P])
 
         def y_quantise(jb):
             cols = slice(jb * P, (jb + 1) * P)
@@ -287,92 +283,137 @@ def tile_boosting_histogram_step_scores_k6_kernel(
                     out=out_1[0].rearrange("p m t -> p (m t)").bitcast(I32)[:, cols], in_=y_q[0][:, 0, cols].bitcast(I32)
                 )
 
-        acc = {(half, s): bank(4 * (s // 2) + 2 * half + s % 2) for half in range(2) for s in range(4)}
-        shares = list(V_A)
+        def shared(key):
+            group("S", key, FIRST_SHARE, W)
+            group("V", key, 0, FIRST_SHARE)
+
+        first = {(half, s): bank(4 * half + s) for half in range(2) for s in range(4)}
+        g_keys = [("gh", k, 0) for k in PASS_ORDER]
+        pieces = []
         for i, k in enumerate(PASS_ORDER):
-            prepare(("gh", k, 1), shares.pop(0))
             if k < HARD:
-                flush()
-                hist_pass(acc, 1, i, 0)
-                hist_pass(acc, 1, i, 1)
+                pieces.append((("gh", k, 1), [(i, 0), (i, 1)]))
             else:
-                flush()
-                prepare(("soft", k - HARD, 0), shares.pop(0))
-                prepare(("soft", k - HARD, 1), shares.pop(0))
-                hist_pass(acc, 1, i, 0)
-                flush()
-                hist_pass(acc, 1, i, 1)
-        prepare(("gh", PASS_ORDER[0], 0), V_B[0])
-        prepare(("gh", PASS_ORDER[1], 0), V_B[1])
-        for n, (s, half) in enumerate((s, half) for s in range(4) for half in range(2)):
-            empty_hist(E_A[n], acc, 1, half, s)
+                pieces.append((("gh", k, 1), []))
+                pieces.extend((("soft", k - HARD, half), [(i, half)]) for half in range(2))
+        ahead = [key for key, passes in pieces] + [g_keys[0]]
+        for n, (key, passes) in enumerate(pieces):
+            if n <= WAITING:
+                shared(key)
+            if n >= WAITING:
+                shared(ahead[n + 1])
+            quantise(key)
+            if key[0] == "gh":
+                load_gh(key[1], 0)
+            for i, half in passes:
+                hist_pass(first, 1, i, half)
+        late_loads()
 
-        acc = {(half, s): bank(2 * half + s) for half in range(2) for s in range(2)}
-        for i in range(6):
-            if i + 2 < 6:
-                prepare(("gh", PASS_ORDER[i + 2], 0), V_B[i + 2])
-            else:
-                flush()
-            for half in range(2):
-                hist_pass(acc, 0, i, half, range(2))
-            if i in (2, 3):
-                for n in (2 * i, 2 * i + 1):
-                    turn(n, n)
-                    empty_turned(E_TA[n - 4], n)
-        quantise_hist(2)
-        prepare(("curve", 0, 0), V_T[0])
-        quantise_hist(3)
-        prepare(("curve", 1, 0), V_T[1])
-        prepare(("curve", 0, 1), V_T[2])
+        for s in range(4):
+            empty_hist("S", first, 1, 0, s)
+        lower = {(0, s): bank(s) for s in range(4)}
+        quantise(g_keys[0])
+        hist_pass(lower, 0, 0, 0)
+        group("V", g_keys[1], 0, W)
+        group("V", g_keys[2], 0, W)
+        quantise(g_keys[1])
+        hist_pass(lower, 0, 1, 0)
+        for s in range(4):
+            empty_hist("S", first, 1, 1, s)
+        shared(g_keys[3])
         for half in range(2):
-            for s in range(2):
-                empty_hist(E_B[2 * half + s], acc, 0, half, s)
+            for pair in range(2):
+                turn(1, half, pair, 4 + 2 * half + pair)
+                empty_turned("S", 1, half, pair)
+        upper = {(1, s): bank(4 + s) for s in range(4)}
+        quantise(g_keys[2])
+        hist_pass(lower, 0, 2, 0)
+        group("V", g_keys[4], 0, W)
+        quantise(g_keys[3])
+        hist_pass(lower, 0, 3, 0)
+        group("V", g_keys[5], 0, W)
+        quantise(g_keys[4])
+        hist_pass(upper, 0, 0, 1)
+        hist_pass(lower, 0, 4, 0)
+        group("S", ("curve", 0, 0), 0, W)
+        quantise_hist(1, 0)
+        quantise(g_keys[5])
+        hist_pass(lower, 0, 5, 0)
+        quantise_hist(1, 1)
+        group("V", ("curve", 1, 0), 0, W)
+        quantise(("curve", 0, 0))
+        for s in range(4):
+            empty_hist("S", lower, 0, 0, s)
+        for i in range(1, 3):
+            hist_pass(upper, 0, i, 1)
+        group("V", ("curve", 0, 1), 0, W)
+        quantise(("curve", 1, 0))
+        for pair in range(2):
+            turn(0, 0, pair, pair)
+            empty_turned("S", 0, 0, pair)
+        denominator(0, 2)
+        denominator(1, 3)
+        root_and_sign(0)
+        root_and_sign(1)
+        for i in range(3, 6):
+            hist_pass(upper, 0, i, 1)
+        group("V", ("curve", 1, 1), 0, W)
+        quantise(("curve", 0, 1))
+        group("V", ("steps", 0, 0), 0, W)
+        quantise(("curve", 1, 1))
+        for s in range(4):
+            empty_hist("S", upper, 0, 1, s)
+        denominator(2, 0)
+        denominator(3, 1)
+        denominator(4, 2)
+        root_and_sign(2)
+        for pair in range(2):
+            turn(0, 1, pair, 4 + pair)
+            empty_turned("S", 0, 1, pair)
+        quantise_hist(0, 0)
+        group("V", ("steps", 1, 0), 0, W)
+        quantise(("steps", 0, 0))
+        group("V", ("steps", 0, 1), 0, W)
+        quantise(("steps", 1, 0))
+        group("V", ("steps", 1, 1), 0, W)
+        quantise(("steps", 0, 1))
+        quantise_hist(0, 1)
+        denominator(5, 3)
+        root_and_sign(3)
+        denominator(6, 0)
+        root_and_sign(4)
 
-        acc = {(half, s): bank(2 * half + s + 2) for half in range(2) for s in range(2, 4)}
-        rest = [("curve", 1, 1)] + [("steps", g, half) for half in range(2) for g in range(2)]
-        for i in range(6):
-            for half in range(2):
-                hist_pass(acc, 0, i, half, range(2, 4))
-            if i < 5:
-                prepare(rest[i], V_T[3 + i])
-            if i == 1:
-                for g in range(2):
-                    turn(2 * g, g)
-                    empty_turned(E_TB[g], 2 * g)
-            for n in range(sum(N_DEN[:i]), sum(N_DEN[: i + 1])):
-                denominator(n, 2 + n % 2)
-        flush()
-        dens = list(range(sum(N_DEN), 8))
-        for n, (half, s) in enumerate((half, s) for half in range(2) for s in range(2, 4)):
-            empty_hist(E_B[4 + n], acc, 0, half, s)
-        while dens and dens[0] < 3:
-            denominator(dens[0], 2 + dens.pop(0) % 2)
-        for g in range(2):
-            turn(2 * g + 1, 4 + g)
-            empty_turned(E_TB[2 + g], 2 * g + 1)
-        while dens and dens[0] < 4:
-            denominator(dens[0], 2 + dens.pop(0) % 2)
-        quantise_hist(0)
-        quantise_hist(1)
-
-        numerator(0, 0)
-        numerator(1, 1)
+        numerator(0, 6)
+        numerator(1, 7)
+        denominator(7, 1)
+        quantise(("steps", 1, 1))
         ratio(0)
+        square(0)
         for jb in range(8):
-            if dens:
-                denominator(dens[0], 2 + dens.pop(0) % 2)
             if jb + 1 < 8:
                 ratio(jb + 1)
+            if jb < 3:
+                root_and_sign(5 + jb)
+            if jb + 1 < 8:
+                square(jb + 1)
             if jb + 2 < 8:
-                numerator(jb + 2, jb % 2)
+                numerator(jb + 2, 6 + jb % 2)
             score(jb)
             if jb > 0:
-                y_quantise(jb - 1)
-            y_interleave(jb)
-            turn_y(jb, 4 + jb % 4)
-            if jb > 0:
-                store_rows(jb - 1)
-        store_rows(7)
+                if jb > 4:
+                    y_interleave("S", jb - 1)
+                else:
+                    y_quantise(jb - 1)
+                turn_y(jb - 1, 2 + (jb - 1) % 4)
+                store_rows("S", jb - 1)
+            if jb > 5:
+                y_quantise(jb - 2)
+            if jb < 4:
+                y_interleave("V", jb)
+        turn_y(7, 5)
+        y_quantise(6)
+        y_interleave("V", 7)
+        store_rows("S", 7)
         y_quantise(7)
         for q in range(4):
             nc.sync.dma_start(out=out_2[0, 4 * q : 4 * q + 4, :].bitcast(I32), in_=y_q[1][32 * q : 32 * q + 4, 0, :].bitcast(I32))

@@ -22,7 +22,12 @@ K_PASS = P * PACK
 W = 512
 HARD = N1 // K_PASS
 SOFT = N2 // K_PASS
-PASS_ORDER = (0, 1, 4, 2, 3, 5)
+FIRST_PIECES = (
+    ("gh", 0, 1), ("gh", 1, 1), ("gh", 2, 1), ("gh", 4, 1), ("soft", 0, 0),
+    ("gh", 3, 1), ("soft", 0, 1), ("gh", 5, 1), ("soft", 1, 0), ("soft", 1, 1),
+)
+GROUPS = HARD + SOFT
+RHO_GUARD = 1e-36
 FIRST_SHARE = 256
 WAITING = 2
 
@@ -53,8 +58,11 @@ def tile_boosting_histogram_step_scores_k6_kernel(
         ident = keep.tile([P, P], F32)
         lam_bf = keep.tile([P, PACK], BF16)
         rho_bf = keep.tile([P, PACK], BF16)
-        warm = keep.tile([P, 1], F32)
-        warm_out = keep.tile([P, 1], F32)
+        rho_root = keep.tile([P, PACK], F32)
+        rho_inv = keep.tile([P, PACK], F32)
+        rho_sign = keep.tile([P, PACK], F32)
+        lam_over_rho = keep.tile([P, PACK], F32)
+        lam_signed = keep.tile([P, PACK], F32)
 
         def bank(b):
             return psum.tile([P, W], F32, name="bank%d" % b, tag="bank%d" % b)
@@ -92,35 +100,36 @@ def tile_boosting_histogram_step_scores_k6_kernel(
             nc.sync.dma_start(out=hot_w[:, k, :].bitcast(I32), in_=hot_words[k].bitcast(I32))
 
         nc.vector.memset(hot_s[:].rearrange("p g n -> p (g n)").bitcast(I32), 0)
-        nc.vector.memset(warm[:], 1.0)
         make_identity(nc, ident[:])
-        nc.scalar.activation(out=warm_out[:], in_=warm[:], func=ACT.Abs_reciprocal_sqrt)
+        nc.scalar.dma_start(out=rho_bf[:], in_=rho.rearrange("(p t) -> p t", t=PACK))
+        nc.scalar.dma_start(out=lam_bf[:], in_=lam.rearrange("(p t) -> p t", t=PACK))
+        nc.scalar.activation(out=rho_root[:], in_=rho_bf[:], func=ACT.Abs_reciprocal_sqrt, bias=RHO_GUARD)
+        nc.scalar.activation(out=rho_sign[:], in_=rho_bf[:], func=ACT.Sign)
 
-        for i, k in enumerate(PASS_ORDER):
-            if i == 0:
-                load_gh(k, 1)
-                load_hot(k)
+        def load_piece(key):
+            name, g, half = key
+            if name == "soft":
+                load_half(key, soft, g)
+            else:
+                if 0 < g < HARD:
+                    load_hot(g)
+                load_gh(g, half)
+
+        for n, key in enumerate(FIRST_PIECES):
+            load_piece(key)
+            if n == 0:
+                load_hot(0)
                 for q in range(4):
                     nc.sync.dma_start(
                         out=hot_s[32 * q : 32 * q + 4, :, :].bitcast(I32),
                         in_=hot_scales[:, 4 * q : 4 * q + 4, :].rearrange("g r n -> r g n").bitcast(I32),
                     )
-            elif k < HARD:
-                load_hot(k)
-                load_gh(k, 1)
-            elif i + 1 < len(PASS_ORDER):
-                load_gh(k, 1)
-                load_full("soft", soft, k - HARD)
-            else:
-                load_gh(k, 1)
-                for half in range(2):
-                    load_half(("soft", k - HARD, half), soft, k - HARD)
+            if n == 7:
+                break
 
         def late_loads():
             for g in range(2):
                 load_full("curve", curve, g)
-            nc.sync.dma_start(out=lam_bf[:], in_=lam.rearrange("(p t) -> p t", t=PACK))
-            nc.sync.dma_start(out=rho_bf[:], in_=rho.rearrange("(p t) -> p t", t=PACK))
             for g in range(2):
                 load_full("steps", steps, g)
 
@@ -132,7 +141,7 @@ def tile_boosting_histogram_step_scores_k6_kernel(
 
         def group(engine, key, a, b):
             if key not in grouped:
-                grouped[key] = work.tile([P, W, PACK], BF16, name="grouped", bufs=6, align_bytes=64)
+                grouped[key] = work.tile([P, W, PACK], BF16, name="grouped", bufs=5, align_bytes=64)
             interleave(engine, grouped[key][:, a:b, :], raw[key][:, :, a:b])
 
         def quantise(key):
@@ -143,8 +152,7 @@ def tile_boosting_histogram_step_scores_k6_kernel(
                 out=codes[:, g, cols].bitcast(FP8X4), scales=scales[:, g, cols], in_=grouped[key][:].rearrange("p c t -> p (c t)")
             )
 
-        def hist_pass(acc, kind, i, half):
-            k = PASS_ORDER[i]
+        def hist_pass(acc, kind, k, half):
             if k < HARD:
                 rhs = hot_w[:, k, 2 * W * half : 2 * W * (half + 1)].bitcast(FP4X4)
                 rhs_scale = hot_s[:, k, W * half : W * (half + 1)]
@@ -159,8 +167,8 @@ def tile_boosting_histogram_step_scores_k6_kernel(
                     lhsT_scale=gh_q[1][:, k, cols],
                     rhs=rhs,
                     rhs_scale=rhs_scale,
-                    start=(i == 0),
-                    stop=(i == len(PASS_ORDER) - 1),
+                    start=(k == 0),
+                    stop=(k == GROUPS - 1),
                 )
 
         hist_t = {}
@@ -207,7 +215,7 @@ def tile_boosting_histogram_step_scores_k6_kernel(
         dens = {}
         nums = {}
         y_turned = {}
-        y_grouped = {}
+        y_grouped = keep.tile([P, J, PACK], BF16, align_bytes=64)
 
         def denominator(n, b):
             jh, t = divmod(n, PACK)
@@ -223,11 +231,29 @@ def tile_boosting_histogram_step_scores_k6_kernel(
                     stop=(g == 1),
                 )
 
-        def root_and_sign(n):
+        def root(n):
             jh, t = divmod(n, PACK)
-            cols = slice(jh * W, (jh + 1) * W)
-            nc.scalar.activation(out=y[:, t, cols], in_=dens[n][:], func=ACT.Abs_reciprocal_sqrt, bias=lam_bf[:, t : t + 1])
-            nc.scalar.activation(out=sign[:, t, cols], in_=dens[n][:], func=ACT.Sign, bias=lam_bf[:, t : t + 1])
+            nc.scalar.activation(
+                out=y[:, t, jh * W : (jh + 1) * W],
+                in_=dens[n][:],
+                func=ACT.Abs_reciprocal_sqrt,
+                scale=rho_inv[:, t : t + 1],
+                bias=lam_over_rho[:, t : t + 1],
+            )
+
+        def signum(n):
+            jh, t = divmod(n, PACK)
+            nc.scalar.activation(
+                out=sign[:, t, jh * W : (jh + 1) * W],
+                in_=dens[n][:],
+                func=ACT.Sign,
+                scale=rho_sign[:, t : t + 1],
+                bias=lam_signed[:, t : t + 1],
+            )
+
+        def root_and_sign(n):
+            root(n)
+            signum(n)
 
         def numerator(jb, b):
             nums[jb] = bank(b)
@@ -253,68 +279,68 @@ def tile_boosting_histogram_step_scores_k6_kernel(
 
         def score(jb):
             cols = slice(jb * P, (jb + 1) * P)
-            for t in range(PACK):
-                nc.vector.scalar_tensor_tensor(
-                    out=y[:, t, cols], in0=y[:, t, cols], scalar=rho_bf[:, t : t + 1], in1=sign[:, t, cols], op0=ALU.mult, op1=ALU.mult
-                )
+            nc.vector.tensor_tensor(out=y[:, :, cols], in0=y[:, :, cols], in1=sign[:, :, cols], op=ALU.mult)
 
         def turn_y(jb, b):
             y_turned[jb] = bank(b)
             for t in range(PACK):
                 nc.tensor.transpose(y_turned[jb][:, t * P : (t + 1) * P], y[:, t, jb * P : (jb + 1) * P], ident[:])
 
-        def store_rows(engine, jb):
-            rows = work.tile([P, P, PACK], F32, name="rows", bufs=4)
+        def store_rows(engine, jb, queue):
+            rows = work.tile([P, P, PACK], F32, name="rows", bufs=8)
             copy_on(engine, rows[:], y_turned[jb][:].rearrange("j (t p) -> j p t", t=PACK))
-            nc.sync.dma_start(out=out_0[jb * P : (jb + 1) * P, :], in_=rows[:].rearrange("j p t -> j (p t)"))
+            queue.dma_start(out=out_0[jb * P : (jb + 1) * P, :], in_=rows[:].rearrange("j p t -> j (p t)"))
 
-        def y_interleave(engine, jb):
-            y_grouped[jb] = work.tile([P, P, PACK], BF16, name="y_grouped", bufs=3, align_bytes=64)
-            interleave(engine, y_grouped[jb][:], y[:, :, jb * P : (jb + 1) * P])
+        def y_interleave(engine, first_jb, count):
+            a, b = first_jb * P, (first_jb + count) * P
+            interleave(engine, y_grouped[:, a:b, :], y[:, :, a:b])
 
-        def y_quantise(jb):
-            cols = slice(jb * P, (jb + 1) * P)
+        def y_quantise(first_jb, count):
+            a, b = first_jb * P, (first_jb + count) * P
             nc.vector.quantize_mx(
-                out=y_q[0][:, 0, cols].bitcast(FP8X4), scales=y_q[1][:, 0, cols], in_=y_grouped[jb][:].rearrange("p c t -> p (c t)")
+                out=y_q[0][:, 0, a:b].bitcast(FP8X4), scales=y_q[1][:, 0, a:b], in_=y_grouped[:, a:b, :].rearrange("p c t -> p (c t)")
             )
-            if jb % 2 == 1:
-                cols = slice((jb - 1) * P, (jb + 1) * P)
-                nc.sync.dma_start(
-                    out=out_1[0].rearrange("p m t -> p (m t)").bitcast(I32)[:, cols], in_=y_q[0][:, 0, cols].bitcast(I32)
-                )
+
+        def store_words(first_jb, count):
+            a, b = first_jb * P, (first_jb + count) * P
+            nc.sync.dma_start(out=out_1[0].rearrange("p m t -> p (m t)").bitcast(I32)[:, a:b], in_=y_q[0][:, 0, a:b].bitcast(I32))
 
         def shared(key):
             group("S", key, FIRST_SHARE, W)
             group("V", key, 0, FIRST_SHARE)
 
         first = {(half, s): bank(4 * half + s) for half in range(2) for s in range(4)}
-        g_keys = [("gh", k, 0) for k in PASS_ORDER]
-        pieces = []
-        for i, k in enumerate(PASS_ORDER):
-            if k < HARD:
-                pieces.append((("gh", k, 1), [(i, 0), (i, 1)]))
-            else:
-                pieces.append((("gh", k, 1), []))
-                pieces.extend((("soft", k - HARD, half), [(i, half)]) for half in range(2))
-        ahead = [key for key, passes in pieces] + [g_keys[0]]
-        for n, (key, passes) in enumerate(pieces):
+        g_keys = [("gh", k, 0) for k in range(GROUPS)]
+        ahead = list(FIRST_PIECES) + g_keys
+        for n, key in enumerate(FIRST_PIECES):
             if n <= WAITING:
                 shared(key)
             if n >= WAITING:
                 shared(ahead[n + 1])
             quantise(key)
-            if key[0] == "gh":
-                load_gh(key[1], 0)
-            for i, half in passes:
-                hist_pass(first, 1, i, half)
+            if n == 0:
+                nc.vector.tensor_tensor(out=rho_inv[:], in0=rho_root[:], in1=rho_root[:], op=ALU.mult)
+                nc.vector.tensor_tensor(out=lam_signed[:], in0=lam_bf[:], in1=rho_sign[:], op=ALU.mult)
+                nc.vector.tensor_tensor(out=lam_over_rho[:], in0=lam_bf[:], in1=rho_inv[:], op=ALU.mult)
+            if n + 8 < len(ahead):
+                if n + 8 < len(FIRST_PIECES):
+                    load_piece(ahead[n + 8])
+                else:
+                    load_gh(ahead[n + 8][1], 0)
+            name, g, half = key
+            if name == "soft":
+                hist_pass(first, 1, HARD + g, half)
+            elif g < HARD:
+                hist_pass(first, 1, g, 0)
+                hist_pass(first, 1, g, 1)
         late_loads()
 
         for s in range(4):
             empty_hist("S", first, 1, 0, s)
         lower = {(0, s): bank(s) for s in range(4)}
+        group("V", g_keys[1], 0, W)
         quantise(g_keys[0])
         hist_pass(lower, 0, 0, 0)
-        group("V", g_keys[1], 0, W)
         group("V", g_keys[2], 0, W)
         quantise(g_keys[1])
         hist_pass(lower, 0, 1, 0)
@@ -340,13 +366,13 @@ def tile_boosting_histogram_step_scores_k6_kernel(
         quantise(g_keys[5])
         hist_pass(lower, 0, 5, 0)
         quantise_hist(1, 1)
-        group("V", ("curve", 1, 0), 0, W)
+        shared(("curve", 1, 0))
         quantise(("curve", 0, 0))
         for s in range(4):
             empty_hist("S", lower, 0, 0, s)
-        for i in range(1, 3):
-            hist_pass(upper, 0, i, 1)
-        group("V", ("curve", 0, 1), 0, W)
+        for k in range(1, 3):
+            hist_pass(upper, 0, k, 1)
+        shared(("steps", 0, 0))
         quantise(("curve", 1, 0))
         for pair in range(2):
             turn(0, 0, pair, pair)
@@ -355,65 +381,101 @@ def tile_boosting_histogram_step_scores_k6_kernel(
         denominator(1, 3)
         root_and_sign(0)
         root_and_sign(1)
-        for i in range(3, 6):
-            hist_pass(upper, 0, i, 1)
+        for k in range(3, 6):
+            hist_pass(upper, 0, k, 1)
+        group("V", ("curve", 0, 1), 0, W)
         group("V", ("curve", 1, 1), 0, W)
         quantise(("curve", 0, 1))
-        group("V", ("steps", 0, 0), 0, W)
+        quantise(("steps", 0, 0))
+        group("V", ("steps", 1, 0), 0, W)
         quantise(("curve", 1, 1))
+        quantise_hist(0, 0)
+        quantise(("steps", 1, 0))
         for s in range(4):
-            empty_hist("S", upper, 0, 1, s)
+            empty_hist("SV"[s % 2], upper, 0, 1, s)
         denominator(2, 0)
         denominator(3, 1)
-        denominator(4, 2)
-        root_and_sign(2)
         for pair in range(2):
             turn(0, 1, pair, 4 + pair)
-            empty_turned("S", 0, 1, pair)
-        quantise_hist(0, 0)
-        group("V", ("steps", 1, 0), 0, W)
-        quantise(("steps", 0, 0))
-        group("V", ("steps", 0, 1), 0, W)
-        quantise(("steps", 1, 0))
-        group("V", ("steps", 1, 1), 0, W)
-        quantise(("steps", 0, 1))
-        quantise_hist(0, 1)
+        root_and_sign(2)
+        group("V", ("steps", 0, 1), 0, W // 2)
+        for pair in range(2):
+            empty_turned("VS"[pair], 0, 1, pair)
+        denominator(4, 2)
         denominator(5, 3)
-        root_and_sign(3)
         denominator(6, 0)
+        group("V", ("steps", 0, 1), W // 2, W)
+        quantise_hist(0, 1)
+        root_and_sign(3)
         root_and_sign(4)
 
-        numerator(0, 6)
-        numerator(1, 7)
+        for jb in range(4):
+            numerator(jb, (6, 7, 4, 5)[jb])
         denominator(7, 1)
-        quantise(("steps", 1, 1))
+        quantise(("steps", 0, 1))
+        group("V", ("steps", 1, 1), 0, W // 2)
         ratio(0)
+        ratio(1)
+        root_and_sign(5)
         square(0)
-        for jb in range(8):
-            if jb + 1 < 8:
-                ratio(jb + 1)
-            if jb < 3:
-                root_and_sign(5 + jb)
-            if jb + 1 < 8:
-                square(jb + 1)
-            if jb + 2 < 8:
-                numerator(jb + 2, 6 + jb % 2)
-            score(jb)
-            if jb > 0:
-                if jb > 4:
-                    y_interleave("S", jb - 1)
-                else:
-                    y_quantise(jb - 1)
-                turn_y(jb - 1, 2 + (jb - 1) % 4)
-                store_rows("S", jb - 1)
-            if jb > 5:
-                y_quantise(jb - 2)
-            if jb < 4:
-                y_interleave("V", jb)
-        turn_y(7, 5)
-        y_quantise(6)
-        y_interleave("V", 7)
-        store_rows("S", 7)
-        y_quantise(7)
+        square(1)
+        group("V", ("steps", 1, 1), W // 2, W)
+        ratio(2)
+        quantise(("steps", 1, 1))
+        score(0)
+        numerator(4, 6)
+        numerator(5, 7)
+        turn_y(0, 2)
+        root(6)
+        root(7)
+        square(2)
+        ratio(3)
+        score(1)
+        numerator(6, 4)
+        numerator(7, 5)
+        turn_y(1, 3)
+        store_rows("S", 0, nc.sync)
+        square(3)
+        signum(6)
+        ratio(4)
+        y_interleave("V", 0, 2)
+        score(2)
+        turn_y(2, 2)
+        store_rows("S", 1, nc.sync)
+        square(4)
+        signum(7)
+        ratio(5)
+        y_quantise(0, 2)
+        score(3)
+        turn_y(3, 3)
+        store_rows("S", 2, nc.sync)
+        square(5)
+        ratio(6)
+        y_interleave("V", 2, 2)
+        score(4)
+        turn_y(4, 0)
+        store_rows("S", 3, nc.sync)
+        square(6)
+        ratio(7)
+        y_quantise(2, 2)
+        store_words(0, 4)
+        score(5)
+        turn_y(5, 1)
+        store_rows("S", 4, nc.sync)
+        square(7)
+        y_interleave("V", 4, 1)
+        score(6)
+        turn_y(6, 2)
+        y_interleave("S", 5, 1)
+        store_rows("S", 5, nc.sync)
+        score(7)
+        turn_y(7, 3)
+        y_interleave("V", 6, 1)
+        store_rows("S", 6, nc.sync)
+        y_interleave("V", 7, 1)
+        y_quantise(4, 2)
+        y_quantise(6, 2)
+        store_rows("S", 7, nc.scalar)
+        store_words(4, 4)
         for q in range(4):
             nc.sync.dma_start(out=out_2[0, 4 * q : 4 * q + 4, :].bitcast(I32), in_=y_q[1][32 * q : 32 * q + 4, 0, :].bitcast(I32))

@@ -137,7 +137,7 @@ def tile_boosting_histogram_step_scores_k6_kernel(
         grouped = {}
 
         def interleave(engine, dst, src):
-            copy_on(engine, dst.rearrange("p (c i) t -> p c t i", i=4), src.rearrange("p t (c i) -> p c t i", i=4))
+            copy_on(engine, dst.rearrange("p (c i) t -> p c t i", i=8), src.rearrange("p t (c i) -> p c t i", i=8))
 
         def group(engine, key, a, b):
             if key not in grouped:
@@ -335,31 +335,35 @@ def tile_boosting_histogram_step_scores_k6_kernel(
                 hist_pass(first, 1, g, 1)
         late_loads()
 
+        quantise(g_keys[0])
+        group("V", g_keys[1], 0, W)
+        group("V", g_keys[2], 0, W // 2)
+        quantise(g_keys[1])
+        group("V", g_keys[2], W // 2, W)
         for s in range(4):
             empty_hist("S", first, 1, 0, s)
-        lower = {(0, s): bank(s) for s in range(4)}
-        group("V", g_keys[1], 0, W)
-        quantise(g_keys[0])
-        hist_pass(lower, 0, 0, 0)
-        group("V", g_keys[2], 0, W)
-        quantise(g_keys[1])
-        hist_pass(lower, 0, 1, 0)
+        for pair in range(2):
+            turn(1, 0, pair, pair)
         for s in range(4):
             empty_hist("S", first, 1, 1, s)
-        shared(g_keys[3])
+        lower = {(0, s): bank(2 + s) for s in range(4)}
+        hist_pass(lower, 0, 0, 0)
+        hist_pass(lower, 0, 1, 0)
+        for pair in range(2):
+            turn(1, 1, pair, 6 + pair)
         for half in range(2):
             for pair in range(2):
-                turn(1, half, pair, 4 + 2 * half + pair)
                 empty_turned("S", 1, half, pair)
-        upper = {(1, s): bank(4 + s) for s in range(4)}
+        upper = {(1, s): bank((6 + s + 2) % 8 if s < 2 else 4 + s) for s in range(4)}
+        group("V", g_keys[3], 0, W)
         quantise(g_keys[2])
         hist_pass(lower, 0, 2, 0)
         group("V", g_keys[4], 0, W)
         quantise(g_keys[3])
-        hist_pass(lower, 0, 3, 0)
-        group("V", g_keys[5], 0, W)
-        quantise(g_keys[4])
         hist_pass(upper, 0, 0, 1)
+        hist_pass(lower, 0, 3, 0)
+        shared(g_keys[5])
+        quantise(g_keys[4])
         hist_pass(lower, 0, 4, 0)
         group("S", ("curve", 0, 0), 0, W)
         quantise_hist(1, 0)
@@ -372,107 +376,107 @@ def tile_boosting_histogram_step_scores_k6_kernel(
             empty_hist("S", lower, 0, 0, s)
         for k in range(1, 3):
             hist_pass(upper, 0, k, 1)
-        shared(("steps", 0, 0))
+        shared(("curve", 0, 1))
         quantise(("curve", 1, 0))
         for pair in range(2):
-            turn(0, 0, pair, pair)
+            turn(0, 0, pair, 2 + pair)
+        denominator(0, 4)
+        denominator(1, 5)
+        for pair in range(2):
             empty_turned("S", 0, 0, pair)
-        denominator(0, 2)
-        denominator(1, 3)
         root_and_sign(0)
         root_and_sign(1)
         for k in range(3, 6):
             hist_pass(upper, 0, k, 1)
-        group("V", ("curve", 0, 1), 0, W)
         group("V", ("curve", 1, 1), 0, W)
+        group("V", ("steps", 0, 0), 0, W)
         quantise(("curve", 0, 1))
-        quantise(("steps", 0, 0))
-        group("V", ("steps", 1, 0), 0, W)
         quantise(("curve", 1, 1))
+        group("V", ("steps", 1, 0), 0, W)
+        quantise(("steps", 0, 0))
         quantise_hist(0, 0)
-        quantise(("steps", 1, 0))
         for s in range(4):
-            empty_hist("SV"[s % 2], upper, 0, 1, s)
-        denominator(2, 0)
-        denominator(3, 1)
+            empty_hist("S", upper, 0, 1, s)
+        denominator(2, 2)
+        denominator(3, 3)
+        denominator(4, 4)
         for pair in range(2):
-            turn(0, 1, pair, 4 + pair)
-        root_and_sign(2)
-        group("V", ("steps", 0, 1), 0, W // 2)
+            turn(0, 1, pair, pair)
+        root(2)
         for pair in range(2):
-            empty_turned("VS"[pair], 0, 1, pair)
-        denominator(4, 2)
-        denominator(5, 3)
-        denominator(6, 0)
-        group("V", ("steps", 0, 1), W // 2, W)
-        quantise_hist(0, 1)
-        root_and_sign(3)
-        root_and_sign(4)
-
-        for jb in range(4):
-            numerator(jb, (6, 7, 4, 5)[jb])
-        denominator(7, 1)
+            empty_turned("S", 0, 1, pair)
+        denominator(5, 5)
+        denominator(6, 6)
+        signum(2)
+        group("V", ("steps", 0, 1), 0, W)
+        quantise(("steps", 1, 0))
+        group("V", ("steps", 1, 1), 0, W)
         quantise(("steps", 0, 1))
-        group("V", ("steps", 1, 1), 0, W // 2)
+        quantise_hist(0, 1)
+        quantise(("steps", 1, 1))
+        root_and_sign(3)
+
+        for jb in range(3):
+            numerator(jb, (7, 0, 1)[jb])
+        denominator(7, 2)
+        numerator(3, 3)
         ratio(0)
         ratio(1)
-        root_and_sign(5)
+        root_and_sign(4)
         square(0)
         square(1)
-        group("V", ("steps", 1, 1), W // 2, W)
         ratio(2)
-        quantise(("steps", 1, 1))
+        root(5)
         score(0)
-        numerator(4, 6)
-        numerator(5, 7)
-        turn_y(0, 2)
+        numerator(4, 7)
+        numerator(5, 0)
+        turn_y(0, 4)
         root(6)
         root(7)
         square(2)
         ratio(3)
         score(1)
-        numerator(6, 4)
-        numerator(7, 5)
-        turn_y(1, 3)
+        numerator(6, 1)
+        numerator(7, 3)
+        signum(5)
+        turn_y(1, 5)
         store_rows("S", 0, nc.sync)
         square(3)
         signum(6)
-        ratio(4)
         y_interleave("V", 0, 2)
+        ratio(4)
         score(2)
-        turn_y(2, 2)
+        turn_y(2, 4)
         store_rows("S", 1, nc.sync)
         square(4)
         signum(7)
         ratio(5)
         y_quantise(0, 2)
         score(3)
-        turn_y(3, 3)
+        turn_y(3, 5)
         store_rows("S", 2, nc.sync)
         square(5)
         ratio(6)
         y_interleave("V", 2, 2)
         score(4)
-        turn_y(4, 0)
-        store_rows("S", 3, nc.sync)
+        turn_y(4, 6)
         square(6)
+        store_rows("S", 3, nc.sync)
         ratio(7)
         y_quantise(2, 2)
         store_words(0, 4)
         score(5)
-        turn_y(5, 1)
-        store_rows("S", 4, nc.sync)
+        turn_y(5, 2)
         square(7)
-        y_interleave("V", 4, 1)
+        store_rows("S", 4, nc.sync)
         score(6)
-        turn_y(6, 2)
-        y_interleave("S", 5, 1)
+        turn_y(6, 4)
         store_rows("S", 5, nc.sync)
         score(7)
-        turn_y(7, 3)
-        y_interleave("V", 6, 1)
+        turn_y(7, 5)
+        y_interleave("V", 4, 2)
         store_rows("S", 6, nc.sync)
-        y_interleave("V", 7, 1)
+        y_interleave("V", 6, 2)
         y_quantise(4, 2)
         y_quantise(6, 2)
         store_rows("S", 7, nc.scalar)

@@ -43,18 +43,18 @@ def tile_boosting_histogram_step_scores_k6_kernel(
         ctx.enter_context(tc.manual_schedule())
 
         def planes(name, groups, width):
-            codes = keep.tile([P, groups, width], U32, name=name + "_codes", align_bytes=64)
-            scales = keep.tile([P, groups, width], U8, name=name + "_scales", align_bytes=64)
+            codes = keep.tile([P, groups, width], U32, name=name + "_codes", align_bytes=256)
+            scales = keep.tile([P, groups, width], U8, name=name + "_scales", align_bytes=256)
             return codes, scales
 
         gh_q = planes("gh", HARD + SOFT, 2 * R)
         soft_q = planes("soft", SOFT, BINS)
         steps_q = planes("steps", 2, J)
         curve_q = planes("curve", 2, J)
-        hist_q = planes("hist", 4, R)
+        hist_q = planes("hist", 2, 2 * R)
         y_q = planes("y", 1, J)
-        hot_w = keep.tile([P, HARD, 2 * BINS], U8, align_bytes=64)
-        hot_s = keep.tile([P, HARD, BINS], U8, align_bytes=64)
+        hot_w = keep.tile([P, HARD, 2 * BINS], U8, align_bytes=256)
+        hot_s = keep.tile([P, HARD, BINS], U8, align_bytes=256)
         ident = keep.tile([P, P], F32)
         lam_bf = keep.tile([P, PACK], BF16)
         rho_bf = keep.tile([P, PACK], BF16)
@@ -79,10 +79,9 @@ def tile_boosting_histogram_step_scores_k6_kernel(
         raw = {}
 
         def load_full(name, src, g):
-            t = work.tile([P, PACK, 2 * W], BF16, name="raw_full", bufs=4)
+            t = work.tile([P, PACK, J], BF16, name="raw_full", bufs=4, align_bytes=64)
             nc.sync.dma_start(out=t[:], in_=rows_of(src, g))
-            raw[name, g, 0] = t[:, :, 0:W]
-            raw[name, g, 1] = t[:, :, W : 2 * W]
+            raw[name, g] = t[:]
 
         def load_half(key, src, g):
             half = key[2]
@@ -133,7 +132,7 @@ def tile_boosting_histogram_step_scores_k6_kernel(
             for g in range(2):
                 load_full("steps", steps, g)
 
-        quantised = {"gh": gh_q, "soft": soft_q, "steps": steps_q, "curve": curve_q}
+        quantised = {"gh": gh_q, "soft": soft_q}
         grouped = {}
 
         def interleave(engine, dst, src):
@@ -141,7 +140,7 @@ def tile_boosting_histogram_step_scores_k6_kernel(
 
         def group(engine, key, a, b):
             if key not in grouped:
-                grouped[key] = work.tile([P, W, PACK], BF16, name="grouped", bufs=5, align_bytes=64)
+                grouped[key] = work.tile([P, W, PACK], BF16, name="grouped", bufs=4, align_bytes=64)
             interleave(engine, grouped[key][:, a:b, :], raw[key][:, :, a:b])
 
         def quantise(key):
@@ -150,6 +149,20 @@ def tile_boosting_histogram_step_scores_k6_kernel(
             cols = slice(half * W, (half + 1) * W)
             nc.vector.quantize_mx(
                 out=codes[:, g, cols].bitcast(FP8X4), scales=scales[:, g, cols], in_=grouped[key][:].rearrange("p c t -> p (c t)")
+            )
+
+        def wide_tile(key):
+            if key not in grouped:
+                grouped[key] = work.tile([P, J, PACK], BF16, name="grouped_wide", bufs=2, align_bytes=64)
+            return grouped[key]
+
+        def group_table(engine, name, g, jh, a, b):
+            interleave(engine, wide_tile((name, jh))[:, g * W + a : g * W + b, :], raw[name, g][:, :, jh * W + a : jh * W + b])
+
+        def quantise_wide(name, n):
+            codes, scales = curve_q if name == "curve" else steps_q
+            nc.vector.quantize_mx(
+                out=codes[:, n, :].bitcast(FP8X4), scales=scales[:, n, :], in_=grouped[name, n][:].rearrange("p c t -> p (c t)")
             )
 
         def hist_pass(acc, kind, k, half):
@@ -182,7 +195,7 @@ def tile_boosting_histogram_step_scores_k6_kernel(
             )
 
         turned = {}
-        grouped_hist = {}
+        grouped_hist = keep.tile([P, 2 * W * PACK], BF16, align_bytes=64)
 
         def turn(kind, half, pair, b):
             turned[kind, half, pair] = bank(b)
@@ -194,20 +207,17 @@ def tile_boosting_histogram_step_scores_k6_kernel(
                     )
 
         def empty_turned(engine, kind, half, pair):
-            if pair == 0:
-                grouped_hist[kind, half] = work.tile([P, W, PACK], BF16, name="grouped_hist", bufs=2, align_bytes=64)
-            words = grouped_hist[kind, half][:].bitcast(F32).rearrange("p (t m) u -> p t m u", t=PACK)
+            words = grouped_hist[:, half * W * PACK : (half + 1) * W * PACK].bitcast(F32).rearrange("p (t m u) -> p t m u", t=PACK, u=2)
             copy_on(
                 engine,
                 words[:, :, 64 * pair : 64 * (pair + 1), :],
                 turned[kind, half, pair][:].rearrange("p (u m t) -> p t m u", u=2, t=PACK),
             )
 
-        def quantise_hist(kind, half):
+        def quantise_hist(kind, first_half, count):
+            a, b = first_half * W, (first_half + count) * W
             nc.vector.quantize_mx(
-                out=hist_q[0][:, 2 * kind + half, :].bitcast(FP8X4),
-                scales=hist_q[1][:, 2 * kind + half, :],
-                in_=grouped_hist[kind, half][:].rearrange("p c t -> p (c t)"),
+                out=hist_q[0][:, kind, a:b].bitcast(FP8X4), scales=hist_q[1][:, kind, a:b], in_=grouped_hist[:, a * PACK : b * PACK]
             )
 
         y = keep.tile([P, PACK, J], F32)
@@ -215,7 +225,6 @@ def tile_boosting_histogram_step_scores_k6_kernel(
         dens = {}
         nums = {}
         y_turned = {}
-        y_grouped = keep.tile([P, J, PACK], BF16, align_bytes=64)
 
         def denominator(n, b):
             jh, t = divmod(n, PACK)
@@ -223,10 +232,10 @@ def tile_boosting_histogram_step_scores_k6_kernel(
             for g in range(2):
                 nc.tensor.matmul_mx(
                     out=dens[n][:],
-                    lhsT=hist_q[0][:, 2 + g, t * P : (t + 1) * P].bitcast(FP8X4),
-                    lhsT_scale=hist_q[1][:, 2 + g, t * P : (t + 1) * P],
-                    rhs=curve_q[0][:, g, jh * W : (jh + 1) * W].bitcast(FP8X4),
-                    rhs_scale=curve_q[1][:, g, jh * W : (jh + 1) * W],
+                    lhsT=hist_q[0][:, 1, g * R + t * P : g * R + (t + 1) * P].bitcast(FP8X4),
+                    lhsT_scale=hist_q[1][:, 1, g * R + t * P : g * R + (t + 1) * P],
+                    rhs=curve_q[0][:, jh, g * W : (g + 1) * W].bitcast(FP8X4),
+                    rhs_scale=curve_q[1][:, jh, g * W : (g + 1) * W],
                     start=(g == 0),
                     stop=(g == 1),
                 )
@@ -259,12 +268,13 @@ def tile_boosting_histogram_step_scores_k6_kernel(
             nums[jb] = bank(b)
             for t in range(PACK):
                 for g in range(2):
+                    cols = slice(g * W + jb % 4 * P, g * W + (jb % 4 + 1) * P)
                     nc.tensor.matmul_mx(
                         out=nums[jb][:, t * P : (t + 1) * P],
-                        lhsT=hist_q[0][:, g, t * P : (t + 1) * P].bitcast(FP8X4),
-                        lhsT_scale=hist_q[1][:, g, t * P : (t + 1) * P],
-                        rhs=steps_q[0][:, g, jb * P : (jb + 1) * P].bitcast(FP8X4),
-                        rhs_scale=steps_q[1][:, g, jb * P : (jb + 1) * P],
+                        lhsT=hist_q[0][:, 0, g * R + t * P : g * R + (t + 1) * P].bitcast(FP8X4),
+                        lhsT_scale=hist_q[1][:, 0, g * R + t * P : g * R + (t + 1) * P],
+                        rhs=steps_q[0][:, jb // 4, cols].bitcast(FP8X4),
+                        rhs_scale=steps_q[1][:, jb // 4, cols],
                         start=(g == 0),
                         stop=(g == 1),
                     )
@@ -273,12 +283,12 @@ def tile_boosting_histogram_step_scores_k6_kernel(
             block = y[:, :, jb * P : (jb + 1) * P]
             nc.vector.tensor_tensor(out=block, in0=nums[jb][:].rearrange("p (t j) -> p t j", t=PACK), in1=block, op=ALU.mult)
 
-        def square(jb):
-            block = y[:, :, jb * P : (jb + 1) * P]
+        def square(jb, count=1):
+            block = y[:, :, jb * P : (jb + count) * P]
             nc.scalar.activation(out=block, in_=block, func=ACT.Square)
 
-        def score(jb):
-            cols = slice(jb * P, (jb + 1) * P)
+        def score(jb, count=1):
+            cols = slice(jb * P, (jb + count) * P)
             nc.vector.tensor_tensor(out=y[:, :, cols], in0=y[:, :, cols], in1=sign[:, :, cols], op=ALU.mult)
 
         def turn_y(jb, b):
@@ -287,18 +297,18 @@ def tile_boosting_histogram_step_scores_k6_kernel(
                 nc.tensor.transpose(y_turned[jb][:, t * P : (t + 1) * P], y[:, t, jb * P : (jb + 1) * P], ident[:])
 
         def store_rows(engine, jb, queue):
-            rows = work.tile([P, P, PACK], F32, name="rows", bufs=8)
+            rows = work.tile([P, P, PACK], F32, name="rows", bufs=6)
             copy_on(engine, rows[:], y_turned[jb][:].rearrange("j (t p) -> j p t", t=PACK))
             queue.dma_start(out=out_0[jb * P : (jb + 1) * P, :], in_=rows[:].rearrange("j p t -> j (p t)"))
 
         def y_interleave(engine, first_jb, count):
             a, b = first_jb * P, (first_jb + count) * P
-            interleave(engine, y_grouped[:, a:b, :], y[:, :, a:b])
+            interleave(engine, wide_tile("y")[:, a:b, :], y[:, :, a:b])
 
         def y_quantise(first_jb, count):
             a, b = first_jb * P, (first_jb + count) * P
             nc.vector.quantize_mx(
-                out=y_q[0][:, 0, a:b].bitcast(FP8X4), scales=y_q[1][:, 0, a:b], in_=y_grouped[:, a:b, :].rearrange("p c t -> p (c t)")
+                out=y_q[0][:, 0, a:b].bitcast(FP8X4), scales=y_q[1][:, 0, a:b], in_=grouped["y"][:, a:b, :].rearrange("p c t -> p (c t)")
             )
 
         def store_words(first_jb, count):
@@ -365,56 +375,54 @@ def tile_boosting_histogram_step_scores_k6_kernel(
         shared(g_keys[5])
         quantise(g_keys[4])
         hist_pass(lower, 0, 4, 0)
-        group("S", ("curve", 0, 0), 0, W)
-        quantise_hist(1, 0)
+        group_table("S", "curve", 0, 0, 0, W)
+        group_table("S", "curve", 1, 0, W // 2, W)
         quantise(g_keys[5])
         hist_pass(lower, 0, 5, 0)
-        quantise_hist(1, 1)
-        shared(("curve", 1, 0))
-        quantise(("curve", 0, 0))
+        quantise_hist(1, 0, 2)
+        group_table("V", "curve", 1, 0, 0, W // 2)
+        group_table("V", "curve", 0, 1, 0, W)
+        quantise_wide("curve", 0)
         for s in range(4):
             empty_hist("S", lower, 0, 0, s)
         for k in range(1, 3):
             hist_pass(upper, 0, k, 1)
-        shared(("curve", 0, 1))
-        quantise(("curve", 1, 0))
+        group_table("S", "curve", 1, 1, W // 2, W)
+        group_table("V", "curve", 1, 1, 0, W // 2)
         for pair in range(2):
             turn(0, 0, pair, 2 + pair)
         denominator(0, 4)
-        denominator(1, 5)
         for pair in range(2):
             empty_turned("S", 0, 0, pair)
         root_and_sign(0)
-        root_and_sign(1)
         for k in range(3, 6):
             hist_pass(upper, 0, k, 1)
-        group("V", ("curve", 1, 1), 0, W)
-        group("V", ("steps", 0, 0), 0, W)
-        quantise(("curve", 0, 1))
-        quantise(("curve", 1, 1))
-        group("V", ("steps", 1, 0), 0, W)
-        quantise(("steps", 0, 0))
-        quantise_hist(0, 0)
+        group_table("V", "steps", 0, 0, 0, W)
+        quantise_wide("curve", 1)
+        group_table("V", "steps", 1, 0, 0, W)
+        quantise_hist(0, 0, 1)
+        quantise_wide("steps", 0)
         for s in range(4):
-            empty_hist("S", upper, 0, 1, s)
+            empty_hist("V" if s == 3 else "S", upper, 0, 1, s)
+        denominator(1, 5)
         denominator(2, 2)
         denominator(3, 3)
-        denominator(4, 4)
         for pair in range(2):
             turn(0, 1, pair, pair)
-        root(2)
+        root_and_sign(1)
         for pair in range(2):
             empty_turned("S", 0, 1, pair)
-        denominator(5, 5)
-        denominator(6, 6)
+        denominator(4, 4)
+        denominator(5, 6)
+        denominator(6, 5)
+        group_table("V", "steps", 0, 1, 0, W)
+        group_table("V", "steps", 1, 1, 0, W)
+        quantise_hist(0, 1, 1)
+        quantise_wide("steps", 1)
+        root(2)
+        root(3)
         signum(2)
-        group("V", ("steps", 0, 1), 0, W)
-        quantise(("steps", 1, 0))
-        group("V", ("steps", 1, 1), 0, W)
-        quantise(("steps", 0, 1))
-        quantise_hist(0, 1)
-        quantise(("steps", 1, 1))
-        root_and_sign(3)
+        signum(3)
 
         for jb in range(3):
             numerator(jb, (7, 0, 1)[jb])
@@ -439,7 +447,7 @@ def tile_boosting_histogram_step_scores_k6_kernel(
         numerator(6, 1)
         numerator(7, 3)
         signum(5)
-        turn_y(1, 5)
+        turn_y(1, 6)
         store_rows("S", 0, nc.sync)
         square(3)
         signum(6)
@@ -453,13 +461,13 @@ def tile_boosting_histogram_step_scores_k6_kernel(
         ratio(5)
         y_quantise(0, 2)
         score(3)
-        turn_y(3, 5)
+        turn_y(3, 6)
         store_rows("S", 2, nc.sync)
         square(5)
         ratio(6)
         y_interleave("V", 2, 2)
         score(4)
-        turn_y(4, 6)
+        turn_y(4, 5)
         square(6)
         store_rows("S", 3, nc.sync)
         ratio(7)
@@ -473,13 +481,14 @@ def tile_boosting_histogram_step_scores_k6_kernel(
         turn_y(6, 4)
         store_rows("S", 5, nc.sync)
         score(7)
-        turn_y(7, 5)
+        turn_y(7, 6)
         y_interleave("V", 4, 2)
         store_rows("S", 6, nc.sync)
         y_interleave("V", 6, 2)
         y_quantise(4, 2)
+        store_words(4, 2)
         y_quantise(6, 2)
         store_rows("S", 7, nc.scalar)
-        store_words(4, 4)
+        store_words(6, 2)
         for q in range(4):
-            nc.sync.dma_start(out=out_2[0, 4 * q : 4 * q + 4, :].bitcast(I32), in_=y_q[1][32 * q : 32 * q + 4, 0, :].bitcast(I32))
+            (nc.sync, nc.scalar)[q % 2].dma_start(out=out_2[0, 4 * q : 4 * q + 4, :].bitcast(I32), in_=y_q[1][32 * q : 32 * q + 4, 0, :].bitcast(I32))

@@ -27,8 +27,9 @@ FIRST_PIECES = (
     ("gh", 3, 1), ("soft", 0, 1), ("gh", 5, 1), ("soft", 1, 0), ("soft", 1, 1),
 )
 GROUPS = HARD + SOFT
+RUN = 4
 RHO_GUARD = 1e-36
-FIRST_SHARE = 256
+FIRST_SHARE = 224
 WAITING = 2
 
 
@@ -55,6 +56,7 @@ def tile_boosting_histogram_step_scores_k6_kernel(
         y_q = planes("y", 1, J)
         hot_w = keep.tile([P, HARD, 2 * BINS], U8, align_bytes=256)
         hot_s = keep.tile([P, HARD, BINS], U8, align_bytes=256)
+        hot_s_raw = keep.tile([P, HARD, BINS], U8, align_bytes=64)
         ident = keep.tile([P, P], F32)
         lam_bf = keep.tile([P, PACK], BF16)
         rho_bf = keep.tile([P, PACK], BF16)
@@ -80,7 +82,9 @@ def tile_boosting_histogram_step_scores_k6_kernel(
 
         def load_full(name, src, g):
             t = work.tile([P, PACK, J], BF16, name="raw_full", bufs=4, align_bytes=64)
-            nc.sync.dma_start(out=t[:], in_=rows_of(src, g))
+            rows = src[g * K_PASS : (g + 1) * K_PASS, :].rearrange("(a t e) c -> e a t c", t=PACK, e=RUN)
+            for e in range(RUN):
+                nc.sync.dma_start(out=t[e:P:RUN, :, :], in_=rows[e])
             raw[name, g] = t[:]
 
         def load_half(key, src, g):
@@ -96,9 +100,22 @@ def tile_boosting_histogram_step_scores_k6_kernel(
                 load_half(("gh", k, kind), gh_soft, k - HARD)
 
         def load_hot(k):
-            nc.sync.dma_start(out=hot_w[:, k, :].bitcast(I32), in_=hot_words[k].bitcast(I32))
+            raw["hot", k] = work.tile([P, BINS // 2], I32, name="raw_hot", bufs=2)
+            nc.sync.dma_start(out=raw["hot", k][:], in_=hot_words[k].bitcast(I32))
 
-        nc.vector.memset(hot_s[:].rearrange("p g n -> p (g n)").bitcast(I32), 0)
+        def deal_hot(k):
+            nc.vector.tensor_copy(
+                out=hot_w[:, k, :].bitcast(I32).rearrange("p (g t a w) -> p g t a w", g=2, t=PACK, w=2),
+                in_=raw["hot", k][:].rearrange("p (g a t w) -> p g t a w", g=2, t=PACK, w=2),
+            )
+
+        def deal_hot_scales(a, b):
+            nc.vector.tensor_copy(
+                out=hot_s[:, a:b, :].bitcast(I32).rearrange("p k (g t a) -> p (k g) t a", g=2, t=PACK),
+                in_=hot_s_raw[:, a:b, :].bitcast(I32).rearrange("p k (g a t) -> p (k g) t a", g=2, t=PACK),
+            )
+
+        nc.vector.memset(hot_s_raw[:].rearrange("p g n -> p (g n)").bitcast(I32), 0)
         make_identity(nc, ident[:])
         nc.scalar.dma_start(out=rho_bf[:], in_=rho.rearrange("(p t) -> p t", t=PACK))
         nc.scalar.dma_start(out=lam_bf[:], in_=lam.rearrange("(p t) -> p t", t=PACK))
@@ -120,7 +137,7 @@ def tile_boosting_histogram_step_scores_k6_kernel(
                 load_hot(0)
                 for q in range(4):
                     nc.sync.dma_start(
-                        out=hot_s[32 * q : 32 * q + 4, :, :].bitcast(I32),
+                        out=hot_s_raw[32 * q : 32 * q + 4, :, :].bitcast(I32),
                         in_=hot_scales[:, 4 * q : 4 * q + 4, :].rearrange("g r n -> r g n").bitcast(I32),
                     )
             if n == 7:
@@ -141,7 +158,15 @@ def tile_boosting_histogram_step_scores_k6_kernel(
         def group(engine, key, a, b):
             if key not in grouped:
                 grouped[key] = work.tile([P, W, PACK], BF16, name="grouped", bufs=4, align_bytes=64)
-            interleave(engine, grouped[key][:, a:b, :], raw[key][:, :, a:b])
+            if key[0] == "gh":
+                interleave(engine, grouped[key][:, a:b, :], raw[key][:, :, a:b])
+            else:
+                runs = slice(a // (PACK * RUN), b // (PACK * RUN))
+                copy_on(
+                    engine,
+                    grouped[key][:].rearrange("p (t a e) j -> p a t j e", t=PACK, e=RUN)[:, runs],
+                    raw[key].rearrange("p j (a t e) -> p a t j e", t=PACK, e=RUN)[:, runs],
+                )
 
         def quantise(key):
             name, g, half = key
@@ -166,53 +191,34 @@ def tile_boosting_histogram_step_scores_k6_kernel(
             )
 
         def hist_pass(acc, kind, k, half):
-            if k < HARD:
-                rhs = hot_w[:, k, 2 * W * half : 2 * W * (half + 1)].bitcast(FP4X4)
-                rhs_scale = hot_s[:, k, W * half : W * (half + 1)]
+            if k in (0, GROUPS - 1):
+                order = [(t, s) for s in range(4) for t in range(PACK)]
             else:
-                rhs = soft_q[0][:, k - HARD, W * half : W * (half + 1)].bitcast(FP8X4)
-                rhs_scale = soft_q[1][:, k - HARD, W * half : W * (half + 1)]
-            for s in range(4):
+                order = [(t, s) for t in range(PACK) for s in range(4)]
+            for t, s in order:
+                tile = slice(W * half + t * P, W * half + (t + 1) * P)
+                if k < HARD:
+                    lhsT = hot_w[:, k, 2 * tile.start : 2 * tile.stop].bitcast(FP4X4)
+                    lhsT_scale = hot_s[:, k, tile]
+                else:
+                    lhsT = soft_q[0][:, k - HARD, tile].bitcast(FP8X4)
+                    lhsT_scale = soft_q[1][:, k - HARD, tile]
                 cols = slice(kind * R + s * P, kind * R + (s + 1) * P)
                 nc.tensor.matmul_mx(
-                    out=acc[half, s][:],
-                    lhsT=gh_q[0][:, k, cols].bitcast(FP8X4),
-                    lhsT_scale=gh_q[1][:, k, cols],
-                    rhs=rhs,
-                    rhs_scale=rhs_scale,
-                    start=(k == 0),
-                    stop=(k == GROUPS - 1),
+                    out=acc[half, s][:, t * P : (t + 1) * P],
+                    lhsT=lhsT,
+                    lhsT_scale=lhsT_scale,
+                    rhs=gh_q[0][:, k, cols].bitcast(FP8X4),
+                    rhs_scale=gh_q[1][:, k, cols],
+                    start=(k == 0 and t == 0),
+                    stop=(k == GROUPS - 1 and t == PACK - 1),
                 )
 
-        hist_t = {}
-
-        def empty_hist(engine, acc, kind, half, s):
-            hist_t[kind, half, s] = work.tile([P, W], BF16, name="hist_t", bufs=8, align_bytes=64)
-            copy_on(
-                engine,
-                hist_t[kind, half, s][:].rearrange("c (u p e) -> c u p e", u=2, e=2),
-                acc[half, s][:].rearrange("c (p u e) -> c u p e", u=2, e=2),
-            )
-
-        turned = {}
         grouped_hist = keep.tile([P, 2 * W * PACK], BF16, align_bytes=64)
 
-        def turn(kind, half, pair, b):
-            turned[kind, half, pair] = bank(b)
-            for j in range(2):
-                words = hist_t[kind, half, 2 * pair + j][:].bitcast(F32)
-                for u in range(2):
-                    nc.tensor.transpose(
-                        turned[kind, half, pair][:, (2 * u + j) * P : (2 * u + j + 1) * P], words[:, u * P : (u + 1) * P], ident[:]
-                    )
-
-        def empty_turned(engine, kind, half, pair):
-            words = grouped_hist[:, half * W * PACK : (half + 1) * W * PACK].bitcast(F32).rearrange("p (t m u) -> p t m u", t=PACK, u=2)
-            copy_on(
-                engine,
-                words[:, :, 64 * pair : 64 * (pair + 1), :],
-                turned[kind, half, pair][:].rearrange("p (u m t) -> p t m u", u=2, t=PACK),
-            )
+        def empty_hist(engine, acc, half, s):
+            dst = grouped_hist[:, half * W * PACK : (half + 1) * W * PACK].rearrange("p (u s m t) -> p s u m t", u=PACK, s=4, t=PACK)
+            copy_on(engine, dst[:, s], acc[half, s][:].rearrange("p (t m u) -> p u m t", t=PACK, u=PACK))
 
         def quantise_hist(kind, first_half, count):
             a, b = first_half * W, (first_half + count) * W
@@ -297,7 +303,7 @@ def tile_boosting_histogram_step_scores_k6_kernel(
                 nc.tensor.transpose(y_turned[jb][:, t * P : (t + 1) * P], y[:, t, jb * P : (jb + 1) * P], ident[:])
 
         def store_rows(engine, jb, queue):
-            rows = work.tile([P, P, PACK], F32, name="rows", bufs=6)
+            rows = work.tile([P, P, PACK], F32, name="rows", bufs=5)
             copy_on(engine, rows[:], y_turned[jb][:].rearrange("j (t p) -> j p t", t=PACK))
             queue.dma_start(out=out_0[jb * P : (jb + 1) * P, :], in_=rows[:].rearrange("j p t -> j (p t)"))
 
@@ -316,8 +322,9 @@ def tile_boosting_histogram_step_scores_k6_kernel(
             nc.sync.dma_start(out=out_1[0].rearrange("p m t -> p (m t)").bitcast(I32)[:, a:b], in_=y_q[0][:, 0, a:b].bitcast(I32))
 
         def shared(key):
-            group("S", key, FIRST_SHARE, W)
-            group("V", key, 0, FIRST_SHARE)
+            cut = FIRST_SHARE if key[0] == "gh" else W // 2
+            group("S", key, cut, W)
+            group("V", key, 0, cut)
 
         first = {(half, s): bank(4 * half + s) for half in range(2) for s in range(4)}
         g_keys = [("gh", k, 0) for k in range(GROUPS)]
@@ -327,11 +334,18 @@ def tile_boosting_histogram_step_scores_k6_kernel(
                 shared(key)
             if n >= WAITING:
                 shared(ahead[n + 1])
+            if n == 0:
+                deal_hot(0)
             quantise(key)
             if n == 0:
+                deal_hot_scales(0, 1)
                 nc.vector.tensor_tensor(out=rho_inv[:], in0=rho_root[:], in1=rho_root[:], op=ALU.mult)
                 nc.vector.tensor_tensor(out=lam_signed[:], in0=lam_bf[:], in1=rho_sign[:], op=ALU.mult)
+                deal_hot(1)
                 nc.vector.tensor_tensor(out=lam_over_rho[:], in0=lam_bf[:], in1=rho_inv[:], op=ALU.mult)
+                deal_hot_scales(1, HARD)
+            if n in (1, 4):
+                deal_hot(2 + n // 4)
             if n + 8 < len(ahead):
                 if n + 8 < len(FIRST_PIECES):
                     load_piece(ahead[n + 8])
@@ -350,145 +364,122 @@ def tile_boosting_histogram_step_scores_k6_kernel(
         group("V", g_keys[2], 0, W // 2)
         quantise(g_keys[1])
         group("V", g_keys[2], W // 2, W)
-        for s in range(4):
-            empty_hist("S", first, 1, 0, s)
-        for pair in range(2):
-            turn(1, 0, pair, pair)
-        for s in range(4):
-            empty_hist("S", first, 1, 1, s)
-        lower = {(0, s): bank(2 + s) for s in range(4)}
-        hist_pass(lower, 0, 0, 0)
-        hist_pass(lower, 0, 1, 0)
-        for pair in range(2):
-            turn(1, 1, pair, 6 + pair)
         for half in range(2):
-            for pair in range(2):
-                empty_turned("S", 1, half, pair)
-        upper = {(1, s): bank((6 + s + 2) % 8 if s < 2 else 4 + s) for s in range(4)}
+            for s in range(4):
+                empty_hist("S", first, half, s)
+        second = {(half, s): bank(4 * half + s) for half in range(2) for s in range(4)}
+        hist_pass(second, 0, 0, 0)
+        hist_pass(second, 0, 1, 0)
+        hist_pass(second, 0, 0, 1)
         group("V", g_keys[3], 0, W)
         quantise(g_keys[2])
-        hist_pass(lower, 0, 2, 0)
-        group("V", g_keys[4], 0, W)
+        hist_pass(second, 0, 2, 0)
+        shared(g_keys[4])
         quantise(g_keys[3])
-        hist_pass(upper, 0, 0, 1)
-        hist_pass(lower, 0, 3, 0)
+        hist_pass(second, 0, 3, 0)
         shared(g_keys[5])
         quantise(g_keys[4])
-        hist_pass(lower, 0, 4, 0)
+        hist_pass(second, 0, 4, 0)
         group_table("S", "curve", 0, 0, 0, W)
         group_table("S", "curve", 1, 0, W // 2, W)
         quantise(g_keys[5])
-        hist_pass(lower, 0, 5, 0)
+        hist_pass(second, 0, 5, 0)
         quantise_hist(1, 0, 2)
         group_table("V", "curve", 1, 0, 0, W // 2)
-        group_table("V", "curve", 0, 1, 0, W)
+        group_table("V", "curve", 0, 1, 0, W // 2)
         quantise_wide("curve", 0)
         for s in range(4):
-            empty_hist("S", lower, 0, 0, s)
-        for k in range(1, 3):
-            hist_pass(upper, 0, k, 1)
-        group_table("S", "curve", 1, 1, W // 2, W)
-        group_table("V", "curve", 1, 1, 0, W // 2)
-        for pair in range(2):
-            turn(0, 0, pair, 2 + pair)
-        denominator(0, 4)
-        for pair in range(2):
-            empty_turned("S", 0, 0, pair)
-        root_and_sign(0)
-        for k in range(3, 6):
-            hist_pass(upper, 0, k, 1)
+            empty_hist("S", second, 0, s)
+        group_table("S", "curve", 0, 1, W // 2, W)
+        hist_pass(second, 0, 1, 1)
+        hist_pass(second, 0, 2, 1)
+        group_table("V", "curve", 1, 1, 0, W)
+        denominator(0, 0)
+        denominator(1, 1)
+        hist_pass(second, 0, 3, 1)
+        denominator(2, 2)
+        for n in range(3):
+            root_and_sign(n)
         group_table("V", "steps", 0, 0, 0, W)
         quantise_wide("curve", 1)
+        hist_pass(second, 0, 4, 1)
+        hist_pass(second, 0, 5, 1)
         group_table("V", "steps", 1, 0, 0, W)
         quantise_hist(0, 0, 1)
         quantise_wide("steps", 0)
-        for s in range(4):
-            empty_hist("V" if s == 3 else "S", upper, 0, 1, s)
-        denominator(1, 5)
-        denominator(2, 2)
-        denominator(3, 3)
-        for pair in range(2):
-            turn(0, 1, pair, pair)
-        root_and_sign(1)
-        for pair in range(2):
-            empty_turned("S", 0, 1, pair)
-        denominator(4, 4)
-        denominator(5, 6)
-        denominator(6, 5)
         group_table("V", "steps", 0, 1, 0, W)
-        group_table("V", "steps", 1, 1, 0, W)
+        for s in range(4):
+            empty_hist("S", second, 1, s)
+        for n in range(3, 7):
+            denominator(n, (3, 0, 1, 2)[n - 3])
+        group_table("V", "steps", 1, 1, 0, W // 2)
         quantise_hist(0, 1, 1)
-        quantise_wide("steps", 1)
-        root(2)
-        root(3)
-        signum(2)
-        signum(3)
+        group_table("V", "steps", 1, 1, W // 2, W)
+        root_and_sign(3)
 
-        for jb in range(3):
-            numerator(jb, (7, 0, 1)[jb])
-        denominator(7, 2)
-        numerator(3, 3)
+        for jb in range(4):
+            numerator(jb, 4 + jb)
+        denominator(7, 3)
+        root_and_sign(4)
+        root_and_sign(5)
         ratio(0)
         ratio(1)
-        root_and_sign(4)
         square(0)
         square(1)
+        quantise_wide("steps", 1)
         ratio(2)
-        root(5)
         score(0)
-        numerator(4, 7)
-        numerator(5, 0)
-        turn_y(0, 4)
+        numerator(4, 4)
+        numerator(5, 5)
+        turn_y(0, 0)
         root(6)
         root(7)
         square(2)
         ratio(3)
         score(1)
-        numerator(6, 1)
-        numerator(7, 3)
-        signum(5)
-        turn_y(1, 6)
+        numerator(6, 6)
+        numerator(7, 7)
+        turn_y(1, 1)
         store_rows("S", 0, nc.sync)
         square(3)
         signum(6)
-        y_interleave("V", 0, 2)
         ratio(4)
+        y_interleave("V", 0, 2)
         score(2)
-        turn_y(2, 4)
+        turn_y(2, 0)
         store_rows("S", 1, nc.sync)
         square(4)
         signum(7)
         ratio(5)
         y_quantise(0, 2)
         score(3)
-        turn_y(3, 6)
+        turn_y(3, 1)
         store_rows("S", 2, nc.sync)
         square(5)
         ratio(6)
         y_interleave("V", 2, 2)
         score(4)
-        turn_y(4, 5)
+        turn_y(4, 2)
         square(6)
         store_rows("S", 3, nc.sync)
         ratio(7)
         y_quantise(2, 2)
         store_words(0, 4)
         score(5)
-        turn_y(5, 2)
+        turn_y(5, 3)
         square(7)
         store_rows("S", 4, nc.sync)
         score(6)
-        turn_y(6, 4)
+        turn_y(6, 0)
+        y_interleave("S", 4, 2)
         store_rows("S", 5, nc.sync)
         score(7)
-        turn_y(7, 6)
-        y_interleave("V", 4, 2)
+        turn_y(7, 1)
         store_rows("S", 6, nc.sync)
         y_interleave("V", 6, 2)
         y_quantise(4, 2)
-        store_words(4, 2)
         y_quantise(6, 2)
         store_rows("S", 7, nc.scalar)
-        store_words(6, 2)
+        store_words(4, 4)
         for q in range(4):
             (nc.sync, nc.scalar)[q % 2].dma_start(out=out_2[0, 4 * q : 4 * q + 4, :].bitcast(I32), in_=y_q[1][32 * q : 32 * q + 4, 0, :].bitcast(I32))

@@ -30,6 +30,7 @@ GROUPS = HARD + SOFT
 RUN = 4
 RHO_GUARD = 1e-36
 FIRST_SHARE = 224
+OPENING_SHARE = 320
 WAITING = 2
 
 
@@ -56,8 +57,8 @@ def tile_boosting_histogram_step_scores_k6_kernel(
         y_q = planes("y", 1, J)
         hot_w = keep.tile([P, HARD, 2 * BINS], U8, align_bytes=256)
         hot_s = keep.tile([P, HARD, BINS], U8, align_bytes=256)
-        hot_s_raw = keep.tile([P, HARD, BINS], U8, align_bytes=64)
-        ident = keep.tile([P, P], F32)
+        hot_s_raw = keep.tile([P, HARD, BINS], U8, align_bytes=256)
+        ident = keep.tile([P, P], F32, align_bytes=256)
         lam_bf = keep.tile([P, PACK], BF16)
         rho_bf = keep.tile([P, PACK], BF16)
         rho_root = keep.tile([P, PACK], F32)
@@ -81,7 +82,7 @@ def tile_boosting_histogram_step_scores_k6_kernel(
         raw = {}
 
         def load_full(name, src, g):
-            t = work.tile([P, PACK, J], BF16, name="raw_full", bufs=4, align_bytes=64)
+            t = work.tile([P, PACK, J], BF16, name="raw_full", bufs=4, align_bytes=256)
             rows = src[g * K_PASS : (g + 1) * K_PASS, :].rearrange("(a t e) c -> e a t c", t=PACK, e=RUN)
             for e in range(RUN):
                 nc.sync.dma_start(out=t[e:P:RUN, :, :], in_=rows[e])
@@ -89,7 +90,7 @@ def tile_boosting_histogram_step_scores_k6_kernel(
 
         def load_half(key, src, g):
             half = key[2]
-            t = work.tile([P, PACK, W], BF16, name="raw_half", bufs=8)
+            t = work.tile([P, PACK, W], BF16, name="raw_half", bufs=8, align_bytes=256)
             nc.sync.dma_start(out=t[:], in_=rows_of(src, g)[:, :, half * W : (half + 1) * W])
             raw[key] = t[:]
 
@@ -100,7 +101,7 @@ def tile_boosting_histogram_step_scores_k6_kernel(
                 load_half(("gh", k, kind), gh_soft, k - HARD)
 
         def load_hot(k):
-            raw["hot", k] = work.tile([P, BINS // 2], I32, name="raw_hot", bufs=2)
+            raw["hot", k] = work.tile([P, BINS // 2], I32, name="raw_hot", bufs=2, align_bytes=256)
             nc.sync.dma_start(out=raw["hot", k][:], in_=hot_words[k].bitcast(I32))
 
         def deal_hot(k):
@@ -157,7 +158,7 @@ def tile_boosting_histogram_step_scores_k6_kernel(
 
         def group(engine, key, a, b):
             if key not in grouped:
-                grouped[key] = work.tile([P, W, PACK], BF16, name="grouped", bufs=4, align_bytes=64)
+                grouped[key] = work.tile([P, W, PACK], BF16, name="grouped", bufs=4, align_bytes=256)
             if key[0] == "gh":
                 interleave(engine, grouped[key][:, a:b, :], raw[key][:, :, a:b])
             else:
@@ -178,7 +179,7 @@ def tile_boosting_histogram_step_scores_k6_kernel(
 
         def wide_tile(key):
             if key not in grouped:
-                grouped[key] = work.tile([P, J, PACK], BF16, name="grouped_wide", bufs=2, align_bytes=64)
+                grouped[key] = work.tile([P, J, PACK], BF16, name="grouped_wide", bufs=2, align_bytes=256)
             return grouped[key]
 
         def group_table(engine, name, g, jh, a, b):
@@ -214,7 +215,7 @@ def tile_boosting_histogram_step_scores_k6_kernel(
                     stop=(k == GROUPS - 1 and t == PACK - 1),
                 )
 
-        grouped_hist = keep.tile([P, 2 * W * PACK], BF16, align_bytes=64)
+        grouped_hist = keep.tile([P, 2 * W * PACK], BF16, align_bytes=256)
 
         def empty_hist(engine, acc, half, s):
             dst = grouped_hist[:, half * W * PACK : (half + 1) * W * PACK].rearrange("p (u s m t) -> p s u m t", u=PACK, s=4, t=PACK)
@@ -226,8 +227,8 @@ def tile_boosting_histogram_step_scores_k6_kernel(
                 out=hist_q[0][:, kind, a:b].bitcast(FP8X4), scales=hist_q[1][:, kind, a:b], in_=grouped_hist[:, a * PACK : b * PACK]
             )
 
-        y = keep.tile([P, PACK, J], F32)
-        sign = keep.tile([P, PACK, J], BF16)
+        y = keep.tile([P, PACK, J], F32, align_bytes=256)
+        sign = keep.tile([P, PACK, J], BF16, align_bytes=256)
         dens = {}
         nums = {}
         y_turned = {}
@@ -303,7 +304,7 @@ def tile_boosting_histogram_step_scores_k6_kernel(
                 nc.tensor.transpose(y_turned[jb][:, t * P : (t + 1) * P], y[:, t, jb * P : (jb + 1) * P], ident[:])
 
         def store_rows(engine, jb, queue):
-            rows = work.tile([P, P, PACK], F32, name="rows", bufs=5)
+            rows = work.tile([P, P, PACK], F32, name="rows", bufs=5, align_bytes=256)
             copy_on(engine, rows[:], y_turned[jb][:].rearrange("j (t p) -> j p t", t=PACK))
             queue.dma_start(out=out_0[jb * P : (jb + 1) * P, :], in_=rows[:].rearrange("j p t -> j (p t)"))
 
@@ -322,7 +323,7 @@ def tile_boosting_histogram_step_scores_k6_kernel(
             nc.sync.dma_start(out=out_1[0].rearrange("p m t -> p (m t)").bitcast(I32)[:, a:b], in_=y_q[0][:, 0, a:b].bitcast(I32))
 
         def shared(key):
-            cut = FIRST_SHARE if key[0] == "gh" else W // 2
+            cut = OPENING_SHARE if key == FIRST_PIECES[0] else FIRST_SHARE if key[0] == "gh" else W // 2
             group("S", key, cut, W)
             group("V", key, 0, cut)
 

@@ -26,11 +26,12 @@ FIRST_PIECES = (
     ("gh", 0, 1), ("gh", 1, 1), ("gh", 2, 1), ("gh", 4, 1), ("soft", 0, 0),
     ("gh", 3, 1), ("soft", 0, 1), ("gh", 5, 1), ("soft", 1, 0), ("soft", 1, 1),
 )
+HOT_AFTER = {("gh", 1, 1): 1, ("gh", 4, 1): 2, ("soft", 0, 1): 3}
 GROUPS = HARD + SOFT
 RUN = 4
 RHO_GUARD = 1e-36
 FIRST_SHARE = 224
-OPENING_SHARE = 320
+OPENING_SHARE = 160
 WAITING = 2
 
 
@@ -90,7 +91,7 @@ def tile_boosting_histogram_step_scores_k6_kernel(
 
         def load_half(key, src, g):
             half = key[2]
-            t = work.tile([P, PACK, W], BF16, name="raw_half", bufs=8, align_bytes=256)
+            t = work.tile([P, PACK, W], BF16, name="raw_half", bufs=7, align_bytes=256)
             nc.sync.dma_start(out=t[:], in_=rows_of(src, g)[:, :, half * W : (half + 1) * W])
             raw[key] = t[:]
 
@@ -117,23 +118,22 @@ def tile_boosting_histogram_step_scores_k6_kernel(
             )
 
         nc.vector.memset(hot_s_raw[:].rearrange("p g n -> p (g n)").bitcast(I32), 0)
-        make_identity(nc, ident[:])
         nc.scalar.dma_start(out=rho_bf[:], in_=rho.rearrange("(p t) -> p t", t=PACK))
-        nc.scalar.dma_start(out=lam_bf[:], in_=lam.rearrange("(p t) -> p t", t=PACK))
-        nc.scalar.activation(out=rho_root[:], in_=rho_bf[:], func=ACT.Abs_reciprocal_sqrt, bias=RHO_GUARD)
-        nc.scalar.activation(out=rho_sign[:], in_=rho_bf[:], func=ACT.Sign)
+        make_identity(nc, ident[:])
 
         def load_piece(key):
             name, g, half = key
             if name == "soft":
                 load_half(key, soft, g)
             else:
-                if 0 < g < HARD:
-                    load_hot(g)
                 load_gh(g, half)
+            if key in HOT_AFTER:
+                load_hot(HOT_AFTER[key])
 
-        for n, key in enumerate(FIRST_PIECES):
-            load_piece(key)
+        quarters = []
+        for n in range(2):
+            quarters.append(work.tile([P, PACK, W // 2], BF16, name="raw_quarter", bufs=2, align_bytes=256))
+            nc.sync.dma_start(out=quarters[n][:], in_=rows_of(gh_hard, 0)[:, :, W + n * W // 2 : W + (n + 1) * W // 2])
             if n == 0:
                 load_hot(0)
                 for q in range(4):
@@ -141,8 +141,12 @@ def tile_boosting_histogram_step_scores_k6_kernel(
                         out=hot_s_raw[32 * q : 32 * q + 4, :, :].bitcast(I32),
                         in_=hot_scales[:, 4 * q : 4 * q + 4, :].rearrange("g r n -> r g n").bitcast(I32),
                     )
-            if n == 7:
-                break
+        nc.scalar.activation(out=rho_root[:], in_=rho_bf[:], func=ACT.Abs_reciprocal_sqrt, bias=RHO_GUARD)
+        nc.scalar.activation(out=rho_sign[:], in_=rho_bf[:], func=ACT.Sign)
+        for key in FIRST_PIECES[1:8]:
+            load_piece(key)
+            if key == FIRST_PIECES[1]:
+                nc.sync.dma_start(out=lam_bf[:], in_=lam.rearrange("(p t) -> p t", t=PACK))
 
         def late_loads():
             for g in range(2):
@@ -191,11 +195,11 @@ def tile_boosting_histogram_step_scores_k6_kernel(
                 out=codes[:, n, :].bitcast(FP8X4), scales=scales[:, n, :], in_=grouped[name, n][:].rearrange("p c t -> p (c t)")
             )
 
-        def hist_pass(acc, kind, k, half):
+        def hist_pass(acc, kind, k, half, tiles=range(4)):
             if k in (0, GROUPS - 1):
-                order = [(t, s) for s in range(4) for t in range(PACK)]
+                order = [(t, s) for s in tiles for t in range(PACK)]
             else:
-                order = [(t, s) for t in range(PACK) for s in range(4)]
+                order = [(t, s) for t in range(PACK) for s in tiles]
             for t, s in order:
                 tile = slice(W * half + t * P, W * half + (t + 1) * P)
                 if k < HARD:
@@ -323,35 +327,52 @@ def tile_boosting_histogram_step_scores_k6_kernel(
             nc.sync.dma_start(out=out_1[0].rearrange("p m t -> p (m t)").bitcast(I32)[:, a:b], in_=y_q[0][:, 0, a:b].bitcast(I32))
 
         def shared(key):
-            cut = OPENING_SHARE if key == FIRST_PIECES[0] else FIRST_SHARE if key[0] == "gh" else W // 2
+            cut = FIRST_SHARE if key[0] == "gh" and key[2] == 1 else W // 2
             group("S", key, cut, W)
             group("V", key, 0, cut)
 
         first = {(half, s): bank(4 * half + s) for half in range(2) for s in range(4)}
         g_keys = [("gh", k, 0) for k in range(GROUPS)]
         ahead = list(FIRST_PIECES) + g_keys
-        for n, key in enumerate(FIRST_PIECES):
-            if n <= WAITING:
-                shared(key)
-            if n >= WAITING:
-                shared(ahead[n + 1])
+        opening = work.tile([P, W, PACK], BF16, name="grouped", bufs=4, align_bytes=256)
+        for n in range(2):
+            base = n * W // 2
+            interleave("S", opening[:, base + OPENING_SHARE : base + W // 2, :], quarters[n][:, :, OPENING_SHARE:])
+            interleave("V", opening[:, base : base + OPENING_SHARE, :], quarters[n][:, :, :OPENING_SHARE])
             if n == 0:
                 deal_hot(0)
-            quantise(key)
+            else:
+                deal_hot_scales(1, HARD)
+            cols = slice(R + base, R + base + W // 2)
+            nc.vector.quantize_mx(
+                out=gh_q[0][:, 0, cols].bitcast(FP8X4),
+                scales=gh_q[1][:, 0, cols],
+                in_=opening[:, base : base + W // 2, :].rearrange("p c t -> p (c t)"),
+            )
             if n == 0:
                 deal_hot_scales(0, 1)
+            for half in range(2):
+                hist_pass(first, 1, 0, half, range(2 * n, 2 * n + 2))
+        for n, key in enumerate(FIRST_PIECES):
+            if n == 0:
+                continue
+            if n == 1:
+                shared(key)
                 nc.vector.tensor_tensor(out=rho_inv[:], in0=rho_root[:], in1=rho_root[:], op=ALU.mult)
-                nc.vector.tensor_tensor(out=lam_signed[:], in0=lam_bf[:], in1=rho_sign[:], op=ALU.mult)
                 deal_hot(1)
+                quantise(key)
+                shared(ahead[2])
+                nc.vector.tensor_tensor(out=lam_signed[:], in0=lam_bf[:], in1=rho_sign[:], op=ALU.mult)
                 nc.vector.tensor_tensor(out=lam_over_rho[:], in0=lam_bf[:], in1=rho_inv[:], op=ALU.mult)
-                deal_hot_scales(1, HARD)
-            if n in (1, 4):
-                deal_hot(2 + n // 4)
-            if n + 8 < len(ahead):
-                if n + 8 < len(FIRST_PIECES):
-                    load_piece(ahead[n + 8])
-                else:
-                    load_gh(ahead[n + 8][1], 0)
+            else:
+                shared(ahead[n + 1])
+                if n in (2, 5):
+                    deal_hot(2 + n // 5)
+                quantise(key)
+            if n + 7 < len(FIRST_PIECES):
+                load_piece(ahead[n + 7])
+            elif n + 7 < len(ahead):
+                load_gh(ahead[n + 7][1], 0)
             name, g, half = key
             if name == "soft":
                 hist_pass(first, 1, HARD + g, half)
@@ -395,40 +416,40 @@ def tile_boosting_histogram_step_scores_k6_kernel(
         hist_pass(second, 0, 1, 1)
         hist_pass(second, 0, 2, 1)
         group_table("V", "curve", 1, 1, 0, W)
+        group_table("S", "steps", 0, 0, W // 2, W)
+        group_table("V", "steps", 0, 0, 0, W // 2)
         denominator(0, 0)
         denominator(1, 1)
         hist_pass(second, 0, 3, 1)
         denominator(2, 2)
         for n in range(3):
             root_and_sign(n)
-        group_table("V", "steps", 0, 0, 0, W)
+        group_table("V", "steps", 1, 0, 0, W)
         quantise_wide("curve", 1)
         hist_pass(second, 0, 4, 1)
         hist_pass(second, 0, 5, 1)
-        group_table("V", "steps", 1, 0, 0, W)
         quantise_hist(0, 0, 1)
         quantise_wide("steps", 0)
         group_table("V", "steps", 0, 1, 0, W)
+        group_table("V", "steps", 1, 1, 0, W)
         for s in range(4):
             empty_hist("S", second, 1, s)
         for n in range(3, 7):
             denominator(n, (3, 0, 1, 2)[n - 3])
-        group_table("V", "steps", 1, 1, 0, W // 2)
-        quantise_hist(0, 1, 1)
-        group_table("V", "steps", 1, 1, W // 2, W)
         root_and_sign(3)
+        quantise_hist(0, 1, 1)
+        quantise_wide("steps", 1)
 
         for jb in range(4):
             numerator(jb, 4 + jb)
         denominator(7, 3)
         root_and_sign(4)
-        root_and_sign(5)
+        root(5)
         ratio(0)
         ratio(1)
+        ratio(2)
         square(0)
         square(1)
-        quantise_wide("steps", 1)
-        ratio(2)
         score(0)
         numerator(4, 4)
         numerator(5, 5)
@@ -438,25 +459,26 @@ def tile_boosting_histogram_step_scores_k6_kernel(
         square(2)
         ratio(3)
         score(1)
-        numerator(6, 6)
-        numerator(7, 7)
-        turn_y(1, 1)
-        store_rows("S", 0, nc.sync)
+        turn_y(1, 6)
+        signum(5)
         square(3)
-        signum(6)
+        store_rows("S", 0, nc.sync)
         ratio(4)
         y_interleave("V", 0, 2)
         score(2)
+        numerator(6, 7)
         turn_y(2, 0)
+        signum(6)
         store_rows("S", 1, nc.sync)
         square(4)
-        signum(7)
         ratio(5)
         y_quantise(0, 2)
         score(3)
+        numerator(7, 4)
         turn_y(3, 1)
-        store_rows("S", 2, nc.sync)
+        signum(7)
         square(5)
+        store_rows("S", 2, nc.sync)
         ratio(6)
         y_interleave("V", 2, 2)
         score(4)
@@ -472,11 +494,11 @@ def tile_boosting_histogram_step_scores_k6_kernel(
         store_rows("S", 4, nc.sync)
         score(6)
         turn_y(6, 0)
-        y_interleave("S", 4, 2)
         store_rows("S", 5, nc.sync)
         score(7)
         turn_y(7, 1)
         store_rows("S", 6, nc.sync)
+        y_interleave("V", 4, 2)
         y_interleave("V", 6, 2)
         y_quantise(4, 2)
         y_quantise(6, 2)

@@ -20,19 +20,26 @@ P = 128
 PACK = 4
 K_PASS = P * PACK
 W = 512
+RUN = 4
+WALK = 8
+ALIGN = 256
 HARD = N1 // K_PASS
 SOFT = N2 // K_PASS
-FIRST_PIECES = (
-    ("gh", 0, 1), ("gh", 1, 1), ("gh", 2, 1), ("gh", 4, 1), ("soft", 0, 0),
-    ("gh", 3, 1), ("soft", 0, 1), ("gh", 5, 1), ("soft", 1, 0), ("soft", 1, 1),
-)
-HOT_AFTER = {("gh", 1, 1): 1, ("gh", 4, 1): 2, ("soft", 0, 1): 3}
 GROUPS = HARD + SOFT
-RUN = 4
+CHUNKS = J // P
+GRAD, CURV = 0, 1
 RHO_GUARD = 1e-36
-FIRST_SHARE = 224
+
+FIRST_PIECES = (
+    ("gh", 0, CURV), ("gh", 1, CURV), ("gh", 2, CURV), ("gh", 4, CURV), ("soft", 0, 0),
+    ("gh", 3, CURV), ("soft", 0, 1), ("gh", 5, CURV), ("soft", 1, 0), ("soft", 1, 1),
+)
+HOT_AFTER = {("gh", 1, CURV): 1, ("gh", 4, CURV): 2, ("soft", 0, 1): 3}
+RAW_SLOTS = 7
 OPENING_SHARE = 160
-WAITING = 2
+FIRST_SHARE = 224
+NUM_BANKS = (4, 5, 6, 7, 4, 5, 7, 4)
+TURN_BANKS = (0, 6, 0, 1, 2, 3, 0, 1)
 
 
 def tile_boosting_histogram_step_scores_k6_kernel(
@@ -46,20 +53,20 @@ def tile_boosting_histogram_step_scores_k6_kernel(
         ctx.enter_context(tc.manual_schedule())
 
         def planes(name, groups, width):
-            codes = keep.tile([P, groups, width], U32, name=name + "_codes", align_bytes=256)
-            scales = keep.tile([P, groups, width], U8, name=name + "_scales", align_bytes=256)
+            codes = keep.tile([P, groups, width], U32, name=name + "_codes", align_bytes=ALIGN)
+            scales = keep.tile([P, groups, width], U8, name=name + "_scales", align_bytes=ALIGN)
             return codes, scales
 
-        gh_q = planes("gh", HARD + SOFT, 2 * R)
+        gh_q = planes("gh", GROUPS, 2 * R)
         soft_q = planes("soft", SOFT, BINS)
         steps_q = planes("steps", 2, J)
         curve_q = planes("curve", 2, J)
         hist_q = planes("hist", 2, 2 * R)
         y_q = planes("y", 1, J)
-        hot_w = keep.tile([P, HARD, 2 * BINS], U8, align_bytes=256)
-        hot_s = keep.tile([P, HARD, BINS], U8, align_bytes=256)
-        hot_s_raw = keep.tile([P, HARD, BINS], U8, align_bytes=256)
-        ident = keep.tile([P, P], F32, align_bytes=256)
+        hot_w = keep.tile([P, HARD, 2 * BINS], U8, align_bytes=ALIGN)
+        hot_s = keep.tile([P, HARD, BINS], U8, align_bytes=ALIGN)
+        hot_s_raw = keep.tile([P, HARD, BINS], U8, align_bytes=ALIGN)
+        ident = keep.tile([P, P], F32, align_bytes=ALIGN)
         lam_bf = keep.tile([P, PACK], BF16)
         rho_bf = keep.tile([P, PACK], BF16)
         rho_root = keep.tile([P, PACK], F32)
@@ -67,6 +74,9 @@ def tile_boosting_histogram_step_scores_k6_kernel(
         rho_sign = keep.tile([P, PACK], F32)
         lam_over_rho = keep.tile([P, PACK], F32)
         lam_signed = keep.tile([P, PACK], F32)
+        grouped_hist = keep.tile([P, 2 * W * PACK], BF16, align_bytes=ALIGN)
+        y = keep.tile([P, PACK, J], F32, align_bytes=ALIGN)
+        sign = keep.tile([P, PACK, J], BF16, align_bytes=ALIGN)
 
         def bank(b):
             return psum.tile([P, W], F32, name="bank%d" % b, tag="bank%d" % b)
@@ -77,33 +87,60 @@ def tile_boosting_histogram_step_scores_k6_kernel(
             else:
                 nc.scalar.copy(out=out, in_=in_)
 
-        def rows_of(src, g):
-            return src[g * K_PASS : (g + 1) * K_PASS, :].rearrange("(p t) c -> p t c", t=PACK)
+        def quantise_into(quantised, n, a, b, src):
+            codes, scales = quantised
+            nc.vector.quantize_mx(out=codes[:, n, a:b].bitcast(FP8X4), scales=scales[:, n, a:b], in_=src)
 
         raw = {}
 
-        def load_full(name, src, g):
-            t = work.tile([P, PACK, J], BF16, name="raw_full", bufs=4, align_bytes=256)
-            rows = src[g * K_PASS : (g + 1) * K_PASS, :].rearrange("(a t e) c -> e a t c", t=PACK, e=RUN)
-            for e in range(RUN):
-                nc.sync.dma_start(out=t[e:P:RUN, :, :], in_=rows[e])
-            raw[name, g] = t[:]
-
-        def load_half(key, src, g):
-            half = key[2]
-            t = work.tile([P, PACK, W], BF16, name="raw_half", bufs=7, align_bytes=256)
-            nc.sync.dma_start(out=t[:], in_=rows_of(src, g)[:, :, half * W : (half + 1) * W])
-            raw[key] = t[:]
-
-        def load_gh(k, kind):
-            if k < HARD:
-                load_half(("gh", k, kind), gh_hard, k)
-            else:
-                load_half(("gh", k, kind), gh_soft, k - HARD)
+        def rows_of(src, g):
+            return src[g * K_PASS : (g + 1) * K_PASS, :].rearrange("(p t) c -> p t c", t=PACK)
 
         def load_hot(k):
-            raw["hot", k] = work.tile([P, BINS // 2], I32, name="raw_hot", bufs=2, align_bytes=256)
+            raw["hot", k] = work.tile([P, BINS // 2], I32, name="raw_hot", bufs=2, align_bytes=ALIGN)
             nc.sync.dma_start(out=raw["hot", k][:], in_=hot_words[k].bitcast(I32))
+
+        def load_piece(key):
+            name, g, half = key
+            if name == "soft":
+                rows = rows_of(soft, g)
+            elif g < HARD:
+                rows = rows_of(gh_hard, g)
+            else:
+                rows = rows_of(gh_soft, g - HARD)
+            raw[key] = work.tile([P, PACK, W], BF16, name="raw_half", bufs=RAW_SLOTS, align_bytes=ALIGN)
+            nc.sync.dma_start(out=raw[key][:], in_=rows[:, :, half * W : (half + 1) * W])
+            if key in HOT_AFTER:
+                load_hot(HOT_AFTER[key])
+
+        def load_table(name, src, g, jh):
+            raw[name, g, jh] = work.tile([P, PACK, W], BF16, name="raw_table", bufs=8, align_bytes=ALIGN)
+            rows = src[g * K_PASS : (g + 1) * K_PASS, jh * W : (jh + 1) * W]
+            rows = rows.rearrange("(a t e) c -> e a t c", t=PACK, e=RUN)
+            for e in range(RUN):
+                nc.sync.dma_start(out=raw[name, g, jh][e:P:RUN, :, :], in_=rows[e])
+
+        nc.vector.memset(hot_s_raw[:].rearrange("p g n -> p (g n)").bitcast(I32), 0)
+        nc.scalar.dma_start(out=rho_bf[:], in_=rho.rearrange("(p t) -> p t", t=PACK))
+        make_identity(nc, ident[:])
+        opening_raw = []
+        for n in range(2):
+            opening_raw.append(work.tile([P, PACK, W // 2], BF16, name="raw_quarter", bufs=2, align_bytes=ALIGN))
+            cols = slice(R + n * W // 2, R + (n + 1) * W // 2)
+            nc.sync.dma_start(out=opening_raw[n][:], in_=rows_of(gh_hard, 0)[:, :, cols])
+            if n == 0:
+                load_hot(0)
+                for q in range(4):
+                    nc.sync.dma_start(
+                        out=hot_s_raw[32 * q : 32 * q + 4, :, :].bitcast(I32),
+                        in_=hot_scales[:, 4 * q : 4 * q + 4, :].rearrange("g r n -> r g n").bitcast(I32),
+                    )
+        nc.scalar.activation(out=rho_root[:], in_=rho_bf[:], func=ACT.Abs_reciprocal_sqrt, bias=RHO_GUARD)
+        nc.scalar.activation(out=rho_sign[:], in_=rho_bf[:], func=ACT.Sign)
+        for key in FIRST_PIECES[1 : 1 + RAW_SLOTS]:
+            load_piece(key)
+
+        grouped = {}
 
         def deal_hot(k):
             nc.vector.tensor_copy(
@@ -117,52 +154,16 @@ def tile_boosting_histogram_step_scores_k6_kernel(
                 in_=hot_s_raw[:, a:b, :].bitcast(I32).rearrange("p k (g a t) -> p (k g) t a", g=2, t=PACK),
             )
 
-        nc.vector.memset(hot_s_raw[:].rearrange("p g n -> p (g n)").bitcast(I32), 0)
-        nc.scalar.dma_start(out=rho_bf[:], in_=rho.rearrange("(p t) -> p t", t=PACK))
-        make_identity(nc, ident[:])
-
-        def load_piece(key):
-            name, g, half = key
-            if name == "soft":
-                load_half(key, soft, g)
-            else:
-                load_gh(g, half)
-            if key in HOT_AFTER:
-                load_hot(HOT_AFTER[key])
-
-        quarters = []
-        for n in range(2):
-            quarters.append(work.tile([P, PACK, W // 2], BF16, name="raw_quarter", bufs=2, align_bytes=256))
-            nc.sync.dma_start(out=quarters[n][:], in_=rows_of(gh_hard, 0)[:, :, W + n * W // 2 : W + (n + 1) * W // 2])
-            if n == 0:
-                load_hot(0)
-                for q in range(4):
-                    nc.sync.dma_start(
-                        out=hot_s_raw[32 * q : 32 * q + 4, :, :].bitcast(I32),
-                        in_=hot_scales[:, 4 * q : 4 * q + 4, :].rearrange("g r n -> r g n").bitcast(I32),
-                    )
-        nc.scalar.activation(out=rho_root[:], in_=rho_bf[:], func=ACT.Abs_reciprocal_sqrt, bias=RHO_GUARD)
-        nc.scalar.activation(out=rho_sign[:], in_=rho_bf[:], func=ACT.Sign)
-        for key in FIRST_PIECES[1:8]:
-            load_piece(key)
-            if key == FIRST_PIECES[1]:
-                nc.sync.dma_start(out=lam_bf[:], in_=lam.rearrange("(p t) -> p t", t=PACK))
-
-        def late_loads():
-            for g in range(2):
-                load_full("curve", curve, g)
-            for g in range(2):
-                load_full("steps", steps, g)
-
-        quantised = {"gh": gh_q, "soft": soft_q}
-        grouped = {}
-
         def interleave(engine, dst, src):
-            copy_on(engine, dst.rearrange("p (c i) t -> p c t i", i=8), src.rearrange("p t (c i) -> p c t i", i=8))
+            copy_on(
+                engine,
+                dst.rearrange("p (c i) t -> p c t i", i=WALK),
+                src.rearrange("p t (c i) -> p c t i", i=WALK),
+            )
 
         def group(engine, key, a, b):
             if key not in grouped:
-                grouped[key] = work.tile([P, W, PACK], BF16, name="grouped", bufs=4, align_bytes=256)
+                grouped[key] = work.tile([P, W, PACK], BF16, name="grouped", bufs=4, align_bytes=ALIGN)
             if key[0] == "gh":
                 interleave(engine, grouped[key][:, a:b, :], raw[key][:, :, a:b])
             else:
@@ -170,30 +171,30 @@ def tile_boosting_histogram_step_scores_k6_kernel(
                 copy_on(
                     engine,
                     grouped[key][:].rearrange("p (t a e) j -> p a t j e", t=PACK, e=RUN)[:, runs],
-                    raw[key].rearrange("p j (a t e) -> p a t j e", t=PACK, e=RUN)[:, runs],
+                    raw[key][:].rearrange("p j (a t e) -> p a t j e", t=PACK, e=RUN)[:, runs],
                 )
+
+        def shared(key):
+            cut = FIRST_SHARE if key[0] == "gh" and key[2] == CURV else W // 2
+            group("S", key, cut, W)
+            group("V", key, 0, cut)
 
         def quantise(key):
             name, g, half = key
-            codes, scales = quantised[name]
-            cols = slice(half * W, (half + 1) * W)
-            nc.vector.quantize_mx(
-                out=codes[:, g, cols].bitcast(FP8X4), scales=scales[:, g, cols], in_=grouped[key][:].rearrange("p c t -> p (c t)")
-            )
+            src = grouped[key][:].rearrange("p c t -> p (c t)")
+            quantise_into(gh_q if name == "gh" else soft_q, g, half * W, (half + 1) * W, src)
 
         def wide_tile(key):
             if key not in grouped:
-                grouped[key] = work.tile([P, J, PACK], BF16, name="grouped_wide", bufs=2, align_bytes=256)
+                grouped[key] = work.tile([P, J, PACK], BF16, name="grouped_wide", bufs=2, align_bytes=ALIGN)
             return grouped[key]
 
         def group_table(engine, name, g, jh, a, b):
-            interleave(engine, wide_tile((name, jh))[:, g * W + a : g * W + b, :], raw[name, g][:, :, jh * W + a : jh * W + b])
+            interleave(engine, wide_tile((name, jh))[:, g * W + a : g * W + b, :], raw[name, g, jh][:, :, a:b])
 
-        def quantise_wide(name, n):
-            codes, scales = curve_q if name == "curve" else steps_q
-            nc.vector.quantize_mx(
-                out=codes[:, n, :].bitcast(FP8X4), scales=scales[:, n, :], in_=grouped[name, n][:].rearrange("p c t -> p (c t)")
-            )
+        def quantise_table(name, jh):
+            src = grouped[name, jh][:].rearrange("p c t -> p (c t)")
+            quantise_into(curve_q if name == "curve" else steps_q, jh, 0, J, src)
 
         def hist_pass(acc, kind, k, half, tiles=range(4)):
             if k in (0, GROUPS - 1):
@@ -219,20 +220,16 @@ def tile_boosting_histogram_step_scores_k6_kernel(
                     stop=(k == GROUPS - 1 and t == PACK - 1),
                 )
 
-        grouped_hist = keep.tile([P, 2 * W * PACK], BF16, align_bytes=256)
-
-        def empty_hist(engine, acc, half, s):
-            dst = grouped_hist[:, half * W * PACK : (half + 1) * W * PACK].rearrange("p (u s m t) -> p s u m t", u=PACK, s=4, t=PACK)
-            copy_on(engine, dst[:, s], acc[half, s][:].rearrange("p (t m u) -> p u m t", t=PACK, u=PACK))
+        def empty_hist(acc, half):
+            dst = grouped_hist[:, half * W * PACK : (half + 1) * W * PACK]
+            dst = dst.rearrange("p (u s m t) -> p s u m t", u=PACK, s=4, t=PACK)
+            for s in range(4):
+                nc.scalar.copy(out=dst[:, s], in_=acc[half, s][:].rearrange("p (t m u) -> p u m t", t=PACK, u=PACK))
 
         def quantise_hist(kind, first_half, count):
             a, b = first_half * W, (first_half + count) * W
-            nc.vector.quantize_mx(
-                out=hist_q[0][:, kind, a:b].bitcast(FP8X4), scales=hist_q[1][:, kind, a:b], in_=grouped_hist[:, a * PACK : b * PACK]
-            )
+            quantise_into(hist_q, kind, a, b, grouped_hist[:, a * PACK : b * PACK])
 
-        y = keep.tile([P, PACK, J], F32, align_bytes=256)
-        sign = keep.tile([P, PACK, J], BF16, align_bytes=256)
         dens = {}
         nums = {}
         y_turned = {}
@@ -241,268 +238,231 @@ def tile_boosting_histogram_step_scores_k6_kernel(
             jh, t = divmod(n, PACK)
             dens[n] = bank(b)
             for g in range(2):
+                tile = slice(g * R + t * P, g * R + (t + 1) * P)
                 nc.tensor.matmul_mx(
                     out=dens[n][:],
-                    lhsT=hist_q[0][:, 1, g * R + t * P : g * R + (t + 1) * P].bitcast(FP8X4),
-                    lhsT_scale=hist_q[1][:, 1, g * R + t * P : g * R + (t + 1) * P],
+                    lhsT=hist_q[0][:, CURV, tile].bitcast(FP8X4),
+                    lhsT_scale=hist_q[1][:, CURV, tile],
                     rhs=curve_q[0][:, jh, g * W : (g + 1) * W].bitcast(FP8X4),
                     rhs_scale=curve_q[1][:, jh, g * W : (g + 1) * W],
                     start=(g == 0),
                     stop=(g == 1),
                 )
 
-        def root(n):
+        def of_denominator(n, dst, func, scale, bias):
             jh, t = divmod(n, PACK)
             nc.scalar.activation(
-                out=y[:, t, jh * W : (jh + 1) * W],
+                out=dst[:, t, jh * W : (jh + 1) * W],
                 in_=dens[n][:],
-                func=ACT.Abs_reciprocal_sqrt,
-                scale=rho_inv[:, t : t + 1],
-                bias=lam_over_rho[:, t : t + 1],
+                func=func,
+                scale=scale[:, t : t + 1],
+                bias=bias[:, t : t + 1],
             )
+
+        def root(n):
+            of_denominator(n, y, ACT.Abs_reciprocal_sqrt, rho_inv, lam_over_rho)
 
         def signum(n):
-            jh, t = divmod(n, PACK)
-            nc.scalar.activation(
-                out=sign[:, t, jh * W : (jh + 1) * W],
-                in_=dens[n][:],
-                func=ACT.Sign,
-                scale=rho_sign[:, t : t + 1],
-                bias=lam_signed[:, t : t + 1],
-            )
+            of_denominator(n, sign, ACT.Sign, rho_sign, lam_signed)
 
-        def root_and_sign(n):
-            root(n)
-            signum(n)
-
-        def numerator(jb, b):
-            nums[jb] = bank(b)
+        def numerator(jb):
+            nums[jb] = bank(NUM_BANKS[jb])
+            jh, part = divmod(jb, PACK)
             for t in range(PACK):
                 for g in range(2):
-                    cols = slice(g * W + jb % 4 * P, g * W + (jb % 4 + 1) * P)
+                    tile = slice(g * R + t * P, g * R + (t + 1) * P)
+                    cols = slice(g * W + part * P, g * W + (part + 1) * P)
                     nc.tensor.matmul_mx(
                         out=nums[jb][:, t * P : (t + 1) * P],
-                        lhsT=hist_q[0][:, 0, g * R + t * P : g * R + (t + 1) * P].bitcast(FP8X4),
-                        lhsT_scale=hist_q[1][:, 0, g * R + t * P : g * R + (t + 1) * P],
-                        rhs=steps_q[0][:, jb // 4, cols].bitcast(FP8X4),
-                        rhs_scale=steps_q[1][:, jb // 4, cols],
+                        lhsT=hist_q[0][:, GRAD, tile].bitcast(FP8X4),
+                        lhsT_scale=hist_q[1][:, GRAD, tile],
+                        rhs=steps_q[0][:, jh, cols].bitcast(FP8X4),
+                        rhs_scale=steps_q[1][:, jh, cols],
                         start=(g == 0),
                         stop=(g == 1),
                     )
 
         def ratio(jb):
             block = y[:, :, jb * P : (jb + 1) * P]
-            nc.vector.tensor_tensor(out=block, in0=nums[jb][:].rearrange("p (t j) -> p t j", t=PACK), in1=block, op=ALU.mult)
+            num = nums[jb][:].rearrange("p (t j) -> p t j", t=PACK)
+            nc.vector.tensor_tensor(out=block, in0=num, in1=block, op=ALU.mult)
 
-        def square(jb, count=1):
-            block = y[:, :, jb * P : (jb + count) * P]
+        def square(jb):
+            block = y[:, :, jb * P : (jb + 1) * P]
             nc.scalar.activation(out=block, in_=block, func=ACT.Square)
 
-        def score(jb, count=1):
-            cols = slice(jb * P, (jb + count) * P)
-            nc.vector.tensor_tensor(out=y[:, :, cols], in0=y[:, :, cols], in1=sign[:, :, cols], op=ALU.mult)
+        def score(jb):
+            block = y[:, :, jb * P : (jb + 1) * P]
+            nc.vector.tensor_tensor(out=block, in0=block, in1=sign[:, :, jb * P : (jb + 1) * P], op=ALU.mult)
 
-        def turn_y(jb, b):
-            y_turned[jb] = bank(b)
+        def turn_y(jb):
+            y_turned[jb] = bank(TURN_BANKS[jb])
             for t in range(PACK):
                 nc.tensor.transpose(y_turned[jb][:, t * P : (t + 1) * P], y[:, t, jb * P : (jb + 1) * P], ident[:])
 
-        def store_rows(engine, jb, queue):
-            rows = work.tile([P, P, PACK], F32, name="rows", bufs=5, align_bytes=256)
-            copy_on(engine, rows[:], y_turned[jb][:].rearrange("j (t p) -> j p t", t=PACK))
+        def store_rows(jb, queue):
+            rows = work.tile([P, P, PACK], F32, name="rows", bufs=5, align_bytes=ALIGN)
+            nc.scalar.copy(out=rows[:], in_=y_turned[jb][:].rearrange("j (t p) -> j p t", t=PACK))
             queue.dma_start(out=out_0[jb * P : (jb + 1) * P, :], in_=rows[:].rearrange("j p t -> j (p t)"))
 
-        def y_interleave(engine, first_jb, count):
-            a, b = first_jb * P, (first_jb + count) * P
-            interleave(engine, wide_tile("y")[:, a:b, :], y[:, :, a:b])
+        def interleave_pair(jb):
+            cols = slice(jb * P, (jb + 2) * P)
+            interleave("V", wide_tile("y")[:, cols, :], y[:, :, cols])
 
-        def y_quantise(first_jb, count):
-            a, b = first_jb * P, (first_jb + count) * P
-            nc.vector.quantize_mx(
-                out=y_q[0][:, 0, a:b].bitcast(FP8X4), scales=y_q[1][:, 0, a:b], in_=grouped["y"][:, a:b, :].rearrange("p c t -> p (c t)")
-            )
+        def quantise_pair(jb):
+            a, b = jb * P, (jb + 2) * P
+            quantise_into(y_q, 0, a, b, grouped["y"][:, a:b, :].rearrange("p c t -> p (c t)"))
 
-        def store_words(first_jb, count):
-            a, b = first_jb * P, (first_jb + count) * P
-            nc.sync.dma_start(out=out_1[0].rearrange("p m t -> p (m t)").bitcast(I32)[:, a:b], in_=y_q[0][:, 0, a:b].bitcast(I32))
-
-        def shared(key):
-            cut = FIRST_SHARE if key[0] == "gh" and key[2] == 1 else W // 2
-            group("S", key, cut, W)
-            group("V", key, 0, cut)
+        def store_words(jh):
+            cols = slice(jh * W, (jh + 1) * W)
+            words = out_1[0].rearrange("p m t -> p (m t)").bitcast(I32)
+            nc.sync.dma_start(out=words[:, cols], in_=y_q[0][:, 0, cols].bitcast(I32))
 
         first = {(half, s): bank(4 * half + s) for half in range(2) for s in range(4)}
-        g_keys = [("gh", k, 0) for k in range(GROUPS)]
-        ahead = list(FIRST_PIECES) + g_keys
-        opening = work.tile([P, W, PACK], BF16, name="grouped", bufs=4, align_bytes=256)
+        grads = [("gh", k, GRAD) for k in range(GROUPS)]
+        ahead = list(FIRST_PIECES) + grads
+        opening = work.tile([P, W, PACK], BF16, name="grouped", bufs=4, align_bytes=ALIGN)
         for n in range(2):
-            base = n * W // 2
-            interleave("S", opening[:, base + OPENING_SHARE : base + W // 2, :], quarters[n][:, :, OPENING_SHARE:])
-            interleave("V", opening[:, base : base + OPENING_SHARE, :], quarters[n][:, :, :OPENING_SHARE])
+            a, b = n * W // 2, (n + 1) * W // 2
+            interleave("S", opening[:, a + OPENING_SHARE : b, :], opening_raw[n][:, :, OPENING_SHARE:])
+            interleave("V", opening[:, a : a + OPENING_SHARE, :], opening_raw[n][:, :, :OPENING_SHARE])
             if n == 0:
                 deal_hot(0)
             else:
                 deal_hot_scales(1, HARD)
-            cols = slice(R + base, R + base + W // 2)
-            nc.vector.quantize_mx(
-                out=gh_q[0][:, 0, cols].bitcast(FP8X4),
-                scales=gh_q[1][:, 0, cols],
-                in_=opening[:, base : base + W // 2, :].rearrange("p c t -> p (c t)"),
-            )
+            quantise_into(gh_q, 0, R + a, R + b, opening[:, a:b, :].rearrange("p c t -> p (c t)"))
             if n == 0:
                 deal_hot_scales(0, 1)
             for half in range(2):
-                hist_pass(first, 1, 0, half, range(2 * n, 2 * n + 2))
-        for n, key in enumerate(FIRST_PIECES):
-            if n == 0:
-                continue
+                hist_pass(first, CURV, 0, half, range(2 * n, 2 * n + 2))
+        for n in range(1, len(FIRST_PIECES)):
+            name, g, half = FIRST_PIECES[n]
             if n == 1:
-                shared(key)
+                shared(FIRST_PIECES[n])
                 nc.vector.tensor_tensor(out=rho_inv[:], in0=rho_root[:], in1=rho_root[:], op=ALU.mult)
-                deal_hot(1)
-                quantise(key)
-                shared(ahead[2])
-                nc.vector.tensor_tensor(out=lam_signed[:], in0=lam_bf[:], in1=rho_sign[:], op=ALU.mult)
-                nc.vector.tensor_tensor(out=lam_over_rho[:], in0=lam_bf[:], in1=rho_inv[:], op=ALU.mult)
+                deal_hot(g)
+                quantise(FIRST_PIECES[n])
+                shared(ahead[n + 1])
             else:
                 shared(ahead[n + 1])
-                if n in (2, 5):
-                    deal_hot(2 + n // 5)
-                quantise(key)
-            if n + 7 < len(FIRST_PIECES):
-                load_piece(ahead[n + 7])
-            elif n + 7 < len(ahead):
-                load_gh(ahead[n + 7][1], 0)
-            name, g, half = key
+                if name == "gh" and g < HARD:
+                    deal_hot(g)
+                quantise(FIRST_PIECES[n])
+            if n + RAW_SLOTS < len(ahead):
+                load_piece(ahead[n + RAW_SLOTS])
             if name == "soft":
-                hist_pass(first, 1, HARD + g, half)
+                hist_pass(first, CURV, HARD + g, half)
             elif g < HARD:
-                hist_pass(first, 1, g, 0)
-                hist_pass(first, 1, g, 1)
-        late_loads()
+                hist_pass(first, CURV, g, 0)
+                hist_pass(first, CURV, g, 1)
+        nc.sync.dma_start(out=lam_bf[:], in_=lam.rearrange("(p t) -> p t", t=PACK))
+        for name, src in (("curve", curve), ("steps", steps)):
+            for jh in range(2):
+                for g in range(2):
+                    load_table(name, src, g, jh)
 
-        quantise(g_keys[0])
-        group("V", g_keys[1], 0, W)
-        group("V", g_keys[2], 0, W // 2)
-        quantise(g_keys[1])
-        group("V", g_keys[2], W // 2, W)
+        quantise(grads[0])
+        group("V", grads[1], 0, W)
+        group("V", grads[2], 0, W // 2)
+        quantise(grads[1])
+        group("V", grads[2], W // 2, W)
         for half in range(2):
-            for s in range(4):
-                empty_hist("S", first, half, s)
+            empty_hist(first, half)
         second = {(half, s): bank(4 * half + s) for half in range(2) for s in range(4)}
-        hist_pass(second, 0, 0, 0)
-        hist_pass(second, 0, 1, 0)
-        hist_pass(second, 0, 0, 1)
-        group("V", g_keys[3], 0, W)
-        quantise(g_keys[2])
-        hist_pass(second, 0, 2, 0)
-        shared(g_keys[4])
-        quantise(g_keys[3])
-        hist_pass(second, 0, 3, 0)
-        shared(g_keys[5])
-        quantise(g_keys[4])
-        hist_pass(second, 0, 4, 0)
+        hist_pass(second, GRAD, 0, 0)
+        hist_pass(second, GRAD, 1, 0)
+        hist_pass(second, GRAD, 0, 1)
+        group("V", grads[3], 0, W)
+        quantise(grads[2])
+        hist_pass(second, GRAD, 2, 0)
+        for k in range(4, GROUPS):
+            shared(grads[k])
+            quantise(grads[k - 1])
+            hist_pass(second, GRAD, k - 1, 0)
         group_table("S", "curve", 0, 0, 0, W)
         group_table("S", "curve", 1, 0, W // 2, W)
-        quantise(g_keys[5])
-        hist_pass(second, 0, 5, 0)
-        quantise_hist(1, 0, 2)
+        quantise(grads[5])
+        hist_pass(second, GRAD, 5, 0)
+        quantise_hist(CURV, 0, 2)
+        nc.vector.tensor_tensor(out=lam_signed[:], in0=lam_bf[:], in1=rho_sign[:], op=ALU.mult)
+        nc.vector.tensor_tensor(out=lam_over_rho[:], in0=lam_bf[:], in1=rho_inv[:], op=ALU.mult)
         group_table("V", "curve", 1, 0, 0, W // 2)
         group_table("V", "curve", 0, 1, 0, W // 2)
-        quantise_wide("curve", 0)
-        for s in range(4):
-            empty_hist("S", second, 0, s)
+        quantise_table("curve", 0)
+        empty_hist(second, 0)
         group_table("S", "curve", 0, 1, W // 2, W)
-        hist_pass(second, 0, 1, 1)
-        hist_pass(second, 0, 2, 1)
+        hist_pass(second, GRAD, 1, 1)
+        hist_pass(second, GRAD, 2, 1)
         group_table("V", "curve", 1, 1, 0, W)
         group_table("S", "steps", 0, 0, W // 2, W)
         group_table("V", "steps", 0, 0, 0, W // 2)
+
         denominator(0, 0)
         denominator(1, 1)
-        hist_pass(second, 0, 3, 1)
+        hist_pass(second, GRAD, 3, 1)
         denominator(2, 2)
         for n in range(3):
-            root_and_sign(n)
+            root(n)
+            signum(n)
         group_table("V", "steps", 1, 0, 0, W)
-        quantise_wide("curve", 1)
-        hist_pass(second, 0, 4, 1)
-        hist_pass(second, 0, 5, 1)
-        quantise_hist(0, 0, 1)
-        quantise_wide("steps", 0)
-        group_table("V", "steps", 0, 1, 0, W)
-        group_table("V", "steps", 1, 1, 0, W)
-        for s in range(4):
-            empty_hist("S", second, 1, s)
+        quantise_table("curve", 1)
+        hist_pass(second, GRAD, 4, 1)
+        hist_pass(second, GRAD, 5, 1)
+        quantise_hist(GRAD, 0, 1)
+        quantise_table("steps", 0)
+        for g in range(2):
+            group_table("V", "steps", g, 1, 0, W)
+        empty_hist(second, 1)
         for n in range(3, 7):
-            denominator(n, (3, 0, 1, 2)[n - 3])
-        root_and_sign(3)
-        quantise_hist(0, 1, 1)
-        quantise_wide("steps", 1)
+            denominator(n, n % 4)
+        root(3)
+        signum(3)
+        quantise_hist(GRAD, 1, 1)
+        quantise_table("steps", 1)
 
         for jb in range(4):
-            numerator(jb, 4 + jb)
+            numerator(jb)
         denominator(7, 3)
-        root_and_sign(4)
+        root(4)
+        signum(4)
         root(5)
-        ratio(0)
-        ratio(1)
-        ratio(2)
-        square(0)
-        square(1)
-        score(0)
-        numerator(4, 4)
-        numerator(5, 5)
-        turn_y(0, 0)
-        root(6)
-        root(7)
-        square(2)
-        ratio(3)
-        score(1)
-        turn_y(1, 6)
-        signum(5)
-        square(3)
-        store_rows("S", 0, nc.sync)
-        ratio(4)
-        y_interleave("V", 0, 2)
-        score(2)
-        numerator(6, 7)
-        turn_y(2, 0)
-        signum(6)
-        store_rows("S", 1, nc.sync)
-        square(4)
-        ratio(5)
-        y_quantise(0, 2)
-        score(3)
-        numerator(7, 4)
-        turn_y(3, 1)
-        signum(7)
-        square(5)
-        store_rows("S", 2, nc.sync)
-        ratio(6)
-        y_interleave("V", 2, 2)
-        score(4)
-        turn_y(4, 2)
-        square(6)
-        store_rows("S", 3, nc.sync)
-        ratio(7)
-        y_quantise(2, 2)
-        store_words(0, 4)
-        score(5)
-        turn_y(5, 3)
-        square(7)
-        store_rows("S", 4, nc.sync)
-        score(6)
-        turn_y(6, 0)
-        store_rows("S", 5, nc.sync)
-        score(7)
-        turn_y(7, 1)
-        store_rows("S", 6, nc.sync)
-        y_interleave("V", 4, 2)
-        y_interleave("V", 6, 2)
-        y_quantise(4, 2)
-        y_quantise(6, 2)
-        store_rows("S", 7, nc.scalar)
-        store_words(4, 4)
+        for jb in range(3):
+            ratio(jb)
+        for jb in range(2):
+            square(jb)
+        for jb in range(CHUNKS):
+            score(jb)
+            if jb == 0:
+                numerator(4)
+                numerator(5)
+            elif jb in (2, 3):
+                numerator(jb + 4)
+            turn_y(jb)
+            if jb == 0:
+                root(6)
+                root(7)
+            elif jb < 4:
+                signum(jb + 4)
+            if jb + 2 < CHUNKS:
+                square(jb + 2)
+            if jb > 0:
+                store_rows(jb - 1, nc.sync)
+            if jb + 3 < CHUNKS:
+                ratio(jb + 3)
+            if jb in (1, 3):
+                interleave_pair(jb - 1)
+            elif jb in (2, 4):
+                quantise_pair(jb - 2)
+            if jb == 4:
+                store_words(0)
+        for jb in (4, 6):
+            interleave_pair(jb)
+        for jb in (4, 6):
+            quantise_pair(jb)
+        store_rows(CHUNKS - 1, nc.scalar)
+        store_words(1)
         for q in range(4):
-            (nc.sync, nc.scalar)[q % 2].dma_start(out=out_2[0, 4 * q : 4 * q + 4, :].bitcast(I32), in_=y_q[1][32 * q : 32 * q + 4, 0, :].bitcast(I32))
+            queue = (nc.sync, nc.scalar)[q % 2]
+            queue.dma_start(
+                out=out_2[0, 4 * q : 4 * q + 4, :].bitcast(I32), in_=y_q[1][32 * q : 32 * q + 4, 0, :].bitcast(I32)
+            )

@@ -65,7 +65,8 @@ def tile_boosting_histogram_step_scores_k6_kernel(
         y_q = planes("y", 1, J)
         hot_w = keep.tile([P, HARD, 2 * BINS], U8, align_bytes=ALIGN)
         hot_s = keep.tile([P, HARD, BINS], U8, align_bytes=ALIGN)
-        hot_s_raw = keep.tile([P, HARD, BINS], U8, align_bytes=ALIGN)
+        hot_s_first = keep.tile([P, 1, BINS], U8, align_bytes=ALIGN)
+        hot_s_rest = keep.tile([P, HARD - 1, BINS], U8, align_bytes=ALIGN)
         ident = keep.tile([P, P], F32, align_bytes=ALIGN)
         lam_bf = keep.tile([P, PACK], BF16)
         rho_bf = keep.tile([P, PACK], BF16)
@@ -112,6 +113,8 @@ def tile_boosting_histogram_step_scores_k6_kernel(
             nc.sync.dma_start(out=raw[key][:], in_=rows[:, :, half * W : (half + 1) * W])
             if key in HOT_AFTER:
                 load_hot(HOT_AFTER[key])
+            if key == FIRST_PIECES[1]:
+                load_hot_scales(hot_s_rest, 1, HARD)
 
         def load_table(name, src, g, jh):
             raw[name, g, jh] = work.tile([P, PACK, W], BF16, name="raw_table", bufs=8, align_bytes=ALIGN)
@@ -120,7 +123,15 @@ def tile_boosting_histogram_step_scores_k6_kernel(
             for e in range(RUN):
                 nc.sync.dma_start(out=raw[name, g, jh][e:P:RUN, :, :], in_=rows[e])
 
-        nc.vector.memset(hot_s_raw[:].rearrange("p g n -> p (g n)").bitcast(I32), 0)
+        def load_hot_scales(dst, a, b):
+            for r in range(4):
+                nc.sync.dma_start(
+                    out=dst[r:P:32, :, :].bitcast(I32),
+                    in_=hot_scales[a:b, r:16:4, :].rearrange("g q n -> q g n").bitcast(I32),
+                )
+
+        for dst in (hot_s_first, hot_s_rest):
+            nc.gpsimd.memset(dst[:].rearrange("p g n -> p (g n)").bitcast(I32), 0)
         nc.scalar.dma_start(out=rho_bf[:], in_=rho.rearrange("(p t) -> p t", t=PACK))
         make_identity(nc, ident[:])
         opening_raw = []
@@ -130,11 +141,7 @@ def tile_boosting_histogram_step_scores_k6_kernel(
             nc.sync.dma_start(out=opening_raw[n][:], in_=rows_of(gh_hard, 0)[:, :, cols])
             if n == 0:
                 load_hot(0)
-                for q in range(4):
-                    nc.sync.dma_start(
-                        out=hot_s_raw[32 * q : 32 * q + 4, :, :].bitcast(I32),
-                        in_=hot_scales[:, 4 * q : 4 * q + 4, :].rearrange("g r n -> r g n").bitcast(I32),
-                    )
+                load_hot_scales(hot_s_first, 0, 1)
         nc.scalar.activation(out=rho_root[:], in_=rho_bf[:], func=ACT.Abs_reciprocal_sqrt, bias=RHO_GUARD)
         nc.scalar.activation(out=rho_sign[:], in_=rho_bf[:], func=ACT.Sign)
         for key in FIRST_PIECES[1 : 1 + RAW_SLOTS]:
@@ -148,10 +155,10 @@ def tile_boosting_histogram_step_scores_k6_kernel(
                 in_=raw["hot", k][:].rearrange("p (g a t w) -> p g t a w", g=2, t=PACK, w=2),
             )
 
-        def deal_hot_scales(a, b):
+        def deal_hot_scales(src, a, b):
             nc.vector.tensor_copy(
                 out=hot_s[:, a:b, :].bitcast(I32).rearrange("p k (g t a) -> p (k g) t a", g=2, t=PACK),
-                in_=hot_s_raw[:, a:b, :].bitcast(I32).rearrange("p k (g a t) -> p (k g) t a", g=2, t=PACK),
+                in_=src[:].bitcast(I32).rearrange("p k (g a t) -> p (k g) t a", g=2, t=PACK),
             )
 
         def interleave(engine, dst, src):
@@ -328,11 +335,9 @@ def tile_boosting_histogram_step_scores_k6_kernel(
             interleave("V", opening[:, a : a + OPENING_SHARE, :], opening_raw[n][:, :, :OPENING_SHARE])
             if n == 0:
                 deal_hot(0)
-            else:
-                deal_hot_scales(1, HARD)
             quantise_into(gh_q, 0, R + a, R + b, opening[:, a:b, :].rearrange("p c t -> p (c t)"))
             if n == 0:
-                deal_hot_scales(0, 1)
+                deal_hot_scales(hot_s_first, 0, 1)
             for half in range(2):
                 hist_pass(first, CURV, 0, half, range(2 * n, 2 * n + 2))
         for n in range(1, len(FIRST_PIECES)):
@@ -342,6 +347,7 @@ def tile_boosting_histogram_step_scores_k6_kernel(
                 nc.vector.tensor_tensor(out=rho_inv[:], in0=rho_root[:], in1=rho_root[:], op=ALU.mult)
                 deal_hot(g)
                 quantise(FIRST_PIECES[n])
+                deal_hot_scales(hot_s_rest, 1, HARD)
                 shared(ahead[n + 1])
             else:
                 shared(ahead[n + 1])

@@ -28,7 +28,7 @@ SOFT = N2 // K_PASS
 GROUPS = HARD + SOFT
 CHUNKS = J // P
 GRAD, CURV = 0, 1
-RHO_GUARD = 1e-36
+GUARD_EXPONENT = 80
 
 FIRST_PIECES = (
     ("gh", 0, CURV), ("gh", 1, CURV), ("gh", 2, CURV), ("gh", 4, CURV), ("soft", 0, 0),
@@ -68,6 +68,7 @@ def tile_boosting_histogram_step_scores_k6_kernel(
         hot_s_first = keep.tile([P, 1, BINS], U8, align_bytes=ALIGN)
         hot_s_rest = keep.tile([P, HARD - 1, BINS], U8, align_bytes=ALIGN)
         ident = keep.tile([P, P], F32, align_bytes=ALIGN)
+        guard = keep.tile([P, 3], F32)
         lam_bf = keep.tile([P, PACK], BF16)
         rho_bf = keep.tile([P, PACK], BF16)
         rho_root = keep.tile([P, PACK], F32)
@@ -130,9 +131,11 @@ def tile_boosting_histogram_step_scores_k6_kernel(
                     in_=hot_scales[a:b, r:16:4, :].rearrange("g q n -> q g n").bitcast(I32),
                 )
 
+        nc.gpsimd.memset(guard[:, 0:1], 2.0**GUARD_EXPONENT)
+        nc.scalar.activation(out=guard[:, 1:2], in_=guard[:, 0:1], func=ACT.Abs_reciprocal_sqrt)
+        nc.scalar.activation(out=guard[:, 2:3], in_=guard[:, 1:2], func=ACT.Square)
         for dst in (hot_s_first, hot_s_rest):
             nc.gpsimd.memset(dst[:].rearrange("p g n -> p (g n)").bitcast(I32), 0)
-        nc.scalar.dma_start(out=rho_bf[:], in_=rho.rearrange("(p t) -> p t", t=PACK))
         make_identity(nc, ident[:])
         opening_raw = []
         for n in range(2):
@@ -142,8 +145,6 @@ def tile_boosting_histogram_step_scores_k6_kernel(
             if n == 0:
                 load_hot(0)
                 load_hot_scales(hot_s_first, 0, 1)
-        nc.scalar.activation(out=rho_root[:], in_=rho_bf[:], func=ACT.Abs_reciprocal_sqrt, bias=RHO_GUARD)
-        nc.scalar.activation(out=rho_sign[:], in_=rho_bf[:], func=ACT.Sign)
         for key in FIRST_PIECES[1 : 1 + RAW_SLOTS]:
             load_piece(key)
 
@@ -320,8 +321,8 @@ def tile_boosting_histogram_step_scores_k6_kernel(
             a, b = jb * P, (jb + 2) * P
             quantise_into(y_q, 0, a, b, grouped["y"][:, a:b, :].rearrange("p c t -> p (c t)"))
 
-        def store_words(jh):
-            cols = slice(jh * W, (jh + 1) * W)
+        def store_words(a, b):
+            cols = slice(a * P, b * P)
             words = out_1[0].rearrange("p m t -> p (m t)").bitcast(I32)
             nc.sync.dma_start(out=words[:, cols], in_=y_q[0][:, 0, cols].bitcast(I32))
 
@@ -344,7 +345,6 @@ def tile_boosting_histogram_step_scores_k6_kernel(
             name, g, half = FIRST_PIECES[n]
             if n == 1:
                 shared(FIRST_PIECES[n])
-                nc.vector.tensor_tensor(out=rho_inv[:], in0=rho_root[:], in1=rho_root[:], op=ALU.mult)
                 deal_hot(g)
                 quantise(FIRST_PIECES[n])
                 deal_hot_scales(hot_s_rest, 1, HARD)
@@ -361,6 +361,7 @@ def tile_boosting_histogram_step_scores_k6_kernel(
             elif g < HARD:
                 hist_pass(first, CURV, g, 0)
                 hist_pass(first, CURV, g, 1)
+        nc.sync.dma_start(out=rho_bf[:], in_=rho.rearrange("(p t) -> p t", t=PACK))
         nc.sync.dma_start(out=lam_bf[:], in_=lam.rearrange("(p t) -> p t", t=PACK))
         for name, src in (("curve", curve), ("steps", steps)):
             for jh in range(2):
@@ -385,14 +386,17 @@ def tile_boosting_histogram_step_scores_k6_kernel(
             shared(grads[k])
             quantise(grads[k - 1])
             hist_pass(second, GRAD, k - 1, 0)
+        nc.scalar.activation(out=rho_root[:], in_=rho_bf[:], func=ACT.Abs_reciprocal_sqrt, bias=guard[:, 2:3])
+        nc.scalar.activation(out=rho_sign[:], in_=rho_bf[:], func=ACT.Sign)
         group_table("S", "curve", 0, 0, 0, W)
         group_table("S", "curve", 1, 0, W // 2, W)
         quantise(grads[5])
         hist_pass(second, GRAD, 5, 0)
         quantise_hist(CURV, 0, 2)
+        nc.vector.tensor_tensor(out=rho_inv[:], in0=rho_root[:], in1=rho_root[:], op=ALU.mult)
         nc.vector.tensor_tensor(out=lam_signed[:], in0=lam_bf[:], in1=rho_sign[:], op=ALU.mult)
-        nc.vector.tensor_tensor(out=lam_over_rho[:], in0=lam_bf[:], in1=rho_inv[:], op=ALU.mult)
         group_table("V", "curve", 1, 0, 0, W // 2)
+        nc.vector.tensor_tensor(out=lam_over_rho[:], in0=lam_bf[:], in1=rho_inv[:], op=ALU.mult)
         group_table("V", "curve", 0, 1, 0, W // 2)
         quantise_table("curve", 0)
         empty_hist(second, 0)
@@ -460,15 +464,14 @@ def tile_boosting_histogram_step_scores_k6_kernel(
             elif jb in (2, 4):
                 quantise_pair(jb - 2)
             if jb == 4:
-                store_words(0)
+                store_words(0, 4)
         for jb in (4, 6):
             interleave_pair(jb)
-        for jb in (4, 6):
-            quantise_pair(jb)
+        quantise_pair(4)
+        store_words(4, 6)
+        quantise_pair(6)
+        store_words(6, 8)
         store_rows(CHUNKS - 1, nc.scalar)
-        store_words(1)
-        for q in range(4):
-            queue = (nc.sync, nc.scalar)[q % 2]
-            queue.dma_start(
-                out=out_2[0, 4 * q : 4 * q + 4, :].bitcast(I32), in_=y_q[1][32 * q : 32 * q + 4, 0, :].bitcast(I32)
-            )
+        for r in range(4):
+            queue = (nc.sync, nc.scalar)[r % 2]
+            queue.dma_start(out=out_2[0, r:16:4, :].bitcast(I32), in_=y_q[1][r:P:32, 0, :].bitcast(I32))

@@ -165,8 +165,8 @@ def tile_boosting_histogram_step_scores_k6_kernel(
         def interleave(engine, dst, src):
             copy_on(
                 engine,
-                dst.rearrange("p (c i) t -> p c t i", i=WALK),
-                src.rearrange("p t (c i) -> p c t i", i=WALK),
+                dst.rearrange("p (c i) (h l) -> p c h i l", i=WALK, l=2),
+                src.rearrange("p (h l) (c i) -> p c h i l", i=WALK, l=2),
             )
 
         def group(engine, key, a, b):

@@ -23,6 +23,7 @@ W = 512
 RUN = 4
 WALK = 8
 ALIGN = 256
+ROW_ALIGN = 1024
 HARD = N1 // K_PASS
 SOFT = N2 // K_PASS
 GROUPS = HARD + SOFT
@@ -99,7 +100,7 @@ def tile_boosting_histogram_step_scores_k6_kernel(
             return src[g * K_PASS : (g + 1) * K_PASS, :].rearrange("(p t) c -> p t c", t=PACK)
 
         def load_hot(k):
-            raw["hot", k] = work.tile([P, BINS // 2], I32, name="raw_hot", bufs=2, align_bytes=ALIGN)
+            raw["hot", k] = work.tile([P, BINS // 2], I32, name="raw_hot", bufs=2, align_bytes=ROW_ALIGN)
             nc.sync.dma_start(out=raw["hot", k][:], in_=hot_words[k].bitcast(I32))
 
         def load_piece(key):
@@ -110,7 +111,7 @@ def tile_boosting_histogram_step_scores_k6_kernel(
                 rows = rows_of(gh_hard, g)
             else:
                 rows = rows_of(gh_soft, g - HARD)
-            raw[key] = work.tile([P, PACK, W], BF16, name="raw_half", bufs=RAW_SLOTS, align_bytes=ALIGN)
+            raw[key] = work.tile([P, PACK, W], BF16, name="raw_half", bufs=RAW_SLOTS, align_bytes=ROW_ALIGN)
             nc.sync.dma_start(out=raw[key][:], in_=rows[:, :, half * W : (half + 1) * W])
             if key in HOT_AFTER:
                 load_hot(HOT_AFTER[key])
@@ -118,7 +119,7 @@ def tile_boosting_histogram_step_scores_k6_kernel(
                 load_hot_scales(hot_s_rest, 1, HARD)
 
         def load_table(name, src, g, jh):
-            raw[name, g, jh] = work.tile([P, PACK, W], BF16, name="raw_table", bufs=8, align_bytes=ALIGN)
+            raw[name, g, jh] = work.tile([P, PACK, W], BF16, name="raw_table", bufs=6, align_bytes=ALIGN)
             rows = src[g * K_PASS : (g + 1) * K_PASS, jh * W : (jh + 1) * W]
             rows = rows.rearrange("(a t e) c -> e a t c", t=PACK, e=RUN)
             for e in range(RUN):

@@ -153,14 +153,14 @@ def tile_boosting_histogram_step_scores_k6_kernel(
 
         def deal_hot(k):
             nc.vector.tensor_copy(
-                out=hot_w[:, k, :].bitcast(I32).rearrange("p (g t a w) -> p g t a w", g=2, t=PACK, w=2),
-                in_=raw["hot", k][:].rearrange("p (g a t w) -> p g t a w", g=2, t=PACK, w=2),
+                out=hot_w[:, k, :].bitcast(I32).rearrange("p (g t a w) -> p g a t w", g=2, t=PACK, w=2),
+                in_=raw["hot", k][:].rearrange("p (g a t w) -> p g a t w", g=2, t=PACK, w=2),
             )
 
         def deal_hot_scales(src, a, b):
             nc.vector.tensor_copy(
-                out=hot_s[:, a:b, :].bitcast(I32).rearrange("p k (g t a) -> p (k g) t a", g=2, t=PACK),
-                in_=src[:].bitcast(I32).rearrange("p k (g a t) -> p (k g) t a", g=2, t=PACK),
+                out=hot_s[:, a:b, :].bitcast(I32).rearrange("p k (g t a) -> p (k g) a t", g=2, t=PACK),
+                in_=src[:].bitcast(I32).rearrange("p k (g a t) -> p (k g) a t", g=2, t=PACK),
             )
 
         def interleave(engine, dst, src):
@@ -188,10 +188,10 @@ def tile_boosting_histogram_step_scores_k6_kernel(
             group("S", key, cut, W)
             group("V", key, 0, cut)
 
-        def quantise(key):
+        def quantise(key, a=0, b=W):
             name, g, half = key
-            src = grouped[key][:].rearrange("p c t -> p (c t)")
-            quantise_into(gh_q if name == "gh" else soft_q, g, half * W, (half + 1) * W, src)
+            src = grouped[key][:, a:b, :].rearrange("p c t -> p (c t)")
+            quantise_into(gh_q if name == "gh" else soft_q, g, half * W + a, half * W + b, src)
 
         def wide_tile(key):
             if key not in grouped:
@@ -206,7 +206,7 @@ def tile_boosting_histogram_step_scores_k6_kernel(
             quantise_into(curve_q if name == "curve" else steps_q, jh, 0, J, src)
 
         def hist_pass(acc, kind, k, half, tiles=range(4)):
-            if k in (0, GROUPS - 1):
+            if k in (0, GROUPS - 1) or (kind, k, half) == (GRAD, 1, 0):
                 order = [(t, s) for s in tiles for t in range(PACK)]
             else:
                 order = [(t, s) for t in range(PACK) for s in tiles]
@@ -370,10 +370,11 @@ def tile_boosting_histogram_step_scores_k6_kernel(
                     load_table(name, src, g, jh)
 
         quantise(grads[0])
-        group("V", grads[1], 0, W)
-        group("V", grads[2], 0, W // 2)
-        quantise(grads[1])
-        group("V", grads[2], W // 2, W)
+        group("V", grads[1], 0, W // 2)
+        group("V", grads[1], W // 2, W)
+        quantise(grads[1], 0, W // 2)
+        quantise(grads[1], W // 2, W)
+        group("V", grads[2], 0, W)
         for half in range(2):
             empty_hist(first, half)
         second = {(half, s): bank(4 * half + s) for half in range(2) for s in range(4)}
@@ -382,6 +383,7 @@ def tile_boosting_histogram_step_scores_k6_kernel(
         hist_pass(second, GRAD, 0, 1)
         group("V", grads[3], 0, W)
         quantise(grads[2])
+        hist_pass(second, GRAD, 1, 1)
         hist_pass(second, GRAD, 2, 0)
         for k in range(4, GROUPS):
             shared(grads[k])
@@ -391,6 +393,7 @@ def tile_boosting_histogram_step_scores_k6_kernel(
         nc.scalar.activation(out=rho_sign[:], in_=rho_bf[:], func=ACT.Sign)
         group_table("S", "curve", 0, 0, 0, W)
         group_table("S", "curve", 1, 0, W // 2, W)
+        group_table("S", "curve", 0, 1, W // 2, W)
         quantise(grads[5])
         hist_pass(second, GRAD, 5, 0)
         quantise_hist(CURV, 0, 2)
@@ -401,8 +404,6 @@ def tile_boosting_histogram_step_scores_k6_kernel(
         group_table("V", "curve", 0, 1, 0, W // 2)
         quantise_table("curve", 0)
         empty_hist(second, 0)
-        group_table("S", "curve", 0, 1, W // 2, W)
-        hist_pass(second, GRAD, 1, 1)
         hist_pass(second, GRAD, 2, 1)
         group_table("V", "curve", 1, 1, 0, W)
         group_table("S", "steps", 0, 0, W // 2, W)

@@ -36,9 +36,10 @@ FIRST_PIECES = (
     ("gh", 3, CURV), ("soft", 0, 1), ("gh", 5, CURV), ("soft", 1, 0), ("soft", 1, 1),
 )
 HOT_AFTER = {("gh", 1, CURV): 1, ("gh", 4, CURV): 2, ("soft", 0, 1): 3}
+STEPS_SHARE = 176
 RAW_SLOTS = 7
 OPENING_SHARE = 160
-FIRST_SHARE = 224
+FIRST_SHARE = 256
 NUM_BANKS = (4, 5, 6, 7, 4, 5, 7, 4)
 TURN_BANKS = (0, 6, 0, 1, 2, 3, 0, 1)
 
@@ -309,17 +310,17 @@ def tile_boosting_histogram_step_scores_k6_kernel(
             for t in range(PACK):
                 nc.tensor.transpose(y_turned[jb][:, t * P : (t + 1) * P], y[:, t, jb * P : (jb + 1) * P], ident[:])
 
-        def store_rows(jb, queue):
+        def store_rows(jb, queue, engine="S"):
             rows = work.tile([P, P, PACK], F32, name="rows", bufs=5, align_bytes=ALIGN)
-            nc.scalar.copy(out=rows[:], in_=y_turned[jb][:].rearrange("j (t p) -> j p t", t=PACK))
+            copy_on(engine, rows[:], y_turned[jb][:].rearrange("j (t p) -> j p t", t=PACK))
             queue.dma_start(out=out_0[jb * P : (jb + 1) * P, :], in_=rows[:].rearrange("j p t -> j (p t)"))
 
-        def interleave_pair(jb):
-            cols = slice(jb * P, (jb + 2) * P)
+        def interleave_pair(jb, count=2):
+            cols = slice(jb * P, (jb + count) * P)
             interleave("V", wide_tile("y")[:, cols, :], y[:, :, cols])
 
-        def quantise_pair(jb):
-            a, b = jb * P, (jb + 2) * P
+        def quantise_pair(jb, count=2):
+            a, b = jb * P, (jb + count) * P
             quantise_into(y_q, 0, a, b, grouped["y"][:, a:b, :].rearrange("p c t -> p (c t)"))
 
         def store_words(a, b):
@@ -406,8 +407,8 @@ def tile_boosting_histogram_step_scores_k6_kernel(
         empty_hist(second, 0)
         hist_pass(second, GRAD, 2, 1)
         group_table("V", "curve", 1, 1, 0, W)
-        group_table("S", "steps", 0, 0, W // 2, W)
-        group_table("V", "steps", 0, 0, 0, W // 2)
+        group_table("S", "steps", 0, 0, STEPS_SHARE, W)
+        group_table("V", "steps", 0, 0, 0, STEPS_SHARE)
 
         denominator(0, 0)
         denominator(1, 1)
@@ -432,48 +433,70 @@ def tile_boosting_histogram_step_scores_k6_kernel(
         quantise_hist(GRAD, 1, 1)
         quantise_table("steps", 1)
 
-        for jb in range(4):
-            numerator(jb)
+        for jb in range(4): numerator(jb)
         denominator(7, 3)
         root(4)
         signum(4)
         root(5)
-        for jb in range(3):
-            ratio(jb)
-        for jb in range(2):
-            square(jb)
-        for jb in range(CHUNKS):
-            score(jb)
-            if jb == 0:
-                numerator(4)
-                numerator(5)
-            elif jb in (2, 3):
-                numerator(jb + 4)
-            turn_y(jb)
-            if jb == 0:
-                root(6)
-                root(7)
-            elif jb < 4:
-                signum(jb + 4)
-            if jb + 2 < CHUNKS:
-                square(jb + 2)
-            if jb > 0:
-                store_rows(jb - 1, nc.sync)
-            if jb + 3 < CHUNKS:
-                ratio(jb + 3)
-            if jb in (1, 3):
-                interleave_pair(jb - 1)
-            elif jb in (2, 4):
-                quantise_pair(jb - 2)
-            if jb == 4:
-                store_words(0, 4)
-        for jb in (4, 6):
-            interleave_pair(jb)
+        ratio(0)
+        ratio(1)
+        ratio(2)
+        square(0)
+        square(1)
+        score(0)
+        numerator(4)
+        numerator(5)
+        turn_y(0)
+        root(6)
+        root(7)
+        square(2)
+        ratio(3)
+        score(1)
+        turn_y(1)
+        signum(5)
+        square(3)
+        signum(6)
+        ratio(4)
+        interleave_pair(0)
+        score(2)
+        store_rows(0, nc.sync)
+        numerator(6)
+        turn_y(2)
+        square(4)
+        signum(7)
+        ratio(5)
+        quantise_pair(0)
+        score(3)
+        numerator(7)
+        store_rows(1, nc.sync)
+        turn_y(3)
+        square(5)
+        store_rows(2, nc.sync)
+        ratio(6)
+        interleave_pair(2)
+        score(4)
+        turn_y(4)
+        square(6)
+        ratio(7)
+        quantise_pair(2)
+        store_words(0, 4)
+        score(5)
+        square(7)
+        store_rows(3, nc.sync)
+        turn_y(5)
+        store_rows(4, nc.sync)
+        score(6)
+        turn_y(6)
+        store_rows(5, nc.sync)
+        score(7)
+        turn_y(7)
+        store_rows(6, nc.sync)
+        interleave_pair(4)
+        interleave_pair(6)
         quantise_pair(4)
-        store_words(4, 6)
         quantise_pair(6)
-        store_words(6, 8)
-        store_rows(CHUNKS - 1, nc.scalar)
+        store_words(4, 8)
+        store_rows(7, nc.scalar)
         for r in range(4):
             queue = (nc.sync, nc.scalar)[r % 2]
             queue.dma_start(out=out_2[0, r:16:4, :].bitcast(I32), in_=y_q[1][r:P:32, 0, :].bitcast(I32))

@@ -36,7 +36,7 @@ FIRST_PIECES = (
     ("gh", 3, CURV), ("soft", 0, 1), ("gh", 5, CURV), ("soft", 1, 0), ("soft", 1, 1),
 )
 HOT_AFTER = {("gh", 1, CURV): 1, ("gh", 4, CURV): 2, ("soft", 0, 1): 3}
-STEPS_SHARE = 176
+STEPS_SHARE = 320
 RAW_SLOTS = 7
 OPENING_SHARE = 160
 FIRST_SHARE = 256

@@ -28,6 +28,7 @@ HARD = N1 // K_PASS
 SOFT = N2 // K_PASS
 GROUPS = HARD + SOFT
 CHUNKS = J // P
+Q = J // 4
 GRAD, CURV = 0, 1
 GUARD_EXPONENT = 80
 
@@ -36,12 +37,11 @@ FIRST_PIECES = (
     ("gh", 3, CURV), ("soft", 0, 1), ("gh", 5, CURV), ("soft", 1, 0), ("soft", 1, 1),
 )
 HOT_AFTER = {("gh", 1, CURV): 1, ("gh", 4, CURV): 2, ("soft", 0, 1): 3}
-STEPS_SHARE = 320
+STEPS_SHARE = 256
+ASIDE = 2
 RAW_SLOTS = 7
 OPENING_SHARE = 160
 FIRST_SHARE = 256
-NUM_BANKS = (4, 5, 6, 7, 4, 5, 7, 4)
-TURN_BANKS = (0, 6, 0, 1, 2, 3, 0, 1)
 
 
 def tile_boosting_histogram_step_scores_k6_kernel(
@@ -79,7 +79,10 @@ def tile_boosting_histogram_step_scores_k6_kernel(
         lam_over_rho = keep.tile([P, PACK], F32)
         lam_signed = keep.tile([P, PACK], F32)
         grouped_hist = keep.tile([P, 2 * W * PACK], BF16, align_bytes=ALIGN)
-        y = keep.tile([P, PACK, J], F32, align_bytes=ALIGN)
+        y_all = keep.tile([P, PACK * (Q + J) + 2 * ASIDE * Q], F32, align_bytes=ALIGN)
+        y_rows = y_all[:, : PACK * (Q + J)].rearrange("p (t j) -> p t j", t=PACK)
+        y = y_rows[:, :, Q:]
+        aside = y_rows[:, :2, :Q]
         sign = keep.tile([P, PACK, J], BF16, align_bytes=ALIGN)
 
         def bank(b):
@@ -120,7 +123,7 @@ def tile_boosting_histogram_step_scores_k6_kernel(
                 load_hot_scales(hot_s_rest, 1, HARD)
 
         def load_table(name, src, g, jh):
-            raw[name, g, jh] = work.tile([P, PACK, W], BF16, name="raw_table", bufs=6, align_bytes=ALIGN)
+            raw[name, g, jh] = work.tile([P, PACK, W], BF16, name="raw_table", bufs=5, align_bytes=ALIGN)
             rows = src[g * K_PASS : (g + 1) * K_PASS, jh * W : (jh + 1) * W]
             rows = rows.rearrange("(a t e) c -> e a t c", t=PACK, e=RUN)
             for e in range(RUN):
@@ -275,49 +278,73 @@ def tile_boosting_histogram_step_scores_k6_kernel(
         def signum(n):
             of_denominator(n, sign, ACT.Sign, rho_sign, lam_signed)
 
-        def numerator(jb):
-            nums[jb] = bank(NUM_BANKS[jb])
-            jh, part = divmod(jb, PACK)
-            for t in range(PACK):
-                for g in range(2):
-                    tile = slice(g * R + t * P, g * R + (t + 1) * P)
-                    cols = slice(g * W + part * P, g * W + (part + 1) * P)
-                    nc.tensor.matmul_mx(
-                        out=nums[jb][:, t * P : (t + 1) * P],
-                        lhsT=hist_q[0][:, GRAD, tile].bitcast(FP8X4),
-                        lhsT_scale=hist_q[1][:, GRAD, tile],
-                        rhs=steps_q[0][:, jh, cols].bitcast(FP8X4),
-                        rhs_scale=steps_q[1][:, jh, cols],
-                        start=(g == 0),
-                        stop=(g == 1),
-                    )
+        def numerator_half(n, g, b=None):
+            if g == 0:
+                nums[n] = bank(b)
+            q, h = divmod(n, 2)
+            jh, part = divmod(q, 2)
+            for l in range(2):
+                tile = slice(g * R + (2 * h + l) * P, g * R + (2 * h + l + 1) * P)
+                cols = slice(g * W + part * Q, g * W + (part + 1) * Q)
+                nc.tensor.matmul_mx(
+                    out=nums[n][:, l * Q : (l + 1) * Q],
+                    lhsT=hist_q[0][:, GRAD, tile].bitcast(FP8X4),
+                    lhsT_scale=hist_q[1][:, GRAD, tile],
+                    rhs=steps_q[0][:, jh, cols].bitcast(FP8X4),
+                    rhs_scale=steps_q[1][:, jh, cols],
+                    start=(g == 0 and l == 0),
+                    stop=(g == 1 and l == 1),
+                )
 
-        def ratio(jb):
-            block = y[:, :, jb * P : (jb + 1) * P]
-            num = nums[jb][:].rearrange("p (t j) -> p t j", t=PACK)
-            nc.vector.tensor_tensor(out=block, in0=num, in1=block, op=ALU.mult)
+        def numerator(n, b):
+            numerator_half(n, 0, b)
+            numerator_half(n, 1)
 
-        def square(jb):
-            block = y[:, :, jb * P : (jb + 1) * P]
-            nc.scalar.activation(out=block, in_=block, func=ACT.Square)
+        def unit(tile, n):
+            q, h = divmod(n, 2)
+            return tile[:, 2 * h : 2 * h + 2, q * Q : (q + 1) * Q]
 
-        def score(jb):
-            block = y[:, :, jb * P : (jb + 1) * P]
-            nc.vector.tensor_tensor(out=block, in0=block, in1=sign[:, :, jb * P : (jb + 1) * P], op=ALU.mult)
+        def ratio(n):
+            num = nums[n][:].rearrange("p (l j) -> p l j", l=2)
+            nc.vector.tensor_tensor(out=unit(y, n), in0=num, in1=unit(y, n), op=ALU.mult)
 
-        def turn_y(jb):
-            y_turned[jb] = bank(TURN_BANKS[jb])
-            for t in range(PACK):
-                nc.tensor.transpose(y_turned[jb][:, t * P : (t + 1) * P], y[:, t, jb * P : (jb + 1) * P], ident[:])
+        def square(n):
+            nc.scalar.activation(out=unit(y, n), in_=unit(y, n), func=ACT.Square)
+
+        def score(n, a=0, b=Q):
+            part = unit(y, n)[:, :, a:b]
+            nc.vector.tensor_tensor(out=part, in0=part, in1=unit(sign, n)[:, :, a:b], op=ALU.mult)
+
+        def score_aside(n):
+            nc.gpsimd.tensor_tensor(out=aside, in0=unit(y, n), in1=unit(sign, n), op=ALU.mult)
+
+        def turn_y(jb, b):
+            y_turned[jb] = bank(b)
+            for t in reversed(range(PACK)):
+                if t < 2 and jb // 2 < ASIDE:
+                    src = aside[:, t, (jb % 2) * P : (jb % 2 + 1) * P]
+                else:
+                    src = y[:, t, jb * P : (jb + 1) * P]
+                nc.tensor.transpose(y_turned[jb][:, t * P : (t + 1) * P], src, ident[:])
 
         def store_rows(jb, queue, engine="S"):
             rows = work.tile([P, P, PACK], F32, name="rows", bufs=5, align_bytes=ALIGN)
             copy_on(engine, rows[:], y_turned[jb][:].rearrange("j (t p) -> j p t", t=PACK))
             queue.dma_start(out=out_0[jb * P : (jb + 1) * P, :], in_=rows[:].rearrange("j p t -> j (p t)"))
 
-        def interleave_pair(jb, count=2):
-            cols = slice(jb * P, (jb + count) * P)
-            interleave("V", wide_tile("y")[:, cols, :], y[:, :, cols])
+        def interleave_pair(jb):
+            q = jb // 2
+            dst = wide_tile("y")[:, q * Q : (q + 1) * Q, :]
+            if q >= ASIDE:
+                interleave("V", dst, y[:, :, q * Q : (q + 1) * Q])
+                return
+            far = 2 * (Q + J) + (q + 1) * Q
+            src = y_all[:, : 2 * far].rearrange("p (h x) -> p h x", h=2)[:, :, : 2 * (Q + J)]
+            src = src.rearrange("p h (l x) -> p h l x", l=2)[:, :, :, :Q]
+            nc.vector.tensor_copy(
+                out=dst.rearrange("p (c i) (h l) -> p c h i l", i=WALK, l=2),
+                in_=src.rearrange("p h l (c i) -> p c h i l", i=WALK),
+            )
 
         def quantise_pair(jb, count=2):
             a, b = jb * P, (jb + count) * P
@@ -429,70 +456,73 @@ def tile_boosting_histogram_step_scores_k6_kernel(
         for n in range(3, 7):
             denominator(n, n % 4)
         root(3)
-        signum(3)
+        numerator_half(0, 0, 4)
         quantise_hist(GRAD, 1, 1)
         quantise_table("steps", 1)
-
-        for jb in range(4): numerator(jb)
-        denominator(7, 3)
+        numerator_half(0, 1)
+        for n in range(1, 4):
+            numerator(n, 4 + n)
         root(4)
-        signum(4)
+        signum(3)
+        denominator(7, 3)
         root(5)
-        ratio(0)
-        ratio(1)
-        ratio(2)
-        square(0)
-        square(1)
-        score(0)
-        numerator(4)
-        numerator(5)
-        turn_y(0)
         root(6)
+        ratio(0)
+        numerator(4, 4)
+        ratio(1)
+        square(0)
+        score_aside(0)
+        ratio(2)
+        numerator(5, 5)
+        square(1)
+        signum(4)
+        ratio(3)
+        square(3)
+        ratio(4)
+        numerator(6, 4)
         root(7)
         square(2)
-        ratio(3)
         score(1)
-        turn_y(1)
-        signum(5)
-        square(3)
-        signum(6)
-        ratio(4)
-        interleave_pair(0)
-        score(2)
-        store_rows(0, nc.sync)
-        numerator(6)
-        turn_y(2)
-        square(4)
-        signum(7)
-        ratio(5)
-        quantise_pair(0)
+        turn_y(0, 6)
+        turn_y(1, 0)
+        numerator(7, 7)
         score(3)
-        numerator(7)
-        store_rows(1, nc.sync)
-        turn_y(3)
-        square(5)
-        store_rows(2, nc.sync)
+        interleave_pair(0)
+        score_aside(2)
+        store_rows(0, nc.sync)
+        square(4)
+        signum(5)
+        ratio(5)
         ratio(6)
-        interleave_pair(2)
-        score(4)
-        turn_y(4)
-        square(6)
         ratio(7)
+        store_rows(1, nc.sync, "V")
+        signum(6)
+        square(5)
+        turn_y(2, 1)
+        turn_y(3, 6)
+        signum(7)
+        score(4)
+        quantise_pair(0)
+        square(6)
+        store_rows(2, nc.sync)
+        interleave_pair(2)
+        score(5)
+        turn_y(4, 5)
+        turn_y(5, 4)
+        square(7)
+        score(6)
         quantise_pair(2)
         store_words(0, 4)
-        score(5)
-        square(7)
-        store_rows(3, nc.sync)
-        turn_y(5)
+        store_rows(3, nc.sync, "V")
+        score(7, 0, P)
+        turn_y(6, 2)
+        score(7, P, Q)
+        turn_y(7, 3)
         store_rows(4, nc.sync)
-        score(6)
-        turn_y(6)
-        store_rows(5, nc.sync)
-        score(7)
-        turn_y(7)
-        store_rows(6, nc.sync)
         interleave_pair(4)
+        store_rows(5, nc.sync)
         interleave_pair(6)
+        store_rows(6, nc.sync)
         quantise_pair(4)
         quantise_pair(6)
         store_words(4, 8)

@@ -23,7 +23,7 @@ W = 512
 RUN = 4
 WALK = 8
 ALIGN = 256
-ROW_ALIGN = 1024
+ROW_ALIGN = 256
 HARD = N1 // K_PASS
 SOFT = N2 // K_PASS
 GROUPS = HARD + SOFT
@@ -37,7 +37,7 @@ FIRST_PIECES = (
     ("gh", 3, CURV), ("soft", 0, 1), ("gh", 5, CURV), ("soft", 1, 0), ("soft", 1, 1),
 )
 HOT_AFTER = {("gh", 1, CURV): 1, ("gh", 4, CURV): 2, ("soft", 0, 1): 3}
-STEPS_SHARE = 256
+STEPS_SHARE = 352
 ASIDE = 2
 RAW_SLOTS = 7
 OPENING_SHARE = 160
@@ -79,10 +79,8 @@ def tile_boosting_histogram_step_scores_k6_kernel(
         lam_over_rho = keep.tile([P, PACK], F32)
         lam_signed = keep.tile([P, PACK], F32)
         grouped_hist = keep.tile([P, 2 * W * PACK], BF16, align_bytes=ALIGN)
-        y_all = keep.tile([P, PACK * (Q + J) + 2 * ASIDE * Q], F32, align_bytes=ALIGN)
-        y_rows = y_all[:, : PACK * (Q + J)].rearrange("p (t j) -> p t j", t=PACK)
-        y = y_rows[:, :, Q:]
-        aside = y_rows[:, :2, :Q]
+        y = keep.tile([P, PACK, J], F32, align_bytes=ALIGN)
+        aside = keep.tile([P, 2, PACK, Q], F32, align_bytes=ALIGN)
         sign = keep.tile([P, PACK, J], BF16, align_bytes=ALIGN)
 
         def bank(b):
@@ -209,6 +207,20 @@ def tile_boosting_histogram_step_scores_k6_kernel(
             src = grouped[name, jh][:].rearrange("p c t -> p (c t)")
             quantise_into(curve_q if name == "curve" else steps_q, jh, 0, J, src)
 
+        def quantise_steps(a, b, at):
+            src = grouped["steps", 1][:, at : at + b - a, :].rearrange("p c t -> p (c t)")
+            quantise_into(steps_q, 1, a, b, src)
+
+        def last_steps_on_gpsimd():
+            nc.gpsimd.tensor_scalar(
+                out=grouped["steps", 1][:, :Q, :],
+                in0=raw["steps", 1, 1][:, :, Q:].rearrange("p t c -> p c t"),
+                scalar1=1.0,
+                scalar2=0.0,
+                op0=ALU.mult,
+                op1=ALU.add,
+            )
+
         def hist_pass(acc, kind, k, half, tiles=range(4)):
             if k in (0, GROUPS - 1) or (kind, k, half) == (GRAD, 1, 0):
                 order = [(t, s) for s in tiles for t in range(PACK)]
@@ -311,20 +323,25 @@ def tile_boosting_histogram_step_scores_k6_kernel(
         def square(n):
             nc.scalar.activation(out=unit(y, n), in_=unit(y, n), func=ACT.Square)
 
+        def scores_of(q):
+            if q >= ASIDE:
+                return y[:, :, q * Q : (q + 1) * Q].rearrange("p (h l) j -> p h l j", l=2)
+            if q == 0:
+                return aside[:, 0].rearrange("p (h l) j -> p h l j", l=2)
+            return aside[:, :, :2, :]
+
         def score(n, a=0, b=Q):
             part = unit(y, n)[:, :, a:b]
-            nc.vector.tensor_tensor(out=part, in0=part, in1=unit(sign, n)[:, :, a:b], op=ALU.mult)
+            dst = scores_of(n // 2)[:, n % 2, :, a:b]
+            nc.vector.tensor_tensor(out=dst, in0=part, in1=unit(sign, n)[:, :, a:b], op=ALU.mult)
 
         def score_aside(n):
-            nc.gpsimd.tensor_tensor(out=aside, in0=unit(y, n), in1=unit(sign, n), op=ALU.mult)
+            nc.gpsimd.tensor_tensor(out=aside[:, 0, :2, :], in0=unit(y, n), in1=unit(sign, n), op=ALU.mult)
 
         def turn_y(jb, b):
             y_turned[jb] = bank(b)
             for t in reversed(range(PACK)):
-                if t < 2 and jb // 2 < ASIDE:
-                    src = aside[:, t, (jb % 2) * P : (jb % 2 + 1) * P]
-                else:
-                    src = y[:, t, jb * P : (jb + 1) * P]
+                src = scores_of(jb // 2)[:, t // 2, t % 2, (jb % 2) * P : (jb % 2 + 1) * P]
                 nc.tensor.transpose(y_turned[jb][:, t * P : (t + 1) * P], src, ident[:])
 
         def store_rows(jb, queue, engine="S"):
@@ -335,15 +352,9 @@ def tile_boosting_histogram_step_scores_k6_kernel(
         def interleave_pair(jb):
             q = jb // 2
             dst = wide_tile("y")[:, q * Q : (q + 1) * Q, :]
-            if q >= ASIDE:
-                interleave("V", dst, y[:, :, q * Q : (q + 1) * Q])
-                return
-            far = 2 * (Q + J) + (q + 1) * Q
-            src = y_all[:, : 2 * far].rearrange("p (h x) -> p h x", h=2)[:, :, : 2 * (Q + J)]
-            src = src.rearrange("p h (l x) -> p h l x", l=2)[:, :, :, :Q]
             nc.vector.tensor_copy(
                 out=dst.rearrange("p (c i) (h l) -> p c h i l", i=WALK, l=2),
-                in_=src.rearrange("p h l (c i) -> p c h i l", i=WALK),
+                in_=scores_of(q).rearrange("p h l (c i) -> p c h i l", i=WALK),
             )
 
         def quantise_pair(jb, count=2):
@@ -450,18 +461,21 @@ def tile_boosting_histogram_step_scores_k6_kernel(
         hist_pass(second, GRAD, 5, 1)
         quantise_hist(GRAD, 0, 1)
         quantise_table("steps", 0)
-        for g in range(2):
-            group_table("V", "steps", g, 1, 0, W)
+        group_table("V", "steps", 0, 1, 0, W)
+        group_table("V", "steps", 1, 1, 0, Q)
         empty_hist(second, 1)
         for n in range(3, 7):
             denominator(n, n % 4)
         root(3)
-        numerator_half(0, 0, 4)
+        for n in range(3):
+            numerator_half(n, 0, 4 + n)
         quantise_hist(GRAD, 1, 1)
-        quantise_table("steps", 1)
-        numerator_half(0, 1)
-        for n in range(1, 4):
-            numerator(n, 4 + n)
+        quantise_steps(0, W, 0)
+        quantise_steps(W, W + Q, W)
+        last_steps_on_gpsimd()
+        for n in range(3):
+            numerator_half(n, 1)
+        numerator(3, 7)
         root(4)
         signum(3)
         denominator(7, 3)
@@ -474,46 +488,49 @@ def tile_boosting_histogram_step_scores_k6_kernel(
         score_aside(0)
         ratio(2)
         numerator(5, 5)
-        square(1)
-        signum(4)
-        ratio(3)
-        square(3)
-        ratio(4)
-        numerator(6, 4)
         root(7)
+        square(1)
+        ratio(3)
+        numerator_half(6, 0, 6)
+        ratio(4)
+        square(3)
+        ratio(5)
+        signum(4)
         square(2)
+        numerator_half(7, 0, 7)
+        quantise_steps(W + Q, J, 0)
+        numerator_half(6, 1)
+        numerator_half(7, 1)
         score(1)
-        turn_y(0, 6)
+        turn_y(0, 4)
         turn_y(1, 0)
-        numerator(7, 7)
         score(3)
         interleave_pair(0)
         score_aside(2)
-        store_rows(0, nc.sync)
-        square(4)
         signum(5)
-        ratio(5)
+        square(4)
+        store_rows(0, nc.sync)
         ratio(6)
         ratio(7)
         store_rows(1, nc.sync, "V")
         signum(6)
+        signum(7)
         square(5)
         turn_y(2, 1)
-        turn_y(3, 6)
-        signum(7)
-        score(4)
+        turn_y(3, 5)
         quantise_pair(0)
+        score(4)
         square(6)
         store_rows(2, nc.sync)
         interleave_pair(2)
         score(5)
-        turn_y(4, 5)
+        turn_y(4, 6)
         turn_y(5, 4)
         square(7)
-        score(6)
+        store_rows(3, nc.sync)
         quantise_pair(2)
         store_words(0, 4)
-        store_rows(3, nc.sync, "V")
+        score(6)
         score(7, 0, P)
         turn_y(6, 2)
         score(7, P, Q)

@@ -338,9 +338,10 @@ def tile_boosting_histogram_step_scores_k6_kernel(
         def score_aside(n):
             nc.gpsimd.tensor_tensor(out=aside[:, 0, :2, :], in0=unit(y, n), in1=unit(sign, n), op=ALU.mult)
 
-        def turn_y(jb, b):
-            y_turned[jb] = bank(b)
-            for t in reversed(range(PACK)):
+        def turn_y(jb, h, b=None):
+            if b is not None:
+                y_turned[jb] = bank(b)
+            for t in (2 * h, 2 * h + 1):
                 src = scores_of(jb // 2)[:, t // 2, t % 2, (jb % 2) * P : (jb % 2 + 1) * P]
                 nc.tensor.transpose(y_turned[jb][:, t * P : (t + 1) * P], src, ident[:])
 
@@ -501,9 +502,11 @@ def tile_boosting_histogram_step_scores_k6_kernel(
         quantise_steps(W + Q, J, 0)
         numerator_half(6, 1)
         numerator_half(7, 1)
+        turn_y(0, 0, 4)
+        turn_y(1, 0, 0)
         score(1)
-        turn_y(0, 4)
-        turn_y(1, 0)
+        turn_y(0, 1)
+        turn_y(1, 1)
         score(3)
         interleave_pair(0)
         score_aside(2)
@@ -516,25 +519,31 @@ def tile_boosting_histogram_step_scores_k6_kernel(
         signum(6)
         signum(7)
         square(5)
-        turn_y(2, 1)
-        turn_y(3, 5)
+        turn_y(3, 1, 5)
+        turn_y(2, 1, 1)
+        turn_y(2, 0)
+        turn_y(3, 0)
         quantise_pair(0)
         score(4)
+        turn_y(4, 0, 6)
+        turn_y(5, 0, 4)
         square(6)
         store_rows(2, nc.sync)
         interleave_pair(2)
         score(5)
-        turn_y(4, 6)
-        turn_y(5, 4)
+        turn_y(4, 1)
+        turn_y(5, 1)
         square(7)
         store_rows(3, nc.sync)
         quantise_pair(2)
         store_words(0, 4)
         score(6)
+        turn_y(6, 0, 2)
+        turn_y(7, 0, 3)
         score(7, 0, P)
-        turn_y(6, 2)
+        turn_y(6, 1)
         score(7, P, Q)
-        turn_y(7, 3)
+        turn_y(7, 1)
         store_rows(4, nc.sync)
         interleave_pair(4)
         store_rows(5, nc.sync)

@@ -37,7 +37,7 @@ FIRST_PIECES = (
     ("gh", 3, CURV), ("soft", 0, 1), ("gh", 5, CURV), ("soft", 1, 0), ("soft", 1, 1),
 )
 HOT_AFTER = {("gh", 1, CURV): 1, ("gh", 4, CURV): 2, ("soft", 0, 1): 3}
-STEPS_SHARE = 352
+STEPS_SHARE = 288
 ASIDE = 2
 RAW_SLOTS = 7
 OPENING_SHARE = 160
@@ -206,20 +206,6 @@ def tile_boosting_histogram_step_scores_k6_kernel(
         def quantise_table(name, jh):
             src = grouped[name, jh][:].rearrange("p c t -> p (c t)")
             quantise_into(curve_q if name == "curve" else steps_q, jh, 0, J, src)
-
-        def quantise_steps(a, b, at):
-            src = grouped["steps", 1][:, at : at + b - a, :].rearrange("p c t -> p (c t)")
-            quantise_into(steps_q, 1, a, b, src)
-
-        def last_steps_on_gpsimd():
-            nc.gpsimd.tensor_scalar(
-                out=grouped["steps", 1][:, :Q, :],
-                in0=raw["steps", 1, 1][:, :, Q:].rearrange("p t c -> p c t"),
-                scalar1=1.0,
-                scalar2=0.0,
-                op0=ALU.mult,
-                op1=ALU.add,
-            )
 
         def hist_pass(acc, kind, k, half, tiles=range(4)):
             if k in (0, GROUPS - 1) or (kind, k, half) == (GRAD, 1, 0):
@@ -462,18 +448,18 @@ def tile_boosting_histogram_step_scores_k6_kernel(
         hist_pass(second, GRAD, 5, 1)
         quantise_hist(GRAD, 0, 1)
         quantise_table("steps", 0)
-        group_table("V", "steps", 0, 1, 0, W)
-        group_table("V", "steps", 1, 1, 0, Q)
+        for g in range(2):
+            group_table("V", "steps", g, 1, 0, W)
         empty_hist(second, 1)
         for n in range(3, 7):
             denominator(n, n % 4)
         root(3)
         for n in range(3):
             numerator_half(n, 0, 4 + n)
-        quantise_hist(GRAD, 1, 1)
-        quantise_steps(0, W, 0)
-        quantise_steps(W, W + Q, W)
-        last_steps_on_gpsimd()
+        for h in range(2):
+            a, b = W + h * Q, W + (h + 1) * Q
+            quantise_into(hist_q, GRAD, a, b, grouped_hist[:, a * PACK : b * PACK])
+        quantise_table("steps", 1)
         for n in range(3):
             numerator_half(n, 1)
         numerator(3, 7)
@@ -492,16 +478,13 @@ def tile_boosting_histogram_step_scores_k6_kernel(
         root(7)
         square(1)
         ratio(3)
-        numerator_half(6, 0, 6)
+        numerator(6, 6)
         ratio(4)
         square(3)
         ratio(5)
         signum(4)
         square(2)
-        numerator_half(7, 0, 7)
-        quantise_steps(W + Q, J, 0)
-        numerator_half(6, 1)
-        numerator_half(7, 1)
+        numerator(7, 7)
         turn_y(0, 0, 4)
         turn_y(1, 0, 0)
         score(1)

@@ -321,6 +321,11 @@ def tile_boosting_histogram_step_scores_k6_kernel(
             dst = scores_of(n // 2)[:, n % 2, :, a:b]
             nc.vector.tensor_tensor(out=dst, in0=part, in1=unit(sign, n)[:, :, a:b], op=ALU.mult)
 
+        def square_shared(n):
+            first, second = unit(y, n)[:, 0, :], unit(y, n)[:, 1, :]
+            nc.gpsimd.tensor_tensor(out=first, in0=first, in1=first, op=ALU.mult)
+            nc.scalar.activation(out=second, in_=second, func=ACT.Square)
+
         def score_aside(n):
             nc.gpsimd.tensor_tensor(out=aside[:, 0, :2, :], in0=unit(y, n), in1=unit(sign, n), op=ALU.mult)
 
@@ -468,10 +473,11 @@ def tile_boosting_histogram_step_scores_k6_kernel(
         denominator(7, 3)
         root(5)
         root(6)
+        signum(4)
         ratio(0)
         numerator(4, 4)
         ratio(1)
-        square(0)
+        square_shared(0)
         score_aside(0)
         ratio(2)
         numerator(5, 5)
@@ -482,7 +488,6 @@ def tile_boosting_histogram_step_scores_k6_kernel(
         ratio(4)
         square(3)
         ratio(5)
-        signum(4)
         square(2)
         numerator(7, 7)
         turn_y(0, 0, 4)
@@ -510,31 +515,32 @@ def tile_boosting_histogram_step_scores_k6_kernel(
         score(4)
         turn_y(4, 0, 6)
         turn_y(5, 0, 4)
-        square(6)
         store_rows(2, nc.sync)
+        square(6)
         interleave_pair(2)
         score(5)
         turn_y(4, 1)
         turn_y(5, 1)
-        square(7)
-        store_rows(3, nc.sync)
         quantise_pair(2)
         store_words(0, 4)
+        store_rows(3, nc.sync)
+        square(7)
         score(6)
         turn_y(6, 0, 2)
         turn_y(7, 0, 3)
+        interleave_pair(4)
         score(7, 0, P)
         turn_y(6, 1)
         score(7, P, Q)
         turn_y(7, 1)
         store_rows(4, nc.sync)
-        interleave_pair(4)
+        quantise_pair(4)
+        store_words(4, 6)
         store_rows(5, nc.sync)
         interleave_pair(6)
         store_rows(6, nc.sync)
-        quantise_pair(4)
         quantise_pair(6)
-        store_words(4, 8)
+        store_words(6, 8)
         store_rows(7, nc.scalar)
         for r in range(4):
             queue = (nc.sync, nc.scalar)[r % 2]

from contextlib import ExitStack

import concourse.mybir as mybir
from concourse.masks import make_identity

N1, N2, BINS, R, J = 2048, 1024, 1024, 512, 1024
FLOPS = 2 * (N1 + N2) * BINS * 2 * R + 2 * BINS * J * 2 * R

F32 = mybir.dt.float32
BF16 = mybir.dt.bfloat16
I32 = mybir.dt.int32
U32 = mybir.dt.uint32
U8 = mybir.dt.uint8
FP8X4 = mybir.dt.float8_e4m3fn_x4
FP4X4 = mybir.dt.float4_e2m1fn_x4
ACT = mybir.ActivationFunctionType
ALU = mybir.AluOpType

P = 128
PACK = 4
K_PASS = P * PACK
W = 512
RUN = 4
WALK = 8
ALIGN = 256
ROW_ALIGN = 256
HARD = N1 // K_PASS
SOFT = N2 // K_PASS
GROUPS = HARD + SOFT
CHUNKS = J // P
Q = J // 4
GRAD, CURV = 0, 1
GUARD_EXPONENT = 80

FIRST_PIECES = (
    ("gh", 0, CURV), ("gh", 1, CURV), ("gh", 2, CURV), ("gh", 4, CURV), ("soft", 0, 0),
    ("gh", 3, CURV), ("soft", 0, 1), ("gh", 5, CURV), ("soft", 1, 0), ("soft", 1, 1),
)
HOT_AFTER = {("gh", 1, CURV): 1, ("gh", 4, CURV): 2, ("soft", 0, 1): 3}
STEPS_SHARE = 288
ASIDE = 2
RAW_SLOTS = 7
OPENING_SHARE = 160
FIRST_SHARE = 256


def tile_boosting_histogram_step_scores_k6_kernel(
    tc, gh_hard, hot_words, hot_scales, gh_soft, soft, steps, curve, lam, rho, out_0, out_1, out_2
):
    nc = tc.nc
    with ExitStack() as ctx:
        keep = ctx.enter_context(tc.tile_pool(name="keep", bufs=1))
        work = ctx.enter_context(tc.tile_pool(name="work", bufs=2))
        psum = ctx.enter_context(tc.psum_pool(name="psum", bufs=1))
        ctx.enter_context(tc.manual_schedule())

        def planes(name, groups, width):
            codes = keep.tile([P, groups, width], U32, name=name + "_codes", align_bytes=ALIGN)
            scales = keep.tile([P, groups, width], U8, name=name + "_scales", align_bytes=ALIGN)
            return codes, scales

        gh_q = planes("gh", GROUPS, 2 * R)
        soft_q = planes("soft", SOFT, BINS)
        steps_q = planes("steps", 2, J)
        curve_q = planes("curve", 2, J)
        hist_q = planes("hist", 2, 2 * R)
        y_q = planes("y", 1, J)
        hot_w = keep.tile([P, HARD, 2 * BINS], U8, align_bytes=ALIGN)
        hot_s = keep.tile([P, HARD, BINS], U8, align_bytes=ALIGN)
        hot_s_first = keep.tile([P, 1, BINS], U8, align_bytes=ALIGN)
        hot_s_rest = keep.tile([P, HARD - 1, BINS], U8, align_bytes=ALIGN)
        ident = keep.tile([P, P], F32, align_bytes=ALIGN)
        guard = keep.tile([P, 3], F32)
        lam_bf = keep.tile([P, PACK], BF16)
        rho_bf = keep.tile([P, PACK], BF16)
        rho_root = keep.tile([P, PACK], F32)
        rho_inv = keep.tile([P, PACK], F32)
        rho_sign = keep.tile([P, PACK], F32)
        lam_over_rho = keep.tile([P, PACK], F32)
        lam_signed = keep.tile([P, PACK], F32)
        grouped_hist = keep.tile([P, 2 * W * PACK], BF16, align_bytes=ALIGN)
        y = keep.tile([P, PACK, J], F32, align_bytes=ALIGN)
        aside = keep.tile([P, 2, PACK, Q], F32, align_bytes=ALIGN)
        sign = keep.tile([P, PACK, J], BF16, align_bytes=ALIGN)

        def bank(b):
            return psum.tile([P, W], F32, name="bank%d" % b, tag="bank%d" % b)

        def copy_on(engine, out, in_):
            if engine == "V":
                nc.vector.tensor_copy(out=out, in_=in_)
            else:
                nc.scalar.copy(out=out, in_=in_)

        def quantise_into(quantised, n, a, b, src):
            codes, scales = quantised
            nc.vector.quantize_mx(out=codes[:, n, a:b].bitcast(FP8X4), scales=scales[:, n, a:b], in_=src)

        raw = {}

        def rows_of(src, g):
            return src[g * K_PASS : (g + 1) * K_PASS, :].rearrange("(p t) c -> p t c", t=PACK)

        def load_hot(k):
            raw["hot", k] = work.tile([P, BINS // 2], I32, name="raw_hot", bufs=2, align_bytes=ROW_ALIGN)
            nc.sync.dma_start(out=raw["hot", k][:], in_=hot_words[k].bitcast(I32))

        def load_piece(key):
            name, g, half = key
            if name == "soft":
                rows = rows_of(soft, g)
            elif g < HARD:
                rows = rows_of(gh_hard, g)
            else:
                rows = rows_of(gh_soft, g - HARD)
            raw[key] = work.tile([P, PACK, W], BF16, name="raw_half", bufs=RAW_SLOTS, align_bytes=ROW_ALIGN)
            nc.sync.dma_start(out=raw[key][:], in_=rows[:, :, half * W : (half + 1) * W])
            if key in HOT_AFTER:
                load_hot(HOT_AFTER[key])
            if key == FIRST_PIECES[1]:
                load_hot_scales(hot_s_rest, 1, HARD)

        def load_table(name, src, g, jh):
            raw[name, g, jh] = work.tile([P, PACK, W], BF16, name="raw_table", bufs=5, align_bytes=ALIGN)
            rows = src[g * K_PASS : (g + 1) * K_PASS, jh * W : (jh + 1) * W]
            rows = rows.rearrange("(a t e) c -> e a t c", t=PACK, e=RUN)
            for e in range(RUN):
                nc.sync.dma_start(out=raw[name, g, jh][e:P:RUN, :, :], in_=rows[e])

        def load_hot_scales(dst, a, b):
            for r in range(4):
                nc.sync.dma_start(
                    out=dst[r:P:32, :, :].bitcast(I32),
                    in_=hot_scales[a:b, r:16:4, :].rearrange("g q n -> q g n").bitcast(I32),
                )

        nc.gpsimd.memset(guard[:, 0:1], 2.0**GUARD_EXPONENT)
        nc.scalar.activation(out=guard[:, 1:2], in_=guard[:, 0:1], func=ACT.Abs_reciprocal_sqrt)
        nc.scalar.activation(out=guard[:, 2:3], in_=guard[:, 1:2], func=ACT.Square)
        for dst in (hot_s_first, hot_s_rest):
            nc.gpsimd.memset(dst[:].rearrange("p g n -> p (g n)").bitcast(I32), 0)
        make_identity(nc, ident[:])
        opening_raw = []
        for n in range(2):
            opening_raw.append(work.tile([P, PACK, W // 2], BF16, name="raw_quarter", bufs=2, align_bytes=ALIGN))
            cols = slice(R + n * W // 2, R + (n + 1) * W // 2)
            nc.sync.dma_start(out=opening_raw[n][:], in_=rows_of(gh_hard, 0)[:, :, cols])
            if n == 0:
                load_hot(0)
                load_hot_scales(hot_s_first, 0, 1)
        for key in FIRST_PIECES[1 : 1 + RAW_SLOTS]:
            load_piece(key)

        grouped = {}

        def deal_hot(k):
            nc.vector.tensor_copy(
                out=hot_w[:, k, :].bitcast(I32).rearrange("p (g t a w) -> p g a t w", g=2, t=PACK, w=2),
                in_=raw["hot", k][:].rearrange("p (g a t w) -> p g a t w", g=2, t=PACK, w=2),
            )

        def deal_hot_scales(src, a, b):
            nc.vector.tensor_copy(
                out=hot_s[:, a:b, :].bitcast(I32).rearrange("p k (g t a) -> p (k g) a t", g=2, t=PACK),
                in_=src[:].bitcast(I32).rearrange("p k (g a t) -> p (k g) a t", g=2, t=PACK),
            )

        def interleave(engine, dst, src):
            copy_on(
                engine,
                dst.rearrange("p (c i) (h l) -> p c h i l", i=WALK, l=2),
                src.rearrange("p (h l) (c i) -> p c h i l", i=WALK, l=2),
            )

        def group(engine, key, a, b):
            if key not in grouped:
                grouped[key] = work.tile([P, W, PACK], BF16, name="grouped", bufs=4, align_bytes=ALIGN)
            if key[0] == "gh":
                interleave(engine, grouped[key][:, a:b, :], raw[key][:, :, a:b])
            else:
                runs = slice(a // (PACK * RUN), b // (PACK * RUN))
                copy_on(
                    engine,
                    grouped[key][:].rearrange("p (t a e) j -> p a t j e", t=PACK, e=RUN)[:, runs],
                    raw[key][:].rearrange("p j (a t e) -> p a t j e", t=PACK, e=RUN)[:, runs],
                )

        def shared(key):
            cut = FIRST_SHARE if key[0] == "gh" and key[2] == CURV else W // 2
            group("S", key, cut, W)
            group("V", key, 0, cut)

        def quantise(key, a=0, b=W):
            name, g, half = key
            src = grouped[key][:, a:b, :].rearrange("p c t -> p (c t)")
            quantise_into(gh_q if name == "gh" else soft_q, g, half * W + a, half * W + b, src)

        def wide_tile(key):
            if key not in grouped:
                grouped[key] = work.tile([P, J, PACK], BF16, name="grouped_wide", bufs=2, align_bytes=ALIGN)
            return grouped[key]

        def group_table(engine, name, g, jh, a, b):
            interleave(engine, wide_tile((name, jh))[:, g * W + a : g * W + b, :], raw[name, g, jh][:, :, a:b])

        def quantise_table(name, jh):
            src = grouped[name, jh][:].rearrange("p c t -> p (c t)")
            quantise_into(curve_q if name == "curve" else steps_q, jh, 0, J, src)

        def hist_pass(acc, kind, k, half, tiles=range(4)):
            if k in (0, GROUPS - 1) or (kind, k, half) == (GRAD, 1, 0):
                order = [(t, s) for s in tiles for t in range(PACK)]
            else:
                order = [(t, s) for t in range(PACK) for s in tiles]
            for t, s in order:
                tile = slice(W * half + t * P, W * half + (t + 1) * P)
                if k < HARD:
                    lhsT = hot_w[:, k, 2 * tile.start : 2 * tile.stop].bitcast(FP4X4)
                    lhsT_scale = hot_s[:, k, tile]
                else:
                    lhsT = soft_q[0][:, k - HARD, tile].bitcast(FP8X4)
                    lhsT_scale = soft_q[1][:, k - HARD, tile]
                cols = slice(kind * R + s * P, kind * R + (s + 1) * P)
                nc.tensor.matmul_mx(
                    out=acc[half, s][:, t * P : (t + 1) * P],
                    lhsT=lhsT,
                    lhsT_scale=lhsT_scale,
                    rhs=gh_q[0][:, k, cols].bitcast(FP8X4),
                    rhs_scale=gh_q[1][:, k, cols],
                    start=(k == 0 and t == 0),
                    stop=(k == GROUPS - 1 and t == PACK - 1),
                )

        def empty_hist(acc, half):
            dst = grouped_hist[:, half * W * PACK : (half + 1) * W * PACK]
            dst = dst.rearrange("p (u s m t) -> p s u m t", u=PACK, s=4, t=PACK)
            for s in range(4):
                nc.scalar.copy(out=dst[:, s], in_=acc[half, s][:].rearrange("p (t m u) -> p u m t", t=PACK, u=PACK))

        def quantise_hist(kind, first_half, count):
            a, b = first_half * W, (first_half + count) * W
            quantise_into(hist_q, kind, a, b, grouped_hist[:, a * PACK : b * PACK])

        dens = {}
        nums = {}
        y_turned = {}

        def denominator(n, b):
            jh, t = divmod(n, PACK)
            dens[n] = bank(b)
            for g in range(2):
                tile = slice(g * R + t * P, g * R + (t + 1) * P)
                nc.tensor.matmul_mx(
                    out=dens[n][:],
                    lhsT=hist_q[0][:, CURV, tile].bitcast(FP8X4),
                    lhsT_scale=hist_q[1][:, CURV, tile],
                    rhs=curve_q[0][:, jh, g * W : (g + 1) * W].bitcast(FP8X4),
                    rhs_scale=curve_q[1][:, jh, g * W : (g + 1) * W],
                    start=(g == 0),
                    stop=(g == 1),
                )

        def of_denominator(n, dst, func, scale, bias):
            jh, t = divmod(n, PACK)
            nc.scalar.activation(
                out=dst[:, t, jh * W : (jh + 1) * W],
                in_=dens[n][:],
                func=func,
                scale=scale[:, t : t + 1],
                bias=bias[:, t : t + 1],
            )

        def root(n):
            of_denominator(n, y, ACT.Abs_reciprocal_sqrt, rho_inv, lam_over_rho)

        def signum(n):
            of_denominator(n, sign, ACT.Sign, rho_sign, lam_signed)

        def numerator_half(n, g, b=None):
            if g == 0:
                nums[n] = bank(b)
            q, h = divmod(n, 2)
            jh, part = divmod(q, 2)
            for l in range(2):
                tile = slice(g * R + (2 * h + l) * P, g * R + (2 * h + l + 1) * P)
                cols = slice(g * W + part * Q, g * W + (part + 1) * Q)
                nc.tensor.matmul_mx(
                    out=nums[n][:, l * Q : (l + 1) * Q],
                    lhsT=hist_q[0][:, GRAD, tile].bitcast(FP8X4),
                    lhsT_scale=hist_q[1][:, GRAD, tile],
                    rhs=steps_q[0][:, jh, cols].bitcast(FP8X4),
                    rhs_scale=steps_q[1][:, jh, cols],
                    start=(g == 0 and l == 0),
                    stop=(g == 1 and l == 1),
                )

        def numerator(n, b):
            numerator_half(n, 0, b)
            numerator_half(n, 1)

        def unit(tile, n):
            q, h = divmod(n, 2)
            return tile[:, 2 * h : 2 * h + 2, q * Q : (q + 1) * Q]

        def ratio(n):
            num = nums[n][:].rearrange("p (l j) -> p l j", l=2)
            nc.vector.tensor_tensor(out=unit(y, n), in0=num, in1=unit(y, n), op=ALU.mult)

        def square(n):
            nc.scalar.activation(out=unit(y, n), in_=unit(y, n), func=ACT.Square)

        def scores_of(q):
            if q >= ASIDE:
                return y[:, :, q * Q : (q + 1) * Q].rearrange("p (h l) j -> p h l j", l=2)
            if q == 0:
                return aside[:, 0].rearrange("p (h l) j -> p h l j", l=2)
            return aside[:, :, :2, :]

        def score(n, a=0, b=Q):
            part = unit(y, n)[:, :, a:b]
            dst = scores_of(n // 2)[:, n % 2, :, a:b]
            nc.vector.tensor_tensor(out=dst, in0=part, in1=unit(sign, n)[:, :, a:b], op=ALU.mult)

        def square_shared(n):
            first, second = unit(y, n)[:, 0, :], unit(y, n)[:, 1, :]
            nc.gpsimd.tensor_tensor(out=first, in0=first, in1=first, op=ALU.mult)
            nc.scalar.activation(out=second, in_=second, func=ACT.Square)

        def score_aside(n):
            nc.gpsimd.tensor_tensor(out=aside[:, 0, :2, :], in0=unit(y, n), in1=unit(sign, n), op=ALU.mult)

        def turn_y(jb, h, b=None):
            if b is not None:
                y_turned[jb] = bank(b)
            for t in (2 * h, 2 * h + 1):
                src = scores_of(jb // 2)[:, t // 2, t % 2, (jb % 2) * P : (jb % 2 + 1) * P]
                nc.tensor.transpose(y_turned[jb][:, t * P : (t + 1) * P], src, ident[:])

        def store_rows(jb, queue, engine="S"):
            rows = work.tile([P, P, PACK], F32, name="rows", bufs=5, align_bytes=ALIGN)
            copy_on(engine, rows[:], y_turned[jb][:].rearrange("j (t p) -> j p t", t=PACK))
            queue.dma_start(out=out_0[jb * P : (jb + 1) * P, :], in_=rows[:].rearrange("j p t -> j (p t)"))

        def interleave_pair(jb):
            q = jb // 2
            dst = wide_tile("y")[:, q * Q : (q + 1) * Q, :]
            nc.vector.tensor_copy(
                out=dst.rearrange("p (c i) (h l) -> p c h i l", i=WALK, l=2),
                in_=scores_of(q).rearrange("p h l (c i) -> p c h i l", i=WALK),
            )

        def quantise_pair(jb, count=2):
            a, b = jb * P, (jb + count) * P
            quantise_into(y_q, 0, a, b, grouped["y"][:, a:b, :].rearrange("p c t -> p (c t)"))

        def store_words(a, b):
            cols = slice(a * P, b * P)
            words = out_1[0].rearrange("p m t -> p (m t)").bitcast(I32)
            nc.sync.dma_start(out=words[:, cols], in_=y_q[0][:, 0, cols].bitcast(I32))

        first = {(half, s): bank(4 * half + s) for half in range(2) for s in range(4)}
        grads = [("gh", k, GRAD) for k in range(GROUPS)]
        ahead = list(FIRST_PIECES) + grads
        opening = work.tile([P, W, PACK], BF16, name="grouped", bufs=4, align_bytes=ALIGN)
        for n in range(2):
            a, b = n * W // 2, (n + 1) * W // 2
            interleave("S", opening[:, a + OPENING_SHARE : b, :], opening_raw[n][:, :, OPENING_SHARE:])
            interleave("V", opening[:, a : a + OPENING_SHARE, :], opening_raw[n][:, :, :OPENING_SHARE])
            if n == 0:
                deal_hot(0)
            quantise_into(gh_q, 0, R + a, R + b, opening[:, a:b, :].rearrange("p c t -> p (c t)"))
            if n == 0:
                deal_hot_scales(hot_s_first, 0, 1)
            for half in range(2):
                hist_pass(first, CURV, 0, half, range(2 * n, 2 * n + 2))
        for n in range(1, len(FIRST_PIECES)):
            name, g, half = FIRST_PIECES[n]
            if n == 1:
                shared(FIRST_PIECES[n])
                deal_hot(g)
                quantise(FIRST_PIECES[n])
                deal_hot_scales(hot_s_rest, 1, HARD)
                shared(ahead[n + 1])
            else:
                shared(ahead[n + 1])
                if name == "gh" and g < HARD:
                    deal_hot(g)
                quantise(FIRST_PIECES[n])
            if n + RAW_SLOTS < len(ahead):
                load_piece(ahead[n + RAW_SLOTS])
            if name == "soft":
                hist_pass(first, CURV, HARD + g, half)
            elif g < HARD:
                hist_pass(first, CURV, g, 0)
                hist_pass(first, CURV, g, 1)
        nc.sync.dma_start(out=rho_bf[:], in_=rho.rearrange("(p t) -> p t", t=PACK))
        nc.sync.dma_start(out=lam_bf[:], in_=lam.rearrange("(p t) -> p t", t=PACK))
        for name, src in (("curve", curve), ("steps", steps)):
            for jh in range(2):
                for g in range(2):
                    load_table(name, src, g, jh)

        quantise(grads[0])
        group("V", grads[1], 0, W // 2)
        group("V", grads[1], W // 2, W)
        quantise(grads[1], 0, W // 2)
        quantise(grads[1], W // 2, W)
        group("V", grads[2], 0, W)
        for half in range(2):
            empty_hist(first, half)
        second = {(half, s): bank(4 * half + s) for half in range(2) for s in range(4)}
        hist_pass(second, GRAD, 0, 0)
        hist_pass(second, GRAD, 1, 0)
        hist_pass(second, GRAD, 0, 1)
        group("V", grads[3], 0, W)
        quantise(grads[2])
        hist_pass(second, GRAD, 1, 1)
        hist_pass(second, GRAD, 2, 0)
        for k in range(4, GROUPS):
            shared(grads[k])
            quantise(grads[k - 1])
            hist_pass(second, GRAD, k - 1, 0)
        nc.scalar.activation(out=rho_root[:], in_=rho_bf[:], func=ACT.Abs_reciprocal_sqrt, bias=guard[:, 2:3])
        nc.scalar.activation(out=rho_sign[:], in_=rho_bf[:], func=ACT.Sign)
        group_table("S", "curve", 0, 0, 0, W)
        group_table("S", "curve", 1, 0, W // 2, W)
        group_table("S", "curve", 0, 1, W // 2, W)
        quantise(grads[5])
        hist_pass(second, GRAD, 5, 0)
        quantise_hist(CURV, 0, 2)
        nc.vector.tensor_tensor(out=rho_inv[:], in0=rho_root[:], in1=rho_root[:], op=ALU.mult)
        nc.vector.tensor_tensor(out=lam_signed[:], in0=lam_bf[:], in1=rho_sign[:], op=ALU.mult)
        group_table("V", "curve", 1, 0, 0, W // 2)
        nc.vector.tensor_tensor(out=lam_over_rho[:], in0=lam_bf[:], in1=rho_inv[:], op=ALU.mult)
        group_table("V", "curve", 0, 1, 0, W // 2)
        quantise_table("curve", 0)
        empty_hist(second, 0)
        hist_pass(second, GRAD, 2, 1)
        group_table("V", "curve", 1, 1, 0, W)
        group_table("S", "steps", 0, 0, STEPS_SHARE, W)
        group_table("V", "steps", 0, 0, 0, STEPS_SHARE)

        denominator(0, 0)
        denominator(1, 1)
        hist_pass(second, GRAD, 3, 1)
        denominator(2, 2)
        for n in range(3):
            root(n)
            signum(n)
        group_table("V", "steps", 1, 0, 0, W)
        quantise_table("curve", 1)
        hist_pass(second, GRAD, 4, 1)
        hist_pass(second, GRAD, 5, 1)
        quantise_hist(GRAD, 0, 1)
        quantise_table("steps", 0)
        for g in range(2):
            group_table("V", "steps", g, 1, 0, W)
        empty_hist(second, 1)
        for n in range(3, 7):
            denominator(n, n % 4)
        root(3)
        for n in range(3):
            numerator_half(n, 0, 4 + n)
        for h in range(2):
            a, b = W + h * Q, W + (h + 1) * Q
            quantise_into(hist_q, GRAD, a, b, grouped_hist[:, a * PACK : b * PACK])
        quantise_table("steps", 1)
        for n in range(3):
            numerator_half(n, 1)
        numerator(3, 7)
        root(4)
        signum(3)
        denominator(7, 3)
        root(5)
        root(6)
        signum(4)
        ratio(0)
        numerator(4, 4)
        ratio(1)
        square_shared(0)
        score_aside(0)
        ratio(2)
        numerator(5, 5)
        root(7)
        square(1)
        ratio(3)
        numerator(6, 6)
        ratio(4)
        square(3)
        ratio(5)
        square(2)
        numerator(7, 7)
        turn_y(0, 0, 4)
        turn_y(1, 0, 0)
        score(1)
        turn_y(0, 1)
        turn_y(1, 1)
        score(3)
        interleave_pair(0)
        score_aside(2)
        signum(5)
        square(4)
        store_rows(0, nc.sync)
        ratio(6)
        ratio(7)
        store_rows(1, nc.sync, "V")
        signum(6)
        signum(7)
        square(5)
        turn_y(3, 1, 5)
        turn_y(2, 1, 1)
        turn_y(2, 0)
        turn_y(3, 0)
        quantise_pair(0)
        score(4)
        turn_y(4, 0, 6)
        turn_y(5, 0, 4)
        store_rows(2, nc.sync)
        square(6)
        interleave_pair(2)
        score(5)
        turn_y(4, 1)
        turn_y(5, 1)
        quantise_pair(2)
        store_words(0, 4)
        store_rows(3, nc.sync)
        square(7)
        score(6)
        turn_y(6, 0, 2)
        turn_y(7, 0, 3)
        interleave_pair(4)
        score(7, 0, P)
        turn_y(6, 1)
        score(7, P, Q)
        turn_y(7, 1)
        store_rows(4, nc.sync)
        quantise_pair(4)
        store_words(4, 6)
        store_rows(5, nc.sync)
        interleave_pair(6)
        store_rows(6, nc.sync)
        quantise_pair(6)
        store_words(6, 8)
        store_rows(7, nc.scalar)
        for r in range(4):
            queue = (nc.sync, nc.scalar)[r % 2]
            queue.dma_start(out=out_2[0, r:16:4, :].bitcast(I32), in_=y_q[1][r:P:32, 0, :].bitcast(I32))
